import numpy as np, ml_dtypes
CORES = [51,54,179,182]
N = 4
BF = ml_dtypes.bfloat16
def gentries(a):
    return np.ascontiguousarray(a.reshape(8, 16, -1).transpose(0, 2, 1)).reshape(8, -1)
def gtable(e):
    e = np.asarray(e); return np.ascontiguousarray(e.reshape(8, -1, 16).transpose(0, 2, 1)).reshape(128, -1).astype(np.int32)
H, W, P, F, S, R, CAP = 32, 16, 512, 5, 6, 7, 96
def near(rng, e):
    c = 2 + np.arange(F) + np.add.accumulate(e, axis=-1); n = np.concatenate([np.zeros((N, 8, 1), np.int64), np.ones((N, 8, 1), np.int64), c], axis=-1)
    j = np.maximum(np.arange(F) + 1 - rng.integers(0, 3, e.shape), 0)
    return np.minimum(c - np.take_along_axis(n, j, -1), R)
def near3(rng, e):
    return np.stack([near(rng, e) for k in range(3)], axis=-1)
def parts(rng):
    e = rng.choice(np.array([0, 0, 0, 1, 1, 2]), (N, 8, F)); op = rng.choice(np.array([0, 0, 1, 1, 2]), (N, 8, F))
    rel = np.where(rng.random((N, 8, F, 3)) < 0.6, near3(rng, e), rng.integers(1, R + 1, (N, 8, F, 3)))
    sh = rng.choice(np.array([0.0, 0.1, 0.45]), (N, 8, F, 1)); sd = rng.choice(np.array([0.2, 0.35, 0.5]), (N, 8, F, 1)); z = (N, 8, F, P)
    ia = np.where(rng.random(z) < sh, S, rng.integers(0, S, z)); ib = np.where(rng.random(z) < sh, S, rng.integers(0, S, z))
    ia = np.where(rng.random(z) < sd, S + 1, ia); z = (N, 8, F, 2, P); b = np.arange(P)
    vy = np.where(rng.random(z) < 0.15, rng.integers(-H, H + 1, z), rng.integers(0, H, z) - b // W)
    vx = np.where(rng.random(z) < 0.15, rng.integers(-W, W + 1, z), rng.integers(0, W, z) - b % W)
    z = (N, 8, 16, F, P); res = np.where(rng.random(z) < 0.05, rng.integers(-255, 256, z), rng.integers(-48, 49, z))
    return e, op, rel, ia, ib, vy, vx, res, rng.integers(0, 256, (N, 8, 16, 2, P))
def keep(rng, ia, ib, top):
    w = np.concatenate([ia == S, (ib == S) & (ia <= S)], axis=-1); o = np.argsort(rng.random(w.shape), axis=-1)
    s = np.take_along_axis(w, o, -1); over = s & (np.add.accumulate(s.astype(np.int64), axis=-1) > CAP)
    cut = np.zeros(w.shape, bool); np.put_along_axis(cut, o, over, -1); new = rng.integers(0, top, w.shape)
    return np.where(cut[..., :P], new[..., :P], ia), np.where(cut[..., P:], new[..., P:], ib)
def gts(a):
    return np.stack([gtable(np.ascontiguousarray(v).reshape(8, -1)) for v in a])
def pack(rng, e, op, rel, ia, ib, vy, vx, res, pic, top=S):
    ia, ib = keep(rng, ia, ib, top)
    return {"res": np.ascontiguousarray(res).reshape(N, 128, F * P).astype(np.float32).astype(BF), "pic0": np.ascontiguousarray(pic).reshape(N, 128, 2 * P).astype(np.float32).astype(BF),
            "ia": gts(ia), "ib": gts(ib), "vy": gts(vy), "vx": gts(vx), "gaps": e.astype(np.int32), "cmd": op.astype(np.int32), "rel": np.ascontiguousarray(rel).reshape(N, 8, 3 * F).astype(np.int32)}
def setup_inputs(rng):
    return pack(rng, *parts(rng))
def setup_inputs_spread(rng):
    e, op, rel, ia, ib, vy, vx, res, pic = parts(rng)
    res = np.clip(np.rint((2 * rng.random(res.shape) - 1) * np.exp2(8 * rng.random((N, 8, 1, F, P)))), -255, 255).astype(np.int64)
    pic = np.minimum((rng.random(pic.shape) * np.exp2(8 * rng.random((N, 8, 1, 2, P)))).astype(np.int64), 255); pic = np.where(rng.random((N, 8, 16, 1, P)) < 0.5, pic, 255 - pic)
    big = rng.random((N, 8, F, 2, P))
    vy = np.where(big < 0.5, vy, np.rint((2 * rng.random(vy.shape) - 1) * H * np.exp2(-6 * rng.random(vy.shape))).astype(np.int64))
    vx = np.where(big < 0.5, vx, np.rint((2 * rng.random(vx.shape) - 1) * W * np.exp2(-6 * rng.random(vx.shape))).astype(np.int64))
    return pack(rng, e, op, rel, ia, ib, vy, vx, res, pic)
def setup_inputs_ends(rng):
    e, op, rel, ia, ib, vy, vx, res, pic = parts(rng); z = ia.shape
    e = np.where(rng.random(e.shape) < 0.35, 2, 0); op = rng.choice(np.array([0, 0, 2, 2, 1]), e.shape); rel = np.where(rng.random(rel.shape) < 0.5, 1, R)
    e[:, 0, 1] = 2; e[:, 0, 2] = 0; op[:, 0, 2] = 2; op[:, 0, 1] = 0
    ia = np.where(rng.random(z) < 0.15, rng.integers(0, S + 1, z), np.where(rng.random(z) < 0.5, S + 1, 0)); ib = np.where(rng.random(z) < 0.5, S, 0)
    vy = np.where(rng.random(vy.shape) < 0.2, vy, np.where(rng.random(vy.shape) < 0.5, H, -H)); vx = np.where(rng.random(vx.shape) < 0.2, vx, np.where(rng.random(vx.shape) < 0.5, W, -W))
    res = np.where(rng.random(res.shape) < 0.65, np.where(rng.random(res.shape) < 0.5, 255, -255), rng.integers(-64, 65, res.shape)); pic = np.where(rng.random(pic.shape) < 0.5, 255, 0)
    e[:, 6:] = 0; op[:, 6:] = 0; rel[:, 6:, :, 1:] = 1
    ia[:, 6:, :, P - 1] = 0; ib[:, 6:, :, P - 1] = 0; vy[:, 6:, :, :, P - 1] = H; vx[:, 6:, :, :, P - 1] = W
    pic[:, 6, :, :, P - 1] = 0; pic[:, 7, :, :, P - 1] = 255
    res[:, 6, :, :, P - 1] = np.tile(np.array([0, 1, 255, -255]), 4)[:, None]; res[:, 7, :, :, P - 1] = np.tile(np.array([0, -1, -255, 255]), 4)[:, None]
    return pack(rng, e, op, rel, ia, ib, vy, vx, res, pic, 1)
def roles():
    return (np.arange(8)[None, :] + np.arange(N)[:, None]) % 8
def setup_inputs_corners(rng):
    e, op, rel, ia, ib, vy, vx, res, pic = parts(rng); k = roles(); b = np.arange(P)
    e[k == 0] = 0; op[k == 0] = 0; e[k == 1] = 2; op[k == 2] = 1; e[k == 3] = 0; op[k == 3] = 2
    nr = near3(rng, e); m = (k == 1) | (k == 2) | (k == 4); rel[m] = nr[m]
    rel[..., 2] = np.where(rng.random((N, 8, F)) < 0.3, rel[..., 1], rel[..., 2]); rel[..., 0] = np.where(rng.random((N, 8, F)) < 0.3, rel[..., 1], rel[..., 0])
    x = rel[..., 0]; x = np.where((k == 3)[..., None], rng.integers(1, 3, x.shape), x); rel[..., 0] = x
    m = (k == 0)[..., None, None]; ia = np.where(m & (ia > S), rng.integers(0, S, ia.shape), ia)
    m = (k == 4)[..., None, None]; late = np.arange(F)[:, None] >= 1
    ia = np.where(m & late, S + 1, np.where(m, rng.integers(0, S, ia.shape), ia))
    m = (k == 5)[..., None, None, None]; z = (N, 8, F, 2, 1)
    vy = np.where(m, rng.choice(np.array([0, H - 1]), z) - b // W, vy); vx = np.where(m, rng.choice(np.array([0, W - 1]), z) - b % W, vx)
    m = (k == 5)[..., None, None]; ib = np.where(m, S, ib); ia = np.where(m, rng.integers(0, S, ia.shape), ia)
    m = (k == 6)[..., None, None, None]; vy = np.where(m, np.where(rng.random(vy.shape) < 0.5, H, -H), vy); vx = np.where(m, np.where(rng.random(vx.shape) < 0.5, W, -W), vx)
    m = (k == 6)[..., None, None]; ia = np.where(m & (ia == S), 0, ia); ib = np.where(m & (ib == S), S - 1, ib)
    m = (k == 7)[..., None, None]; n = CAP - (np.arange(F)[:, None] & 1)
    ia = np.where(m, np.where(b < n, S, rng.integers(0, S, ia.shape)), ia); ib = np.where(m, rng.integers(0, S, ib.shape), ib)
    return pack(rng, e, op, rel, ia, ib, vy, vx, res, pic)
def setup_inputs_calm(rng):
    e, op, rel, ia, ib, vy, vx, res, pic = parts(rng); k = roles(); e0, op0 = e, op; odd = (np.arange(N)[:, None] & 1) == 1
    e = np.zeros(e.shape, np.int64); op = np.zeros(op.shape, np.int64); x = rng.integers(1, 4, e.shape)
    op[k < 2] = 2; x[k == 0] = 1; x[k == 1] = 2
    e[k == 3, 0] = 1; op[k == 3, 0] = 1; x[k == 3, 0] = 4; op[k == 3, F - 1] = 2; e[k == 4, 0] = 2
    e[k == 5, 0] = 2; e[k == 5, 1] = 2; op[k == 5, 2:] = 2
    op[k == 6] = 1; x[k == 6] = 1; e[k == 6, 1] = 1
    m = (k == 6) & odd; e[m] = 0; e[m, 0] = min(S - F, 2); x[m, :F - 1] = 2; e[m, F - 1] = 2
    for t, (o, v) in enumerate(((1, 1), (1, 2), (2, 3))):
        op[k == 2, t] = o; x[k == 2, t] = v
    m = (k == 2) & odd
    for t, (o, v) in enumerate(((1, 1), (2, 2), (0, 3))):
        op[m, t] = o; x[m, t] = v
    e[k == 7] = e0[k == 7]; op[k == 7] = op0[k == 7]
    rel = np.where(rng.random(rel.shape) < 0.7, near3(rng, e), rng.integers(1, 4, rel.shape)); rel[..., 0] = x
    rel[k == 3, 1, 1:] = 2; rel[k == 6, F - 1, 1:] = rng.integers(2, R + 1, (N, 2))
    vy = rng.integers(-3, 4, vy.shape); vx = rng.integers(-3, 4, vx.shape)
    return pack(rng, e, op, rel, ia, ib, vy, vx, res, pic)
def check_inputs(d):
    bad = []
    for k, lo, hi in (("res", -255, 255), ("pic0", 0, 255), ("ia", 0, S + 1), ("ib", 0, S), ("vy", -H, H), ("vx", -W, W), ("gaps", 0, 2), ("cmd", 0, 2), ("rel", 1, R)):
        v = np.asarray(d[k]).astype(np.float64)
        if not (np.min(v) >= lo and np.max(v) <= hi): bad.append("range of " + k)
        if np.any(v != np.rint(v)): bad.append("whole numbers in " + k)
    a, b = [np.stack([gentries(v) for v in np.asarray(d[k])]).reshape(N, 8, F, P) for k in ("ia", "ib")]
    if np.max(np.sum((a == S).astype(np.int64) + ((b == S) & (a <= S)), axis=-1)) > CAP: bad.append("view blocks of a frame and group")
    return bad
def insert(h, n):
    if len(h) == S: del h[min(k for k in h if not h[k])]
    h[n] = False
def step(h, nxt, cur, first, e, op, x, m0, m1):
    if not first: insert(h, cur)
    for k in range(e): insert(h, nxt + k)
    cur = nxt + e
    if op == 1 and cur - x in h: h[cur - x] = True
    if op == 2 and cur - x in h and len(h) > 2: del h[cur - x]
    key = {n: (63 - n if h[n] else 64 + n) + 128 * (n == cur - m0) + 256 * (n == cur - m1) for n in h}
    return sorted(h, key=lambda n: -key[n]), cur + 1, cur
def reference(res, pic0, ia, ib, vy, vx, gaps, cmd, rel):
    M = 3 * F + 2
    rs = res.astype(np.float32).astype(np.int64).reshape(N, 8, 16, F, P); st = pic0.astype(np.float32).astype(np.int64).reshape(N, 8, 16, 2, P)
    la, lb = [np.stack([gentries(v) for v in a]).astype(np.int64).reshape(N, 8, F, P) for a in (ia, ib)]
    ly, lx = [np.stack([gentries(v) for v in a]).astype(np.int64).reshape(N, 8, F, 2, P) for a in (vy, vx)]
    by = np.arange(P) // W; bx = np.arange(P) % W; g8 = np.arange(8); y = np.zeros((N, 8, 16, F, P), np.int64)
    pics = np.full((N, 8, 16, M + 2, P), 128, np.int32); pics[:, :, :, 0:2] = st
    mq = np.full((N, 8, M, P), -1, np.int64); my = np.zeros((N, 8, M, P), np.int64); mx = np.zeros((N, 8, M, P), np.int64)
    held = [[{0: False, 1: False} for g in range(8)] for r in range(N)]; nxt = np.full((N, 8), 2); cur = np.zeros((N, 8), np.int64)
    for f in range(F):
        for r in range(N):
            q = (r - 1) % N; src = (g8 + f) % 8
            pics[r, :, :, M + 1] = st[q, src, :, 1] if f == 0 else y[q, src, :, f - 1]
            A = np.full((8, S + 1), M, np.int64); A[:, S] = M + 1; here = np.zeros((8, M), bool)
            for g in range(8):
                lst, a, b = step(held[r][g], int(nxt[r, g]), int(cur[r, g]), f == 0, int(gaps[r, g, f]), int(cmd[r, g, f]), int(rel[r, g, 3 * f]), int(rel[r, g, 3 * f + 1]), int(rel[r, g, 3 * f + 2]))
                nxt[r, g] = a; cur[r, g] = b; A[g, :len(lst)] = lst; here[g, lst] = True
            B = np.array(A); B[:, 0] = A[:, 1]; B[:, 1] = A[:, 0]; c = B[:, 0]
            ja = la[r, :, f]; direct = ja == S + 1
            na = np.take_along_axis(A, np.where(direct, 0, ja), 1); nb = np.take_along_axis(B, lb[r, :, f], 1)
            n = mq[r, g8, c]; wy = my[r, g8, c]; wx = mx[r, g8, c]; ay = wy >> 1; ax = wx >> 1
            ok = (n >= 0) & np.take_along_axis(here, np.maximum(n, 0), 1)
            na = np.where(direct, np.where(ok, n, A[:, :1]), na); nb = np.where(direct, c[:, None], nb)
            uy = np.where(direct, ay, ly[r, :, f, 0]); ux = np.where(direct, ax, lx[r, :, f, 0])
            ty = np.where(direct, ay - wy, ly[r, :, f, 1]); tx = np.where(direct, ax - wx, lx[r, :, f, 1])
            flat = pics[r].reshape(8, 16, (M + 2) * P)
            i = na * P + np.clip(by + uy, 0, H - 1) * W + np.clip(bx + ux, 0, W - 1); j = nb * P + np.clip(by + ty, 0, H - 1) * W + np.clip(bx + tx, 0, W - 1)
            s = np.take_along_axis(flat, i[:, None, :], 2) + np.take_along_axis(flat, j[:, None, :], 2) + 1
            v = np.clip((s >> 1) + rs[r, :, :, f], 0, 255)
            y[r, :, :, f] = v
            for g in range(8):
                k = cur[r, g]; pics[r, g, :, k] = v[g]; mq[r, g, k] = np.where(na[g] < M, na[g], -1); my[r, g, k] = uy[g]; mx[r, g, k] = ux[g]
    return {"y": y.reshape(N, 128, F * P).astype(np.float32).astype(BF)}

@@ -1,0 +1,501 @@
+import math
+from concourse.mybir import AluOpType as ALU, AxisListType, ActivationFunctionType as ACT
+
+F = 5
+P = 512
+CH = ((0, 192, "V"), (192, 384, "A"), (384, 512, "V"))
+CW = 192
+MAGIC = 12582912.0
+LN8 = math.log(8.0)
+V0 = F - 1
+SB = F
+MW = 160
+
+
+def _sb(shape, dt):
+    return ("sbuf", [128] + shape, dt)
+
+
+BF, F32, I32 = "bfloat16", "float32", "int32"
+SCRATCH = {
+    "win": _sb([12 * P], BF), "rs": _sb([F * P], BF), "snd": _sb([F * P], BF),
+    "gp": _sb([P], BF), "gq": _sb([P], BF), "yy": _sb([P], F32), "tb": _sb([P], BF),
+    "ctl": _sb([32], I32), "ctb": _sb([32], BF),
+    "lia": _sb([F, 32], I32), "lib": _sb([F, 32], I32), "lvy": _sb([F, 64], I32), "lvx": _sb([F, 64], I32),
+    "cA": _sb([128], F32), "cB": _sb([128], F32), "pi": _sb([2], I32), "pj": _sb([4], I32), "col": _sb([12], F32),
+    "W2": _sb([256], BF), "N2": _sb([256], BF), "I16": _sb([128], BF), "I512": _sb([128], BF),
+    "OO": _sb([128], BF), "NO": _sb([128], BF), "NU": _sb([128], BF), "NL": _sb([128], BF),
+    "tU": _sb([128], BF), "tL": _sb([128], BF), "E8": _sb([128], BF),
+    "qm": _sb([CW], BF), "c128": _sb([CW], BF), "cM": _sb([CW], BF), "K1": _sb([128], BF), "K2": _sb([96], F32),
+    "cc": _sb([32], F32), "CL": _sb([16], F32), "one5": _sb([8], F32), "ph5": _sb([8], F32),
+    "a1": _sb([8], F32), "a2": _sb([8], F32), "z0": _sb([2], F32), "tx": _sb([8], F32),
+    "TG": _sb([32], F32), "OH": _sb([32], BF), "NE": _sb([32], BF),
+    "born": _sb([8], BF), "c23": _sb([8], BF), "R": _sb([8], BF), "f1": _sb([8], F32),
+    "SS": _sb([F, 2], F32), "SZ": _sb([F, 2], F32), "ZU": _sb([F, 2], BF), "LP": _sb([8], BF), "RB": _sb([8], F32),
+    "PH": _sb([8], F32), "pe": _sb([2], F32),
+    "nm2": _sb([2, F], F32), "k0": _sb([8], F32),
+    "XE": _sb([16], F32), "held": _sb([F], BF), "G": _sb([4, F], BF),
+    "Gp": _sb([4, F], F32), "Ge": _sb([4, F], F32), "wts": _sb([4, F], BF), "H": _sb([4, 2, F], BF),
+    "XE0": _sb([2], F32), "held0": _sb([1], BF), "G0": _sb([4, 1], BF),
+    "Gp0": _sb([4, 1], F32), "wts0": _sb([4, 1], BF), "H0": _sb([4, 1, 1], BF),
+    "s1": _sb([8], I32), "s2": _sb([8], I32), "s3": _sb([8], F32), "ML": _sb([F, 16], "uint16"),
+    "ND": _sb([F, 2, 32], BF), "idx": _sb([F, 2, 32], BF), "ibn": _sb([F, 32], BF),
+    "mx": _sb([F, 32], BF), "e1": _sb([F, 32], BF), "w": _sb([F, 2, 32], BF),
+    "nv": _sb([F, 64], BF), "thr": _sb([F, 64], BF), "D4": _sb([F, 128], BF),
+    "VN": _sb([F, 128], BF), "Y": _sb([F, 96], I32), "B": _sb([F, 96], I32), "PB": _sb([F, 64], BF),
+    "MS": _sb([F * MW], I32), "ok": _sb([F, 64], BF), "df": _sb([F, 64], BF), "h": _sb([F, 128], BF),
+    "M3": _sb([F, 96], BF), "RC": _sb([F, 128], BF), "OFF": _sb([F, 64], "uint16"),
+}
+for _n in ("X0", "X1", "X2", "C0", "C1", "C2", "P1", "AD"):
+    SCRATCH[_n] = ("psum", [128, 512], F32)
+SEMAPHORES = (["nV", "nA", "nP", "nG", "dctl", "dab", "dv", "dp0", "dp1", "dr0", "dr1", "dy", "ls0", "ls"]
+              + ["arr%d" % f for f in range(F)])
+
+CYC = 1.04
+HOP = 110.0
+
+
+def build(T, topo, core):
+    rank = T.rank_of(core)
+    n = len(T.cores)
+    nxt, prv = T.cores[(rank + 1) % n], T.cores[(rank - 1) % n]
+    rid, pid = topo.addr(nxt, core)
+    emask = topo.mask(core, nxt)
+    n_out, n_in = len(topo.engines(core, nxt)), len(topo.engines(prv, core))
+    ops, wr, rd, bk, lastdma = [], {}, {}, {}, {}
+
+    def op(q, fn, r=(), w=(), banks=(), dur=70.0, lat=0.0, sem=None, inc=0, soft=()):
+        k = len(ops)
+        deps = set()
+        for key in r:
+            deps.add(wr[key])
+        for key in w:
+            if key in wr:
+                deps.add(wr[key])
+            deps.update(rd.get(key, ()))
+        for b in banks:
+            deps.update(o for qq, o in bk.get(b, {}).items() if qq != q or q == "P")
+            bk.setdefault(b, {})[q] = k
+        for key in r:
+            rd.setdefault(key, []).append(k)
+        for key in w:
+            wr[key] = k
+            rd[key] = []
+        ops.append({"q": q, "fn": fn, "deps": deps, "soft": set(soft), "dur": dur, "lat": lat, "sem": sem, "inc": inc, "name": tuple(w)})
+        return k
+
+    def el(ap):
+        m = 1
+        for s in ap.shape[1:]:
+            m *= s
+        return m
+
+    def ts(out, in0, s1, s2, o0, o1=None, r=(), w=(), banks=(), k=1.0, x=0.0):
+        if o1 is None:
+            fn = lambda e: e.tensor_scalar(out, in0, s1, None, o0)
+        else:
+            fn = lambda e: e.tensor_scalar(out, in0, s1, s2, o0, o1)
+        return op("V", fn, r, w, banks, max(64, el(out) * k) * CYC + x)
+
+    def tt(out, a, b, o, r=(), w=(), banks=(), k=2.0):
+        return op("V", lambda e: e.tensor_tensor(out, a, b, o), r, w, banks, max(64, el(out) * k) * CYC)
+
+    def cp(out, a, r=(), w=(), banks=()):
+        return op("V", lambda e: e.tensor_copy(out, a), r, w, banks, max(64, el(out)) * CYC)
+
+    def ms(out, v, w):
+        return op("V", lambda e: e.memset(out, v), (), w, (), max(64, el(out) / 2) * CYC)
+
+    def mm(out, l, x, st, sp, r, w, bank):
+        return op("P", lambda e: e.matmul(out, l, x, st, sp), r, w, (bank,), max(64, el(out)) * 0.55)
+
+    def act(out, a, fu, r, w, banks=(), bias=0.0, scale=1.0, k=1.0, x=0.0):
+        return op("A", lambda e: e.activation(out, a, fu, bias, scale), r, w, banks, max(64, el(out) * k) * CYC + x)
+
+    def dma(q, out, a, sem, r=(), w=(), nbytes=0):
+        k = op(q, lambda e: e.dma_start(out, a), r, w, (), 80.0, 1800.0 + nbytes / 200.0, sem, 16)
+        if q in lastdma:
+            ops[k]["order"] = lastdma[q]
+        lastdma[q] = k
+        return k
+
+    def send(f, a, r):
+        s = (V0 - f) * P
+        out = T["win"][:, s:s + P]
+        ls = "ls0" if f == 0 else "ls"
+        fn = lambda e: e.remote_dma(out, a, T.sem["arr%d" % f], T.sem[ls], pid, rid, emask)
+        k = op("G", fn, r, ("sent%d" % f,), (), 400.0, (3000.0 if f == 0 else 1500.0) + P * 3.0, ls, n_out)
+        op("X", None, (), ("V%d" % f,), (), 0.0, 0.0, "arr%d" % f, n_in, (k,))
+
+    win = T["win"]
+    slot = lambda s: win[:, s * P:(s + 1) * P]
+    dma("S", slot(SB + 2), T.pic0[:, P:2 * P], "dp1", w=("pic1",), nbytes=131072)
+    dma("A", T["ctl"][0:8, 0:5], T.gaps[:], "dctl", w=("ctl0",))
+    dma("S", T["ctl"][0:8, 5:10], T.cmd[:], "dctl", w=("ctl1",))
+    dma("A", T["ctl"][0:8, 10:25], T.rel[:], "dctl", w=("ctl2",))
+    dma("S", T["lia"][:], T.ia[:], "dab", w=("ia",), nbytes=200000)
+    dma("A", T["lib"][:], T.ib[:], "dab", w=("ib",), nbytes=200000)
+    dma("S", T["lvy"][:], T.vy[:], "dv", w=("vy",), nbytes=500000)
+    dma("A", T["lvx"][:], T.vx[:], "dv", w=("vx",), nbytes=500000)
+    dma("S", slot(SB + 1), T.pic0[:, 0:P], "dp0", w=("pic0",), nbytes=700000)
+    dma("A", T["rs"][:, 0:P], T.res[:, 0:P], "dr0", w=("rs0",), nbytes=700000)
+    send(0, slot(SB + 2), ("pic1",))
+    dma("S", T["rs"][:, P:F * P], T.res[:, P:F * P], "dr1", r=("sent0",), w=["rs%d" % f for f in range(1, F)], nbytes=524288)
+
+    cA, cB, col, cc = T["cA"], T["cB"], T["col"], T["cc"]
+    op("G", lambda e: e.iota(T["pi"][:, 0:1], [[1, 1]], 0, 1), w=("pi",), dur=200.0)
+    op("G", lambda e: e.iota(cB[:], [[1, 8], [0, 16]], 0, 0, allow_small_or_imprecise_dtypes=True), w=("cB",), dur=400.0)
+    op("G", lambda e: e.iota(cA[:], [[1, 128]], 0, -1, allow_small_or_imprecise_dtypes=True), w=("cA",), dur=400.0)
+    pc_, gc_, lc_, l1_, lq_, lm_ = [col[:, i:i + 1] for i in range(6)]
+    ts(T["pj"][:, 0:1], T["pi"][:, 0:1], 4, None, ALU.arith_shift_right, r=("pi",), w=("pj0",))
+    ts(T["pj"][:, 1:2], T["pi"][:, 0:1], 15, None, ALU.bitwise_and, r=("pi",), w=("pj1",))
+    cp(pc_, T["pi"][:, 0:1], r=("pi",), w=("p",))
+    cp(col[:, 1:3], T["pj"][:, 0:2], r=("pj0", "pj1"), w=("g", "l"))
+    act(l1_, lc_, ACT.Identity, ("l",), ("l1",), bias=1.0)
+    act(lq_, lc_, ACT.Identity, ("l",), ("lq",), bias=-0.25)
+    act(lm_, lc_, ACT.Identity, ("l",), ("lm",), bias=-2.0 * MW)
+    hu_, hl_, hn_ = [col[:, i:i + 1] for i in (6, 7, 8)]
+    ts(hu_, lc_, 0.5, None, ALU.mult, r=("l",), w=("hu",))
+    ts(hl_, lc_, -0.5, 7.5, ALU.mult, ALU.add, r=("l",), w=("hl",))
+    ts(hn_, lc_, 0.5, -7.5, ALU.mult, ALU.add, r=("l",), w=("hn",))
+    ts(T["E8"][0:8, :], cB[0:8, :], col[0:8, 0:1], None, ALU.is_equal, r=("cB", "p"), w=("E8",))
+    ts(T["OO"][:], cB[:], gc_, None, ALU.is_equal, r=("cB", "g"), w=("OO",))
+    ts(T["NO"][:], cB[:], gc_, -1.0, ALU.is_equal, ALU.mult, r=("cB", "g"), w=("NO",))
+    act(T["tU"][:], cA[:], ACT.Abs, ("cA", "hu"), ("tU",), bias=hu_)
+    act(T["tL"][:], cA[:], ACT.Abs, ("cA", "hn"), ("tL",), bias=hn_)
+    ts(T["NU"][:], T["tU"][:], hu_, -1.0, ALU.is_le, ALU.mult, r=("hu", "tU"), w=("NU",), k=0.5)
+    ts(T["NL"][:], T["tL"][:], hl_, -1.0, ALU.is_le, ALU.mult, r=("hl", "tL"), w=("NL",), k=0.5)
+    ts(T["W2"][:, 0:128], cA[:], 0.0, None, ALU.is_equal, r=("cA",), w=("I",))
+    Id = T["W2"][:, 0:128]
+    act(T["W2"][:, 128:256], Id, ACT.Copy, ("I",), ("I2",))
+    act(T["N2"][:], T["W2"][:], ACT.Copy, ("I", "I2"), ("N2",), scale=-1.0)
+    act(T["I16"][:], Id, ACT.Copy, ("I",), ("I16",), scale=16.0)
+    act(T["I512"][:], Id, ACT.Copy, ("I",), ("I512",), scale=512.0)
+    act(cc[:], cA[:, 0:32], ACT.Identity, ("cA", "p"), ("cc",), bias=pc_)
+    for i in range(2):
+        act(T["K1"][:, 32 * i:32 * i + 32], cc[:], ACT.Identity, ("cc",), ("K1%d" % i,), bias=-0.25)
+    act(T["K1"][:, 64:128], cA[:, 0:64], ACT.Identity, ("cA", "lq"), ("K12",), bias=lq_, scale=0.0)
+    k1 = ("K10", "K11", "K12")
+    act(T["K2"][:], T["K1"][:, 0:96], ACT.Identity, k1, ("K2",), bias=128.25)
+    for c0, s0, m in ((0, 0, 2), (2, 0, 2), (4, 0, 6), (10, 4, 2), (12, 8, 2), (14, 8, 2)):
+        act(T["CL"][:, c0:c0 + m], cc[:, s0:s0 + m], ACT.Identity, ("cc", "lm"), ("CL%d" % c0,), bias=lm_, scale=16.0)
+    cl = ("CL0", "CL2", "CL4", "CL10", "CL12", "CL14")
+    ms(slot(SB), 128.0, ("blank",))
+    ms(T["qm"][:], -0.25, ("qm",))
+    ms(T["c128"][:], 128.0, ("c128",))
+    ms(T["cM"][:], MAGIC, ("cM",))
+    ms(T["one5"][:], 1.0, ("one5",))
+    act(T["ph5"][:, 0:F], cc[:, 0:F], ACT.Identity, ("cc",), ("ph5",), bias=3.0)
+    ts(T["PH"][:, F - 1:F], lc_, 2.0, l1_, ALU.is_lt, ALU.mult, r=("l", "l1"), w=("PH4",))
+    ms(T["R"][:, 0:1], 1.0, ("R0",))
+    ms(T["ZU"][:, 0, 0:1], 1.0, ("Z0",))
+    ms(T["LP"][:, 0:1], 0.0, ("LP0",))
+    ms(T["XE"][:, 15:16], -1.0, ("XEc",))
+    ms(T["MS"][:, 0:MW], 0, ("MS0",))
+    ms(T["M3"][:, :, 64:96], 0.0, ("M3z",))
+    act(T["wts0"][:, 3, :], T["one5"][:, 0:1], ACT.Exp, ("one5",), ("wts30",), scale=0.0, x=1400.0)
+    ms(T["wts"][:, 3, :], 1.0, ("wts3",))
+
+    C0, C1, C2 = T["C0"], T["C1"], T["C2"]
+    TG, OH, NE, R, ZU, LP, SS, XE = T["TG"], T["OH"], T["NE"], T["R"], T["ZU"], T["LP"], T["SS"], T["XE"]
+    OO, NO, NU, NL = T["OO"][:], T["NO"][:], T["NU"][:], T["NL"][:]
+    cp(T["ctb"][0:8, 0:25], T["ctl"][0:8, 0:25], r=("ctl0", "ctl1", "ctl2"), w=("ctb",))
+    mm(C2[:, 0:25], T["E8"][0:8, :], T["ctb"][0:8, 0:25], True, True, ("E8", "ctb"), ("pc",), "C2")
+    Cc = TG[:, 20:25]
+    op("V", lambda e: e.tensor_tensor_scan(Cc, C2[:, 0:5], T["one5"][:, 0:5], 1.0, ALU.add, ALU.add), ("pc", "one5"), ("C",), ("C2",))
+    ts(T["a1"][:, 0:5], C2[:, 5:10], 1.0, 99.0, ALU.not_equal, ALU.mult, r=("pc",), w=("a1",), banks=("C2",))
+    ts(T["a2"][:, 0:5], C2[:, 5:10], 2.0, 99.0, ALU.not_equal, ALU.mult, r=("pc",), w=("a2",), banks=("C2",))
+    ts(T["z0"][:, 0:1], C2[:, 0:1], 0.0, 99.0, ALU.is_equal, ALU.mult, r=("pc",), w=("z0",), banks=("C2",))
+    tt(T["tx"][:, 0:5], Cc, C2[:, 10:25:3], ALU.subtract, r=("pc", "C"), w=("tx",), banks=("C2",))
+    tt(TG[:, 10:15], Cc, C2[:, 11:25:3], ALU.subtract, r=("pc", "C"), w=("tm0",), banks=("C2",))
+    tt(TG[:, 15:20], Cc, C2[:, 12:25:3], ALU.subtract, r=("pc", "C"), w=("tm1",), banks=("C2",))
+    tt(TG[:, 0:5], T["tx"][:, 0:5], T["a1"][:, 0:5], ALU.subtract, r=("tx", "a1"), w=("t1",))
+    tt(TG[:, 6:10], T["tx"][:, 1:5], T["a2"][:, 1:5], ALU.subtract, r=("tx", "a2"), w=("t2",))
+    ts(TG[:, 5:6], T["tx"][:, 0:1], T["a2"][:, 0:1], T["z0"][:, 0:1], ALU.subtract, ALU.subtract, r=("tx", "a2", "z0"), w=("t20",))
+    tg = ("t1", "t2", "t20", "tm0", "tm1", "C")
+    ts(NE[:, 0:20], TG[:, 0:20], lc_, None, ALU.not_equal, r=tg + ("l",), w=("NE",))
+    ts(OH[:, 0:25], TG[:, 0:25], lc_, None, ALU.is_equal, r=tg + ("l",), w=("OH",))
+    act(T["c23"][:, 0:5], Cc, ACT.Identity, ("C",), ("c23",), bias=23.0, scale=-1.0)
+    ts(T["born"][:, 0:5], Cc, lc_, None, ALU.is_gt, r=("C", "l"), w=("born",))
+    ts(XE[:, 10:15], Cc, lc_, None, ALU.is_le, r=("C", "l"), w=("nb",))
+    tt(T["nm2"][:, 0, :], NE[:, 10:15], NE[:, 15:20], ALU.mult, r=("NE",), w=("nm0",))
+    act(T["nm2"][:, 1, :], T["nm2"][:, 0, :], ACT.Copy, ("nm0",), ("nm1",))
+    tt(T["k0"][:, 0:5], OH[:, 10:15], NE[:, 15:20], ALU.mult, r=("OH", "NE"), w=("k0",))
+
+    def lists(t, nf, X, codes, pa, ba, pp, bp):
+        G, held, wts, H = T["G" + t], T["held" + t], T["wts" + t], T["H" + t]
+        sl = ("sh" + t, "lg" + t)
+        tt(held[:], X[:, 0:nf], X[:, nf:2 * nf], ALU.add, r=sl, w=("held" + t,))
+        tt(G[:, 0:2, :], X[:, 0:2 * nf], T["nm2"][:, :, 0:nf], ALU.mult, r=sl + ("nm0", "nm1"), w=("G01" + t,))
+        tt(G[:, 2, :], held[:], T["k0"][:, 0:nf], ALU.mult, r=("held" + t, "k0"), w=("G2" + t,))
+        tt(G[:, 3, :], held[:], OH[:, 15:15 + nf], ALU.mult, r=("held" + t, "OH"), w=("G3" + t,))
+        a_, b_, c_ = [pa[:, 64 + i * nf:64 + (i + 1) * nf] for i in range(3)]
+        abc = ("abc" + t,)
+        mm(a_, OO, held[:], True, False, ("OO", "held" + t), abc, ba)
+        mm(a_, NO, G[:, 1, :], False, False, ("NO", "G01" + t), abc, ba)
+        mm(a_, NL, G[:, 0, :], False, True, ("NL",), abc, ba)
+        mm(b_, OO, held[:], True, False, (), abc, ba)
+        mm(b_, NU, G[:, 1, :], False, True, ("NU",), abc, ba)
+        mm(c_, OO, G[:, 3, :], True, True, ("G3" + t,), abc, ba)
+        act(wts[:, 0:3, :], pa[:, 64:64 + 3 * nf], ACT.Exp, abc + ("wts30",), ("wts" + t,), (ba,), scale=LN8)
+        hk = []
+        for i, (buf, code, key) in enumerate(codes):
+            ts(T[buf][:], G[:], code, None, ALU.mult, r=("G01" + t, "G2" + t, "G3" + t, key), w=(buf,))
+            tt(H[:, :, i, :], T[buf][:], wts[:], ALU.mult, r=(buf, "wts" + t, "wts3" + t), w=("H" + buf,))
+            hk.append("H" + buf)
+        for s in range(4):
+            mm(pp[:, 16:16 + nf * len(codes)], OO, H[:, s, :, :], s == 0, s == 3, tuple(hk), ("pack" + t,), bp)
+
+    ts(T["XE0"][:, 0:1], T["born"][:, 0:1], NE[:, 0:1], NE[:, 5:6], ALU.mult, ALU.mult, r=("born", "NE"), w=("sh0",))
+    ts(T["XE0"][:, 1:2], TG[:, 0:1], lc_, None, ALU.is_equal, r=("t1", "l"), w=("lg0",))
+    lists("0", 1, T["XE0"], (("Gp0", T["PH"][:, F - 1:F], "PH4"),), T["X1"], "X1", T["X2"], "X2")
+
+    op("V", lambda e: e.tensor_tensor_scan(R[:, 1:6], NE[:, 0:5], NE[:, 5:10], 1.0, ALU.mult, ALU.mult), ("NE",), ("R",))
+    mm(C0[:, 1:2], OO, OH[:, 0:1], True, True, ("OO", "OH"), ("Lb1",), "C0")
+    mm(C2[:, 32:37], Id, T["c23"][:, 0:5], True, False, ("I", "c23"), ("S1",), "C2")
+    mm(C2[:, 32:37], NU, R[:, 0:5], False, True, ("NU", "R", "R0"), ("S1",), "C2")
+    tt(T["f1"][:, 0:5], OH[:, 0:5], R[:, 0:5], ALU.mult, r=("OH", "R", "R0"), w=("f1",))
+    cp(SS[:, :, 0], C2[:, 32:37], r=("S1",), w=("SS0",), banks=("C2",))
+    tt(SS[:, :, 1], C2[:, 32:37], T["f1"][:, 0:5], ALU.mult, r=("S1", "f1"), w=("SS1",), banks=("C2",))
+    act(ZU[:, 0, 1:2], OH[:, 0:1], ACT.Copy, ("OH",), ("U0",))
+    ts(LP[:, 1:2], OH[:, 0:1], NE[:, 6:7], None, ALU.mult, r=("OH", "NE"), w=("LP1",))
+    for f in range(1, F):
+        cb, nb = (C0, "C0") if f % 2 else (C1, "C1")
+        ts(ZU[:, f, :], (SS if f == 1 else T["SZ"])[:, f, :], cb[:, f:f + 1], None, ALU.is_gt,
+           r=("SS0", "SS1", "Lb%d" % f) + (("SZ%d" % f,) if f > 1 else ()), w=("Z%d" % f, "U%d" % f), banks=(nb,))
+        if f + 1 < F:
+            ts(T["SZ"][:, f + 1, :], SS[:, f + 1, :], ZU[:, f, 0:1], None, ALU.mult, r=("SS0", "SS1", "Z%d" % f), w=("SZ%d" % (f + 1),))
+            cb, nb = (C1, "C1") if f % 2 else (C0, "C0")
+            mm(cb[:, f + 1:f + 2], OO, LP[:, f:f + 1], True, False, ("LP%d" % f,), ("Lb%d" % (f + 1),), nb)
+            mm(cb[:, f + 1:f + 2], OO, ZU[:, f, 1:2], False, True, ("U%d" % f,), ("Lb%d" % (f + 1),), nb)
+            ts(LP[:, f + 1:f + 2], LP[:, f:f + 1], ZU[:, f, 1:2], NE[:, 6 + f:7 + f], ALU.add, ALU.mult,
+               r=("LP%d" % f, "U%d" % f, "NE"), w=("LP%d" % (f + 1),))
+    tt(T["RB"][:, 0:5], R[:, 1:6], T["born"][:, 0:5], ALU.mult, r=("R", "born"), w=("RB",))
+    tt(T["PH"][:, 0:4], OH[:, 20:24], T["ph5"][:, 0:4], ALU.mult, r=("OH", "ph5"), w=("PH",))
+    op("V", lambda e: e.tensor_reduce(T["pe"][:, 0:1], T["PH"][:, 0:5], AxisListType.X, ALU.add), ("PH", "PH4"), ("phys",))
+    allz = tuple("Z%d" % f for f in range(F))
+    allu = tuple("U%d" % f for f in range(F)) + tuple("LP%d" % f for f in range(F))
+    tt(XE[:, 0:5], ZU[:, :, 0], T["RB"][:, 0:5], ALU.mult, r=allz + ("RB",), w=("sh",))
+    tt(XE[:, 5:10], ZU[:, :, 1], LP[:, 0:5], ALU.add, r=allu, w=("lg",))
+    op("V", lambda e: e.tensor_reduce(T["pe"][:, 1:2], XE[:, 0:16], AxisListType.X, ALU.add), ("sh", "lg", "nb", "XEc"), ("E",))
+    lists("", F, XE, (("Gp", T["pe"][:, 0:1], "phys"), ("Ge", T["pe"][:, 1:2], "E")), C2, "C2", C1, "C1")
+    ts(T["s1"][:, 0:5], C1[:, 16:21], 0.125, -0.4375, ALU.mult, ALU.add, r=("pack",), w=("s1",), banks=("C1",))
+    ts(T["s2"][:, 0:5], T["s1"][:, 0:5], 7, None, ALU.bitwise_and, r=("s1",), w=("s2",))
+    ts(T["s3"][:, 0:5], T["s2"][:, 0:5], 2.0, float(MW), ALU.max, ALU.mult, r=("s2",), w=("s3",))
+
+    ND, idx, VN = T["ND"], T["idx"], T["VN"]
+    ab, vv = ("ia", "ib"), ("vy", "vx")
+    for f0, f1 in ((0, 1), (1, F)):
+        t, fs = "%d" % f0, slice(f0, f1)
+        ts(ND[:, fs, 0, :], T["lia"][:, fs], 7.0, None, ALU.is_lt, r=ab, w=("ND0" + t,))
+        act(ND[:, fs, 1, :], ND[:, fs, 0, :], ACT.Copy, ("ND0" + t,), ("ND1" + t,))
+        tt(T["ibn"][:, fs], T["lib"][:, fs], ND[:, fs, 0, :], ALU.mult, r=ab + ("ND0" + t,), w=("ibn" + t,))
+        tt(idx[:, fs, 0, :], T["lia"][:, fs], ND[:, fs, 0, :], ALU.mult, r=ab + ("ND0" + t,), w=("idx0" + t,))
+        act(T["mx"][:, fs], T["ibn"][:, fs], ACT.Abs, ("ibn" + t,), ("mx" + t,), bias=-1.0)
+        ts(T["e1"][:, fs], T["ibn"][:, fs], 2.0, None, ALU.is_ge, r=("ibn" + t,), w=("e1" + t,), k=0.5)
+        tt(idx[:, fs, 1, :], T["mx"][:, fs], T["e1"][:, fs], ALU.add, r=("mx" + t, "e1" + t), w=("idx1" + t,))
+        act(T["w"][:, fs], idx[:, fs], ACT.Exp, ("idx0" + t, "idx1" + t, "wts30"), ("w" + t,), scale=-LN8)
+    for f in range(F):
+        t = "%d" % min(f, 1)
+        tt(VN[:, f, 0:64], T["lvy"][:, f], ND[:, f], ALU.mult, r=vv + ("ND0" + t, "ND1" + t), w=("VNy%d" % f,))
+        tt(VN[:, f, 64:128], T["lvx"][:, f], ND[:, f], ALU.mult, r=vv + ("ND0" + t, "ND1" + t), w=("VNx%d" % f,))
+    for j in range(4):
+        sg = 0.5 if j % 2 else -0.5
+        act(T["D4"][:, 1:F, 32 * j:32 * j + 32], ND[:, 1:F, 0, :], ACT.Identity, ("ND01",), ("D4%d" % j,), bias=-sg, scale=sg)
+
+    MS, B, Y, P1, AD, OFF, ML, RC = T["MS"], T["B"], T["Y"], T["P1"], T["AD"], T["OFF"], T["ML"], T["RC"]
+
+    def addresses(f):
+        s, t = "%d" % f, "%d" % min(f, 1)
+        m0 = (f + 1) * MW
+        act(T["nv"][:, f, :], idx[:, f], ACT.Relu, ("idx0" + t, "idx1" + t), ("nv" + s,), bias=-5.0 * (f + 1), scale=float(f + 1))
+        pk, pb, pkey = (C1, "C1", "pack") if f else (T["X2"], "X2", "pack0")
+        ts(Y[:, f, 32:96], T["w"][:, f], pk[:, 16 + f:17 + f], -0.4375, ALU.mult, ALU.add, r=("w" + t, pkey), w=("Yp" + s,), banks=(pb,))
+        ts(Y[:, f, 0:32], T["w"][:, f, 0, :], C1[:, 21 + f:22 + f], -0.4375, ALU.mult, ALU.add, r=("w" + t, "pack"), w=("Ye" + s,), banks=("C1",))
+        if f:
+            ts(B[:, f, :], Y[:, f, :], 7, None, ALU.bitwise_and, r=("Yp" + s, "Ye" + s), w=("B" + s,))
+        else:
+            ts(B[:, f, 32:96], Y[:, f, 32:96], 7, None, ALU.bitwise_and, r=("Yp" + s,), w=("B" + s,))
+            ts(MS[:, m0:m0 + 64], Y[:, f, 0:64], 7, None, ALU.bitwise_and, r=("Yp" + s, "Ye" + s), w=("MS1a",))
+        tt(T["PB"][:, f, :], B[:, f, 32:96], T["nv"][:, f, :], ALU.subtract, r=("B" + s, "nv" + s), w=("PB" + s,))
+        p1 = P1[:, 0:128]
+        mm(p1, Id, T["c128"][:, 0:128], True, False, ("I", "c128"), ("P1",), "P1")
+        mm(p1, Id, T["K1"][:], False, False, k1, ("P1",), "P1")
+        mm(p1, Id, VN[:, f], False, f == 0, ("VNy" + s, "VNx" + s), ("P1",), "P1")
+        if f:
+            mw = MS[:, 0:m0]
+            mk = tuple("MS%d%s" % (j, u) for j in range(1, f + 1) for u in "ab") + ("MS0", "ML" + s)
+            ts(ML[:, f, :], T["CL"][:], T["s3"][:, f:f + 1], None, ALU.add, r=cl + ("s3",), w=("ML" + s,))
+            act(T["thr"][:, f, :], ND[:, f], ACT.Identity, ("ND01", "ND11"), ("thr" + s,), bias=float(f), scale=99.0)
+            tt(T["h"][:, f, :], mw.indirect(ML[:, f, 8:16]), T["D4"][:, f, :], ALU.mult, r=mk + ("D40", "D41", "D42", "D43"), w=("h" + s,))
+            tt(T["ok"][:, f, :], mw.indirect(ML[:, f, 0:4]), T["thr"][:, f, :], ALU.is_ge, r=mk + ("thr" + s,), w=("ok" + s,))
+            tt(T["df"][:, f, :], mw.indirect(ML[:, f, 4:8]), B[:, f, 0:64], ALU.subtract, r=mk + ("B" + s,), w=("df" + s,))
+            tt(T["M3"][:, f, 0:64], T["ok"][:, f, :], T["df"][:, f, :], ALU.mult, r=("ok" + s, "df" + s), w=("m" + s,))
+            mm(p1, Id, T["h"][:, f, :], False, True, ("h" + s,), ("P1",), "P1")
+        for i, hi in ((0, 159.0), (1, 143.0)):
+            ts(RC[:, f, 64 * i:64 * i + 64], P1[:, 64 * i:64 * i + 64], 128.0, hi, ALU.max, ALU.min, r=("P1",), w=("RC%d%s" % (i, s),), banks=("P1",))
+        if f + 1 < F:
+            tt(MS[:, m0 + 64:m0 + MW], P1[:, 0:96], T["K2"][:], ALU.subtract, r=("P1", "K2"), w=("MS%db" % (f + 1),), banks=("P1",), k=1.0)
+            if f:
+                tt(MS[:, m0:m0 + 64], T["M3"][:, f, 0:64], B[:, f, 0:64], ALU.add, r=("m" + s, "B" + s), w=("MS%da" % (f + 1),))
+        ad = AD[:, 0:64]
+        mm(ad, T["I16"][:], RC[:, f, 0:64], True, False, ("I16", "RC0" + s), ("AD",), "AD")
+        mm(ad, Id, RC[:, f, 64:128], False, False, ("RC1" + s,), ("AD",), "AD")
+        if f:
+            mm(ad, T["I512"][:], T["M3"][:, f, 32:96], False, False, ("I512", "m" + s, "M3z"), ("AD",), "AD")
+        mm(ad, T["I512"][:], T["PB"][:, f, :], False, True, ("I512", "PB" + s), ("AD",), "AD")
+        ts(OFF[:, f, :], ad, 512.0 * (f + 1) - 2176.0, None, ALU.add, r=("AD",), w=("OFF" + s,), banks=("AD",))
+
+    def pixels(f):
+        s = "%d" % f
+        end = f + 1 == F
+        sh = 0 if end else 16 * (f + 1)
+        rot, nrot = T["W2"][:, sh:sh + 128], T["N2"][:, sh:sh + 128]
+        ww = win[:, (V0 - f) * P:(SB + 3 + f) * P]
+        wk = ("blank", "pic0", "pic1", "OFF" + s) + tuple("V%d" % j for j in range(f + 1)) + tuple("F%d" % j for j in range(f))
+        for c, (a, b, _) in enumerate(CH):
+            X, xb = T["X%d" % c][:, 0:b - a], "X%d" % c
+            mm(X, rot, T["rs"][:, f * P + a:f * P + b], True, False, ("I", "I2", "rs" + s), (xb,), xb)
+            mm(X, Id, T["c128"][:, 0:b - a], False, False, ("c128",), (xb,), xb)
+            mm(X, Id, T["qm"][:, 0:b - a], False, False, ("qm",), (xb,), xb)
+        for c, (a, b, _) in enumerate(CH):
+            ts(T["gp"][:, a:b], ww.indirect(OFF[:, f, a // 16:b // 16]), 255.0, 0.5, ALU.min, ALU.mult, r=wk, w=("gp%d" % c,), k=1.56, x=50.0)
+            act(T["gq"][:, a:b], ww.indirect(OFF[:, f, 32 + a // 16:32 + b // 16]), ACT.Relu, wk, ("gq%d" % c,), bias=127.5, scale=-0.5, k=1.56, x=65.0)
+        for c, (a, b, who) in enumerate(CH):
+            X, xb = T["X%d" % c][:, 0:b - a], "X%d" % c
+            o, ok = T["snd"][:, f * P + a:f * P + b], ("snd%s%d" % (s, c),)
+            mm(X, rot, T["gp"][:, a:b], False, False, ("gp%d" % c,), (xb,), xb)
+            mm(X, nrot, T["gq"][:, a:b], False, end, ("N2", "gq%d" % c), (xb,), xb)
+            if end:
+                ts(T["yy"][:, a:b], X, MAGIC, MAGIC + 255.0, ALU.add, ALU.min, r=(xb,), w=("yy%d" % c,), banks=(xb,))
+                act(o, T["yy"][:, a:b], ACT.Relu, ("yy%d" % c,), ok, bias=-MAGIC)
+                dma("A" if c + 1 == len(CH) else "S", T.y[:, f * P + a:f * P + b], o, "dy", r=ok, nbytes=(b - a) * 256)
+                continue
+            mm(X, Id, T["cM"][:, 0:b - a], False, True, ("cM",), (xb,), xb)
+            if who == "V":
+                ts(o, X, -MAGIC, 0.0, ALU.add, ALU.max, r=(xb,), w=ok, banks=(xb,))
+            else:
+                act(o, X, ACT.Relu, (xb,), ok, (xb,), bias=-MAGIC)
+        if not end:
+            sk = tuple("snd%s%d" % (s, j) for j in range(len(CH)))
+            send(f + 1, T["snd"][:, f * P:(f + 1) * P], sk)
+            mm(C0[:], T["W2"][:, 128 - sh:256 - sh], T["snd"][:, f * P:(f + 1) * P], True, True, sk, ("UN",), "C0")
+            act(T["tb"][:], C0[:], ACT.Relu, ("UN",), ("tb",), ("C0",), bias=255.0, scale=-1.0)
+            act(slot(SB + 3 + f), T["tb"][:], ACT.Identity, ("tb",), ("F" + s,), bias=255.0, scale=-1.0)
+            dma("S", T.y[:, f * P:(f + 1) * P], slot(SB + 3 + f), "dy", r=("F" + s,), nbytes=131072)
+
+    for f in range(F):
+        addresses(f)
+    for f in range(F):
+        pixels(f)
+    return ops
+
+
+def plan(ops):
+    n = len(ops)
+    pre = [o["deps"] | o["soft"] | ({o["order"]} if "order" in o else set()) for o in ops]
+    suc = [[] for _ in ops]
+    for k in range(n):
+        for d in pre[k]:
+            suc[d].append(k)
+
+    def gap(d, k):
+        if (ops[d]["q"] == "P" and ops[k]["q"] == "P") or (d == ops[k].get("order") and d not in ops[k]["deps"]):
+            return 0.0
+        return ops[d]["lat"] + HOP
+
+    def sweep(order, before, rev):
+        start, busy = [0.0] * n, {}
+        for k in order:
+            t = ops[k]["lat"] if rev and not before[k] else 0.0
+            for d in before[k]:
+                t = max(t, start[d] + ops[d]["dur"] + (gap(k, d) if rev else gap(d, k)))
+            iv = busy.setdefault(ops[k]["q"], [])
+            for a, b in iv:
+                if t + ops[k]["dur"] <= a:
+                    break
+                t = max(t, b)
+            start[k] = t
+            iv.append((t, t + ops[k]["dur"]))
+            iv.sort()
+        return start
+
+    start, best = sweep(range(n), pre, False), None
+    for _ in range(6):
+        back = sweep(sorted(range(n), key=lambda j: (-start[j] - ops[j]["dur"], -j)), suc, True)
+        start = sweep(sorted(range(n), key=lambda j: (-back[j] - ops[j]["dur"], j)), pre, False)
+        end = max(start[k] + ops[k]["dur"] + ops[k]["lat"] for k in range(n))
+        if best is None or end < best[0]:
+            best = (end, start)
+    start = best[1]
+    return sorted(range(n), key=lambda j: (start[j], j)), start
+
+
+def rank_program(g, core, T, topo):
+    if T.rank_of(core) is None:
+        return
+    ops = build(T, topo, core)
+    order, _ = plan(ops)
+    eng = {"V": g.vector, "A": g.scalar, "P": g.tensor, "G": g, "S": g.sync}
+    total, many = {}, {}
+    for o in ops:
+        if o["sem"]:
+            total[o["sem"]] = total.get(o["sem"], 0) + o["inc"]
+            many[o["sem"]] = many.get(o["sem"], 0) + 1
+    pos, cnt = {}, {}
+    for k in order:
+        q = ops[k]["q"]
+        if not ops[k]["sem"]:
+            cnt[q] = cnt.get(q, 0) + 1
+            pos[k] = cnt[q]
+    known, clock, waits = {}, {}, {}
+    for k in order:
+        o = ops[k]
+        q = o["q"]
+        if q == "X":
+            clock[k] = {}
+            continue
+        kn = known.setdefault(q, {})
+        need = []
+        for d in sorted(o["deps"], key=lambda j: -pos.get(j, 0)):
+            dq, ds = ops[d]["q"], ops[d]["sem"]
+            if dq == "P" and q == "P":
+                continue
+            key, val = (ds, 1) if ds else ("n" + dq, pos[d])
+            if kn.get(key, 0) >= val:
+                continue
+            need.append(d)
+            kn[key] = val
+            if not ds or many[ds] == 1:
+                for kk, vv in clock[d].items():
+                    kn[kk] = max(kn.get(kk, 0), vv)
+        waits[k] = need
+        clock[k] = dict(kn)
+    signal = set(d for k in waits for d in waits[k] if not ops[d]["sem"])
+    val, cnt = {}, {}
+    for k in order:
+        if k in signal:
+            q = ops[k]["q"]
+            cnt[q] = cnt.get(q, 0) + 1
+            val[k] = cnt[q]
+    waited = set()
+    for k in order:
+        o = ops[k]
+        if o["q"] == "X":
+            continue
+        e = eng[o["q"]]
+        for d in waits[k]:
+            ds = ops[d]["sem"]
+            if ds:
+                e.wait_ge(T.sem[ds], total[ds])
+                waited.add(ds)
+            else:
+                e.wait_ge(T.sem["n" + ops[d]["q"]], val[d])
+        ins = o["fn"](e)
+        if k in signal:
+            ins.then_inc(T.sem["n" + o["q"]], 1)
+        elif o["sem"] and o["q"] != "G":
+            ins.then_inc(T.sem[o["sem"]], 16)
+    for s in sorted(total):
+        if s not in waited:
+            (g if s == "ls" else g.sync).wait_ge(T.sem[s], total[s])

@@ -3,8 +3,10 @@ from concourse.mybir import AluOpType as ALU, AxisListType, ActivationFunctionTy
 
 F = 5
 P = 512
-CH = ((0, 192, "V"), (192, 384, "A"), (384, 512, "V"))
-CW = 192
+CH = ((0, 192, "A"), (192, 352, "A"), (352, 512, "A"))
+ONE, TWO = ((0, 3),), ((0, 1), (1, 3))
+SENDS = (ONE, ONE, ONE, ONE, ONE)
+CW = 256
 MAGIC = 12582912.0
 LN8 = math.log(8.0)
 V0 = F - 1
@@ -19,7 +21,8 @@ def _sb(shape, dt):
 BF, F32, I32 = "bfloat16", "float32", "int32"
 SCRATCH = {
     "win": _sb([12 * P], BF), "rs": _sb([F * P], BF), "snd": _sb([F * P], BF),
-    "gp": _sb([P], BF), "gq": _sb([P], BF), "yy": _sb([P], F32), "tb": _sb([P], BF),
+    "win2": _sb([11 * P], BF), "rs2": _sb([(F - 1) * P], BF), "OF2": _sb([F - 1, 64], "uint16"),
+    "gp": _sb([P], BF), "gq": _sb([P], BF), "yy": _sb([P], F32), "tb": _sb([(F - 1) * P], BF),
     "ctl": _sb([32], I32), "ctb": _sb([32], BF),
     "lia": _sb([F, 32], I32), "lib": _sb([F, 32], I32), "lvy": _sb([F, 64], I32), "lvx": _sb([F, 64], I32),
     "cA": _sb([128], F32), "cB": _sb([128], F32), "pi": _sb([2], I32), "pj": _sb([4], I32), "col": _sb([12], F32),
@@ -48,20 +51,45 @@ SCRATCH = {
 }
 for _n in ("X0", "X1", "X2", "C0", "C1", "C2", "P1", "AD"):
     SCRATCH[_n] = ("psum", [128, 512], F32)
-SEMAPHORES = (["nV", "nA", "nP", "nG", "dctl", "dab", "dv", "dp0", "dp1", "dr0", "dr1", "dy", "ls0", "ls"]
-              + ["arr%d" % f for f in range(F)])
+SEMAPHORES = (["nV", "nA", "nP", "nG", "dctl", "dab", "dv", "dp0", "dp1", "dr0", "dr1", "dr2", "dy", "ls0", "ls1", "ls2", "ls3", "ls4", "ls", "pp", "rr1", "rr2", "rr3"]
+              + ["arr%d" % f for f in range(F)] + ["brr%d" % f for f in range(F - 1)] + ["of%d" % f for f in range(F - 1)])
 
-CYC = 1.04
-HOP = 110.0
+CYC = 1.25
+HOP = 200.0
+LINK = 1.0
+SWEEPS = 60
+F0 = 2
+YCA = ()
+PLAN = {}
+
+
+def joint(T, topo):
+    if not PLAN:
+        pair = sorted(T.cores[:2], key=lambda c: T.cores[T.rank_of(c) - 1] in topo.cores_of(c))
+        parts = [build(T, topo, c) for c in pair]
+        names = [{o["name"][0]: k for k, o in enumerate(p) if o["name"]} for p in parts]
+        base, ops = (0, len(parts[0])), []
+        for i, p in enumerate(parts):
+            for o in p:
+                u = dict(o, q=o["q"], lane=o.get("lane", o["q"]) + str(i), deps={d + base[i] for d in o["deps"]}, soft={d + base[i] for d in o["soft"]})
+                if "order" in o:
+                    u["order"] = o["order"] + base[i]
+                if "link" in o:
+                    u["soft"].add(names[1 - i][o["link"]] + base[1 - i])
+                ops.append(u)
+        order, start = plan(ops)
+        PLAN[False] = [k for k in order if k < base[1]]
+        PLAN[True] = [k - base[1] for k in order if k >= base[1]]
+        PLAN["ops"], PLAN["start"] = ops, start
+    return PLAN
 
 
 def build(T, topo, core):
     rank = T.rank_of(core)
     n = len(T.cores)
     nxt, prv = T.cores[(rank + 1) % n], T.cores[(rank - 1) % n]
-    rid, pid = topo.addr(nxt, core)
-    emask = topo.mask(core, nxt)
-    n_out, n_in = len(topo.engines(core, nxt)), len(topo.engines(prv, core))
+    nx2 = T.cores[(rank + 2) % n]
+    second = prv in topo.cores_of(core)
     ops, wr, rd, bk, lastdma = [], {}, {}, {}, {}
 
     def op(q, fn, r=(), w=(), banks=(), dur=70.0, lat=0.0, sem=None, inc=0, soft=()):
@@ -74,8 +102,8 @@ def build(T, topo, core):
                 deps.add(wr[key])
             deps.update(rd.get(key, ()))
         for b in banks:
-            deps.update(o for qq, o in bk.get(b, {}).items() if qq != q or q == "P")
-            bk.setdefault(b, {})[q] = k
+            deps.update(o for qq, o in bk.get(b, ()) if qq != q or q == "P")
+            bk.setdefault(b, []).append((q, k))
         for key in r:
             rd.setdefault(key, []).append(k)
         for key in w:
@@ -119,13 +147,32 @@ def build(T, topo, core):
         lastdma[q] = k
         return k
 
-    def send(f, a, r):
+    def send(dst, out, a, sem, r, name, first=False, need=None):
+        rid, pid = topo.addr(dst, core)
+        emask, ls = topo.mask(core, dst), "ls0" if first else need or "ls"
+        fn = lambda e: e.remote_dma(out, a, T.sem[sem], T.sem[ls], pid, rid, emask)
+        k = op("G", fn, r, (name,), (), 400.0, 3000.0 if first else 1500.0, ls, len(topo.engines(core, dst)))
+        return k
+
+    def arrive(src, sem, key, like=None, cols=0, rel=None):
+        k = op("X", None, (), (key,), (), LINK * (300.0 + cols * 2.5) if cols else 0.0, 0.0, sem, len(topo.engines(src, core)), () if like is None else (like,))
+        if rel:
+            ops[k]["link"], ops[k]["lane"], ops[k]["dur"] = rel[0], "Y" if rel[1] else key, 150.0 + rel[1] * 1.3 if rel[1] else 0.0
+
+    def view_out(f, a, c0, c1, r, first=False):
         s = (V0 - f) * P
-        out = T["win"][:, s:s + P]
-        ls = "ls0" if f == 0 else "ls"
-        fn = lambda e: e.remote_dma(out, a, T.sem["arr%d" % f], T.sem[ls], pid, rid, emask)
-        k = op("G", fn, r, ("sent%d" % f,), (), 400.0, (3000.0 if f == 0 else 1500.0) + P * 3.0, ls, n_out)
-        op("X", None, (), ("V%d" % f,), (), 0.0, 0.0, "arr%d" % f, n_in, (k,))
+        if F0 <= f < F - 1:
+            k = send(nx2, T["win2"][:, s + c0:s + c1], a, "brr%d" % f, r, "sentB%d_%d" % (f, c0), first)
+            arrive(nx2, "brr%d" % f, "W%d_%d" % (f, c0), k, c1 - c0)
+            views["W"].append("W%d_%d" % (f, c0))
+        else:
+            k = None
+        j = send(nxt, T["win"][:, s + c0:s + c1], a, "arr%d" % f, r, "sentA%d_%d" % (f, c0), first and F0 > 0, "ls%d" % f if f else None)
+        if k and f < F - 2:
+            ops[j]["order"] = k
+        elif k:
+            ops[k]["order"] = j
+        arrive(nx2, None, "A%d_%d" % (f, c0), j, c1 - c0)
 
     win = T["win"]
     slot = lambda s: win[:, s * P:(s + 1) * P]
@@ -139,8 +186,39 @@ def build(T, topo, core):
     dma("A", T["lvx"][:], T.vx[:], "dv", w=("vx",), nbytes=500000)
     dma("S", slot(SB + 1), T.pic0[:, 0:P], "dp0", w=("pic0",), nbytes=700000)
     dma("A", T["rs"][:, 0:P], T.res[:, 0:P], "dr0", w=("rs0",), nbytes=700000)
-    send(0, slot(SB + 2), ("pic1",))
-    dma("S", T["rs"][:, P:F * P], T.res[:, P:F * P], "dr1", r=("sent0",), w=["rs%d" % f for f in range(1, F)], nbytes=524288)
+    views = {"V": ["V0"], "W": []}
+    win2, rs2 = T["win2"], T["rs2"]
+    if second:
+        view_out(0, slot(SB + 2), 0, P, ("pic1",), True)
+        arrive(prv, "arr0", "V0", rel=("sent0", P))
+        arrive(prv, "pp", "pics2", rel=("sentp", P))
+        act(win2[:, (SB + 2) * P:(SB + 3) * P], slot(V0), ACT.Copy, ("V0",), ("pics3",))
+        for i in range(F0, F - 1):
+            arrive(prv, "rr%d" % i, "rs2_%d" % i, rel=("sentr%d" % i, P))
+        for f in range(F0, F - 1):
+            arrive(prv, "of%d" % f, "OF2_%d" % f, rel=("sento%d" % f, 64))
+        for f in range(1, F0 + 1):
+            arrive(prv, "arr%d" % f, "V%d" % f, rel=("sentv%d" % f, P))
+        s0key = "sentA0_0" if F0 else "sentB0_0"
+    else:
+        send(nxt, slot(V0), slot(SB + 2), "arr0", ("pic1",), "sent0", True)
+        for f in range(F):
+            for i, j in SENDS[f]:
+                arrive(prv, "arr%d" % f, "V%d" % f if i == 0 else "V%d_%d" % (f, i), rel=("A%d_%d" % (f, CH[i][0]), 0))
+        s0key = "sent0"
+    dma("S", T["rs"][:, P:3 * P], T.res[:, P:3 * P], "dr1", r=(s0key,), w=("rs1", "rs2"), nbytes=262144)
+
+    def after_send(f, key, k):
+        if f == 0:
+            dma("S", T["rs"][:, 3 * P:F * P], T.res[:, 3 * P:F * P], "dr2", r=(key,), w=("rs3", "rs4"), nbytes=262144)
+        if second:
+            return
+        more = [send(nxt, rs2[:, i * P:(i + 1) * P], T["rs"][:, i * P:(i + 1) * P], "rr%d" % i, ("rs%d" % i,), "sentr%d" % i)
+                for i in range(F0, F - 1) if (f == 0 and i < 3) or (f == F0 - 1 and i == 3)]
+        if f == 0:
+            more.append(send(nxt, win2[:, (SB + 1) * P:(SB + 2) * P], slot(SB + 1), "pp", ("pic0",), "sentp"))
+        for j in more:
+            ops[j]["order"] = k
 
     cA, cB, col, cc = T["cA"], T["cB"], T["col"], T["cc"]
     op("G", lambda e: e.iota(T["pi"][:, 0:1], [[1, 1]], 0, 1), w=("pi",), dur=200.0)
@@ -181,6 +259,8 @@ def build(T, topo, core):
         act(T["CL"][:, c0:c0 + m], cc[:, s0:s0 + m], ACT.Identity, ("cc", "lm"), ("CL%d" % c0,), bias=lm_, scale=16.0)
     cl = ("CL0", "CL2", "CL4", "CL10", "CL12", "CL14")
     ms(slot(SB), 128.0, ("blank",))
+    if second:
+        ms(win2[:, (SB - F0) * P:(SB + 1) * P], 128.0, ("blank2",))
     ms(T["qm"][:], -0.25, ("qm",))
     ms(T["c128"][:], 128.0, ("c128",))
     ms(T["cM"][:], MAGIC, ("cM",))
@@ -345,49 +425,102 @@ def build(T, topo, core):
             mm(ad, T["I512"][:], T["M3"][:, f, 32:96], False, False, ("I512", "m" + s, "M3z"), ("AD",), "AD")
         mm(ad, T["I512"][:], T["PB"][:, f, :], False, True, ("I512", "PB" + s), ("AD",), "AD")
         ts(OFF[:, f, :], ad, 512.0 * (f + 1) - 2176.0, None, ALU.add, r=("AD",), w=("OFF" + s,), banks=("AD",))
+        if not second and F0 <= f < F - 1:
+            send(nxt, T["OF2"][:, f, :], OFF[:, f, :], "of" + s, ("OFF" + s,), "sento" + s)
 
-    def pixels(f):
+    nch = range(len(CH))
+
+    def pixels(f, own):
         s = "%d" % f
         end = f + 1 == F
-        sh = 0 if end else 16 * (f + 1)
+        turn = (second or f < F0) and not end
+        sh = 16 * (f + 1) if turn else 0
         rot, nrot = T["W2"][:, sh:sh + 128], T["N2"][:, sh:sh + 128]
-        ww = win[:, (V0 - f) * P:(SB + 3 + f) * P]
-        wk = ("blank", "pic0", "pic1", "OFF" + s) + tuple("V%d" % j for j in range(f + 1)) + tuple("F%d" % j for j in range(f))
+        if own:
+            ww, off, rs, rk = win, OFF, T["rs"], "rs" + s
+            wk = ("blank", "pic0", "pic1", "OFF" + s) + tuple(views["V"]) + tuple(views.get("F", ()))
+        else:
+            ww, off, rs, rk = win2, T["OF2"], rs2, "rs2_%d" % f
+            wk = ("blank2", "pics2", "pics3", "OF2_" + s) + tuple(k for k in views["W"] if int(k[1]) <= f) + tuple("G%d" % j for j in range(f))
+        ww = ww[:, (V0 - f) * P:(SB + 3 + f) * P]
         for c, (a, b, _) in enumerate(CH):
             X, xb = T["X%d" % c][:, 0:b - a], "X%d" % c
-            mm(X, rot, T["rs"][:, f * P + a:f * P + b], True, False, ("I", "I2", "rs" + s), (xb,), xb)
-            mm(X, Id, T["c128"][:, 0:b - a], False, False, ("c128",), (xb,), xb)
+            mm(X, rot, rs[:, f * P + a:f * P + b], True, False, ("I", "I2", rk), (xb,), xb)
             mm(X, Id, T["qm"][:, 0:b - a], False, False, ("qm",), (xb,), xb)
         for c, (a, b, _) in enumerate(CH):
-            ts(T["gp"][:, a:b], ww.indirect(OFF[:, f, a // 16:b // 16]), 255.0, 0.5, ALU.min, ALU.mult, r=wk, w=("gp%d" % c,), k=1.56, x=50.0)
-            act(T["gq"][:, a:b], ww.indirect(OFF[:, f, 32 + a // 16:32 + b // 16]), ACT.Relu, wk, ("gq%d" % c,), bias=127.5, scale=-0.5, k=1.56, x=65.0)
+            ts(T["gp"][:, a:b], ww.indirect(off[:, f, a // 16:b // 16]), 255.0, 0.5, ALU.min, ALU.mult, r=wk, w=("gp%d" % c,), k=1.56, x=50.0)
+            act(T["gq"][:, a:b], ww.indirect(off[:, f, 32 + a // 16:32 + b // 16]), ACT.Relu, wk, ("gq%d" % c,), bias=127.5, scale=-0.5, k=1.56, x=65.0)
+        if end or (own and turn):
+            dst, name = T["snd"][:, f * P:(f + 1) * P], "snd"
+        elif own:
+            dst, name = slot(SB + 3 + f), "F"
+        else:
+            dst, name = slot(V0 - f - 1), "Vl"
+        sk = tuple("%s%s%d" % (name, s, j) for j in nch)
         for c, (a, b, who) in enumerate(CH):
             X, xb = T["X%d" % c][:, 0:b - a], "X%d" % c
-            o, ok = T["snd"][:, f * P + a:f * P + b], ("snd%s%d" % (s, c),)
+            o, ok = dst[:, a:b], sk[c:c + 1]
             mm(X, rot, T["gp"][:, a:b], False, False, ("gp%d" % c,), (xb,), xb)
             mm(X, nrot, T["gq"][:, a:b], False, end, ("N2", "gq%d" % c), (xb,), xb)
             if end:
-                ts(T["yy"][:, a:b], X, MAGIC, MAGIC + 255.0, ALU.add, ALU.min, r=(xb,), w=("yy%d" % c,), banks=(xb,))
+                ts(T["yy"][:, a:b], X, MAGIC + 128.0, MAGIC + 255.0, ALU.add, ALU.min, r=(xb,), w=("yy%d" % c,), banks=(xb,))
                 act(o, T["yy"][:, a:b], ACT.Relu, ("yy%d" % c,), ok, bias=-MAGIC)
                 dma("A" if c + 1 == len(CH) else "S", T.y[:, f * P + a:f * P + b], o, "dy", r=ok, nbytes=(b - a) * 256)
                 continue
             mm(X, Id, T["cM"][:, 0:b - a], False, True, ("cM",), (xb,), xb)
             if who == "V":
-                ts(o, X, -MAGIC, 0.0, ALU.add, ALU.max, r=(xb,), w=ok, banks=(xb,))
+                ts(o, X, 128.0 - MAGIC, 0.0, ALU.add, ALU.max, r=(xb,), w=ok, banks=(xb,))
             else:
-                act(o, X, ACT.Relu, (xb,), ok, (xb,), bias=-MAGIC)
-        if not end:
-            sk = tuple("snd%s%d" % (s, j) for j in range(len(CH)))
-            send(f + 1, T["snd"][:, f * P:(f + 1) * P], sk)
-            mm(C0[:], T["W2"][:, 128 - sh:256 - sh], T["snd"][:, f * P:(f + 1) * P], True, True, sk, ("UN",), "C0")
-            act(T["tb"][:], C0[:], ACT.Relu, ("UN",), ("tb",), ("C0",), bias=255.0, scale=-1.0)
-            act(slot(SB + 3 + f), T["tb"][:], ACT.Identity, ("tb",), ("F" + s,), bias=255.0, scale=-1.0)
-            dma("S", T.y[:, f * P:(f + 1) * P], slot(SB + 3 + f), "dy", r=("F" + s,), nbytes=131072)
+                act(o, X, ACT.Relu, (xb,), ok, (xb,), bias=128.0 - MAGIC)
+        if end:
+            return
+        ys = T.y[:, f * P:(f + 1) * P]
+        if not second:
+            views["V"].extend("V%d" % (f + 1) if i == 0 else "V%d_%d" % (f + 1, i) for i, j in SENDS[f + 1])
+            if not turn:
+                views.setdefault("F", []).extend(sk)
+                o = T["snd"][:, f * P:(f + 1) * P]
+                ts(o, dst, 255.0, None, ALU.min, r=sk, w=("yc" + s,), k=0.5)
+                dma("S", ys, o, "dy", r=("yc" + s,), nbytes=131072)
+                return
+            gone = "sentv%d" % (f + 1)
+            after_send(f, gone, send(nxt, slot(V0 - f - 1), dst, "arr%d" % (f + 1), sk, gone, False, "ls%d" % (f + 1)))
+        elif own:
+            for i, j in SENDS[f + 1]:
+                view_out(f + 1, dst[:, CH[i][0]:CH[j - 1][1]], CH[i][0], CH[j - 1][1], sk[i:j])
+            gone = "sentA%d_0" % (f + 1)
+            after_send(f, gone, None)
+        else:
+            views["V"].extend(sk)
+        if own:
+            mm(C0[:], T["W2"][:, 128 - sh:256 - sh], dst, True, True, sk, ("UN",), "C0")
+            views.setdefault("F", []).append("F" + s)
+            o = T["tb"][:, f * P:(f + 1) * P]
+            if f in YCA:
+                act(o, C0[:], ACT.Relu, ("UN",), ("tb" + s,), ("C0",), bias=255.0, scale=-1.0)
+                act(slot(SB + 3 + f), o, ACT.Identity, ("tb" + s,), ("F" + s,), bias=255.0, scale=-1.0)
+                dma("S", ys, slot(SB + 3 + f), "dy", r=("F" + s, gone), nbytes=131072)
+                return
+            act(slot(SB + 3 + f), C0[:], ACT.Copy, ("UN",), ("F" + s,), ("C0",))
+            ts(o, slot(SB + 3 + f), 255.0, None, ALU.min, r=("F" + s,), w=("yc" + s,), k=0.5)
+            dma("S", ys, o, "dy", r=("yc" + s, gone), nbytes=131072)
+        elif f + 2 < F:
+            turn_back(f, sk)
+
+    def turn_back(f, keys):
+        sh = 16 * (f + 1)
+        mm(C0[:], T["W2"][:, 128 - sh:256 - sh], slot(V0 - f - 1), True, True, keys, ("UN",), "C0")
+        act(win2[:, (SB + 3 + f) * P:(SB + 4 + f) * P], C0[:], ACT.Copy, ("UN",), ("G%d" % f,), ("C0",))
 
     for f in range(F):
         addresses(f)
     for f in range(F):
-        pixels(f)
+        pixels(f, True)
+        if second and F0 <= f < F - 1:
+            pixels(f, False)
+        elif second and f < F0:
+            views["V"].append("V%d" % (f + 1))
+            turn_back(f, ("V%d" % (f + 1),))
     return ops
 
 
@@ -404,13 +537,22 @@ def plan(ops):
             return 0.0
         return ops[d]["lat"] + HOP
 
-    def sweep(order, before, rev):
+    def sweep(prio, before, after, rev):
         start, busy = [0.0] * n, {}
-        for k in order:
-            t = ops[k]["lat"] if rev and not before[k] else 0.0
+        left = [len(b) for b in before]
+        ready = [(prio[k], k) for k in range(n) if not left[k]]
+        while ready:
+            top = min(ready)
+            ready.remove(top)
+            k = top[1]
+            for s in after[k]:
+                left[s] -= 1
+                if not left[s]:
+                    ready.append((prio[s], s))
+            t = max(ops[k]["lat"], ops[k].get("tail", 0.0)) if rev else ops[k].get("rel", 0.0)
             for d in before[k]:
                 t = max(t, start[d] + ops[d]["dur"] + (gap(k, d) if rev else gap(d, k)))
-            iv = busy.setdefault(ops[k]["q"], [])
+            iv = busy.setdefault(ops[k]["lane"], [])
             for a, b in iv:
                 if t + ops[k]["dur"] <= a:
                     break
@@ -420,13 +562,30 @@ def plan(ops):
             iv.sort()
         return start
 
-    start, best = sweep(range(n), pre, False), None
-    for _ in range(6):
-        back = sweep(sorted(range(n), key=lambda j: (-start[j] - ops[j]["dur"], -j)), suc, True)
-        start = sweep(sorted(range(n), key=lambda j: (-back[j] - ops[j]["dur"], j)), pre, False)
-        end = max(start[k] + ops[k]["dur"] + ops[k]["lat"] for k in range(n))
-        if best is None or end < best[0]:
-            best = (end, start)
+    end = lambda st: max(st[k] + ops[k]["dur"] + max(ops[k]["lat"], ops[k].get("tail", 0.0)) for k in range(n))
+    rk, seed = [0.0] * n, [12345]
+    left = [len(s) for s in suc]
+    todo = [k for k in range(n) if not left[k]]
+    while todo:
+        k = todo.pop()
+        rk[k] = ops[k]["dur"] + max([gap(k, s) + rk[s] for s in suc[k]] + [ops[k]["lat"]])
+        for d in pre[k]:
+            left[d] -= 1
+            if not left[d]:
+                todo.append(d)
+
+    def jit(a):
+        seed[0] = (seed[0] * 1103515245 + 12345) % 2147483648
+        return a * seed[0] / 2147483648.0
+
+    start = sweep([-r for r in rk], pre, suc, False)
+    best = (end(start), start)
+    for it in range(SWEEPS):
+        a, start = 400.0 * (it % 3 > 0), best[1]
+        back = sweep([jit(a) - start[j] - ops[j]["dur"] for j in range(n)], suc, pre, True)
+        start = sweep([jit(a) - back[j] - ops[j]["dur"] for j in range(n)], pre, suc, False)
+        if end(start) < best[0]:
+            best = (end(start), start)
     start = best[1]
     return sorted(range(n), key=lambda j: (start[j], j)), start
 
@@ -435,7 +594,7 @@ def rank_program(g, core, T, topo):
     if T.rank_of(core) is None:
         return
     ops = build(T, topo, core)
-    order, _ = plan(ops)
+    order = joint(T, topo)[T.cores[T.rank_of(core) - 1] in topo.cores_of(core)]
     eng = {"V": g.vector, "A": g.scalar, "P": g.tensor, "G": g, "S": g.sync}
     total, many = {}, {}
     for o in ops:

@@ -1,65 +1,56 @@
 import math
-from concourse.mybir import AluOpType as ALU, AxisListType, ActivationFunctionType as ACT
+from concourse.mybir import AluOpType as ALU, ActivationFunctionType as ACT
 
 F = 5
 P = 512
-CH = ((0, 192, "A"), (192, 352, "A"), (352, 512, "A"))
-ONE, TWO = ((0, 3),), ((0, 1), (1, 3))
-SENDS = (ONE, ONE, ONE, ONE, ONE)
+CH = ((0, 192), (192, 384), (384, 512))
 CW = 256
 MAGIC = 12582912.0
 LN8 = math.log(8.0)
 V0 = F - 1
 SB = F
-MW = 160
+MW = 96
+CFG = {
+    "remake": {False: (1, 3), True: (1, 3)},
+    "finish": {(1, True): "AVV", (3, True): "AVV", (1, False): "AVA", (3, False): "AVA", (0, True): "AVA", (2, True): "AVA"},
+    "parts": ((0, 3),),
+    "cases": ((0.85, 220.0, 1.0), (1.05, 150.0, 1.1)), "polish": 20000, "heat": 80.0, "marks": {"A": 0.4, "o": 0.2}, "ahead": False,
+    "late": 2, "copies": "VA", "rate": 34.0, "split": True,
+    "pair": {1: (("X0", 256), ("C2", 0), ("C1", 0)), 3: (("P1", 0), ("AD", 0), ("C0", 0))}, "end": "VVV", "quick": True,
+    "halves": "A", "sign": "A", "cyc": 1.1, "pe": 0.55, "hop": 200.0, "sweeps": 10, "issue": 350.0, "lat": 1500.0, "col": 1.25,
+}
 
 
 def _sb(shape, dt):
     return ("sbuf", [128] + shape, dt)
 
 
-BF, F32, I32 = "bfloat16", "float32", "int32"
+BF, F32, I32, U16 = "bfloat16", "float32", "int32", "uint16"
 SCRATCH = {
     "win": _sb([12 * P], BF), "rs": _sb([F * P], BF), "snd": _sb([F * P], BF),
-    "win2": _sb([11 * P], BF), "rs2": _sb([(F - 1) * P], BF), "OF2": _sb([F - 1, 64], "uint16"),
-    "gp": _sb([P], BF), "gq": _sb([P], BF), "yy": _sb([P], F32), "tb": _sb([(F - 1) * P], BF),
-    "ctl": _sb([32], I32), "ctb": _sb([32], BF),
-    "lia": _sb([F, 32], I32), "lib": _sb([F, 32], I32), "lvy": _sb([F, 64], I32), "lvx": _sb([F, 64], I32),
-    "cA": _sb([128], F32), "cB": _sb([128], F32), "pi": _sb([2], I32), "pj": _sb([4], I32), "col": _sb([12], F32),
-    "W2": _sb([256], BF), "N2": _sb([256], BF), "I16": _sb([128], BF), "I512": _sb([128], BF),
+    "win2": _sb([11 * P], BF), "rs2": _sb([(F - 1) * P], BF), "OF2": _sb([F - 1, 64], U16),
+    "gp": _sb([2, P], BF), "gq": _sb([2, P], BF), "tb": _sb([(F - 1) * P], BF),
+    "ctl": _sb([2, 16], I32), "ctb": _sb([3, 32], BF), "Tb": _sb([128], BF), "Coef": _sb([50], BF),
+    "lia": _sb([F, 32], I32), "lib": _sb([F, 32], I32), "lvy": _sb([F, 2, 32], I32), "lvx": _sb([F, 2, 32], I32),
+    "cA": _sb([128], F32), "cB": _sb([8, 16], F32), "fr": _sb([25], F32), "LK": _sb([25], F32), "c21": _sb([25], BF),
+    "pi": _sb([2], I32), "pj": _sb([4], I32), "col": _sb([12], F32), "ce": _sb([4, F], BF), "rw": _sb([32], F32),
+    "W2": _sb([256], BF), "N2": _sb([256], BF), "I16": _sb([128], BF), "N16": _sb([128], BF), "I32i": _sb([128], BF), "I512i": _sb([128], BF),
     "OO": _sb([128], BF), "NO": _sb([128], BF), "NU": _sb([128], BF), "NL": _sb([128], BF),
     "tU": _sb([128], BF), "tL": _sb([128], BF), "E8": _sb([128], BF),
-    "qm": _sb([CW], BF), "c128": _sb([CW], BF), "cM": _sb([CW], BF), "K1": _sb([128], BF), "K2": _sb([96], F32),
-    "cc": _sb([32], F32), "CL": _sb([16], F32), "one5": _sb([8], F32), "ph5": _sb([8], F32),
-    "a1": _sb([8], F32), "a2": _sb([8], F32), "z0": _sb([2], F32), "tx": _sb([8], F32),
-    "TG": _sb([32], F32), "OH": _sb([32], BF), "NE": _sb([32], BF),
-    "born": _sb([8], BF), "c23": _sb([8], BF), "R": _sb([8], BF), "f1": _sb([8], F32),
-    "SS": _sb([F, 2], F32), "SZ": _sb([F, 2], F32), "ZU": _sb([F, 2], BF), "LP": _sb([8], BF), "RB": _sb([8], F32),
-    "PH": _sb([8], F32), "pe": _sb([2], F32),
-    "nm2": _sb([2, F], F32), "k0": _sb([8], F32),
-    "XE": _sb([16], F32), "held": _sb([F], BF), "G": _sb([4, F], BF),
-    "Gp": _sb([4, F], F32), "Ge": _sb([4, F], F32), "wts": _sb([4, F], BF), "H": _sb([4, 2, F], BF),
-    "XE0": _sb([2], F32), "held0": _sb([1], BF), "G0": _sb([4, 1], BF),
-    "Gp0": _sb([4, 1], F32), "wts0": _sb([4, 1], BF), "H0": _sb([4, 1, 1], BF),
-    "s1": _sb([8], I32), "s2": _sb([8], I32), "s3": _sb([8], F32), "ML": _sb([F, 16], "uint16"),
-    "ND": _sb([F, 2, 32], BF), "idx": _sb([F, 2, 32], BF), "ibn": _sb([F, 32], BF),
-    "mx": _sb([F, 32], BF), "e1": _sb([F, 32], BF), "w": _sb([F, 2, 32], BF),
-    "nv": _sb([F, 64], BF), "thr": _sb([F, 64], BF), "D4": _sb([F, 128], BF),
-    "VN": _sb([F, 128], BF), "Y": _sb([F, 96], I32), "B": _sb([F, 96], I32), "PB": _sb([F, 64], BF),
-    "MS": _sb([F * MW], I32), "ok": _sb([F, 64], BF), "df": _sb([F, 64], BF), "h": _sb([F, 128], BF),
-    "M3": _sb([F, 96], BF), "RC": _sb([F, 128], BF), "OFF": _sb([F, 64], "uint16"),
+    "LP0": _sb([128], BF), "LPh": _sb([128], BF), "LE": _sb([128], BF),
+    "qm": _sb([CW], BF), "cK": _sb([32 + CW], BF), "cM": _sb([CW], BF), "cM2": _sb([32], BF), "K1": _sb([128], BF),
+    "cc": _sb([32], F32), "CL": _sb([8], F32), "Q": _sb([27, 6], BF), "R": _sb([8], BF), "SS": _sb([5, F], F32),
+    "ZU": _sb([7, 6], BF), "LN": _sb([8], BF), "sc": _sb([4], F32), "jk": _sb([24], BF),
+    "wts": _sb([4, F], BF), "wts0": _sb([4], BF), "eq": _sb([3, F], BF), "ML": _sb([F, 8], U16),
+    "IX": _sb([F, 2, 32], BF), "mx": _sb([F, 32], BF), "e1": _sb([F, 32], BF), "w": _sb([F, 2, 32], BF), "vw": _sb([F, 2, 32], BF),
+    "D3": _sb([F, MW], BF), "VN": _sb([F, 4, 32], BF), "Yp": _sb([F, 64], I32), "Bp": _sb([F, 64], I32),
+    "Ye": _sb([F - 1, 32], I32), "Be": _sb([F - 1, 32], I32), "Pb": _sb([F, 3, 32], BF), "Eb": _sb([F - 1, 32], BF),
+    "MS": _sb([8 * MW], BF), "h": _sb([F, MW], BF), "t": _sb([F, 32], BF), "RC": _sb([F, 128], BF), "OFF": _sb([F, 64], U16),
 }
 for _n in ("X0", "X1", "X2", "C0", "C1", "C2", "P1", "AD"):
     SCRATCH[_n] = ("psum", [128, 512], F32)
-SEMAPHORES = (["nV", "nA", "nP", "nG", "dctl", "dab", "dv", "dp0", "dp1", "dr0", "dr1", "dr2", "dy", "ls0", "ls1", "ls2", "ls3", "ls4", "ls", "pp", "rr1", "rr2", "rr3"]
-              + ["arr%d" % f for f in range(F)] + ["brr%d" % f for f in range(F - 1)] + ["of%d" % f for f in range(F - 1)])
-
-CYC = 1.25
-HOP = 200.0
-LINK = 1.0
-SWEEPS = 60
-F0 = 2
-YCA = ()
+SEMAPHORES = (["nV", "nA", "nP", "nG", "dctl", "da", "db", "dvy", "dvx", "dp0", "dp1", "dy", "ls", "pp", "dk", "ds1", "dbl"]
+              + [s + str(f) for s in ("arr", "brr", "of", "rr", "dr", "ls") for f in range(F)])
 PLAN = {}
 
 
@@ -71,11 +62,13 @@ def joint(T, topo):
         base, ops = (0, len(parts[0])), []
         for i, p in enumerate(parts):
             for o in p:
-                u = dict(o, q=o["q"], lane=o.get("lane", o["q"]) + str(i), deps={d + base[i] for d in o["deps"]}, soft={d + base[i] for d in o["soft"]})
+                u = dict(o, lane=o.get("lane", o["q"]) + str(i), deps={d + base[i] for d in o["deps"]}, soft={d + base[i] for d in o["soft"]})
                 if "order" in o:
                     u["order"] = o["order"] + base[i]
-                if "link" in o:
-                    u["soft"].add(names[1 - i][o["link"]] + base[1 - i])
+                u["soft"].update(p[d]["move"] + base[i] for d in o["deps"] if "move" in p[d])
+                for same, name in o.get("link", ()):
+                    j = i if same else 1 - i
+                    u["soft"].add(names[j][name] + base[j])
                 ops.append(u)
         order, start = plan(ops)
         PLAN[False] = [k for k in order if k < base[1]]
@@ -87,9 +80,10 @@ def joint(T, topo):
 def build(T, topo, core):
     rank = T.rank_of(core)
     n = len(T.cores)
-    nxt, prv = T.cores[(rank + 1) % n], T.cores[(rank - 1) % n]
-    nx2 = T.cores[(rank + 2) % n]
+    nxt, prv, nx2 = T.cores[(rank + 1) % n], T.cores[(rank - 1) % n], T.cores[(rank + 2) % n]
     second = prv in topo.cores_of(core)
+    mine, theirs = CFG["remake"][second], CFG["remake"][not second]
+    cyc, parts = CFG["cyc"], CFG["parts"]
     ops, wr, rd, bk, lastdma = [], {}, {}, {}, {}
 
     def op(q, fn, r=(), w=(), banks=(), dur=70.0, lat=0.0, sem=None, inc=0, soft=()):
@@ -123,403 +117,501 @@ def build(T, topo, core):
             fn = lambda e: e.tensor_scalar(out, in0, s1, None, o0)
         else:
             fn = lambda e: e.tensor_scalar(out, in0, s1, s2, o0, o1)
-        return op("V", fn, r, w, banks, max(64, el(out) * k) * CYC + x)
+        return op("V", fn, r, w, banks, max(64, el(out) * k) * cyc + x)
 
-    def tt(out, a, b, o, r=(), w=(), banks=(), k=2.0):
-        return op("V", lambda e: e.tensor_tensor(out, a, b, o), r, w, banks, max(64, el(out) * k) * CYC)
+    def tt(out, a, b, o, r=(), w=(), banks=(), k=2.0, x=0.0):
+        return op("V", lambda e: e.tensor_tensor(out, a, b, o), r, w, banks, max(64, el(out) * (1.0 if banks else k)) * cyc + x)
 
     def cp(out, a, r=(), w=(), banks=()):
-        return op("V", lambda e: e.tensor_copy(out, a), r, w, banks, max(64, el(out)) * CYC)
+        return op("V", lambda e: e.tensor_copy(out, a), r, w, banks, max(64, el(out)) * cyc)
 
     def ms(out, v, w):
-        return op("V", lambda e: e.memset(out, v), (), w, (), max(64, el(out) / 2) * CYC)
+        return op("V", lambda e: e.memset(out, v), (), w, (), max(64, el(out) / 2) * cyc)
 
-    def mm(out, l, x, st, sp, r, w, bank):
-        return op("P", lambda e: e.matmul(out, l, x, st, sp), r, w, (bank,), max(64, el(out)) * 0.55)
+    def mm(out, l, x, r, w, bank, st=False, sp=False):
+        return op("P", lambda e: e.matmul(out, l, x, st, sp), r, w, (bank,), max(64, el(out)) * CFG["pe"])
 
-    def act(out, a, fu, r, w, banks=(), bias=0.0, scale=1.0, k=1.0, x=0.0):
-        return op("A", lambda e: e.activation(out, a, fu, bias, scale), r, w, banks, max(64, el(out) * k) * CYC + x)
+    def act(out, a, fu, r, w, banks=(), bias=0.0, scale=1.0, k=1.0, x=0.0, acc=None):
+        return op("A", lambda e: e.activation(out, a, fu, bias, scale, accum_out=acc), r, w, banks, max(64, el(out) * k) * cyc + x)
 
-    def dma(q, out, a, sem, r=(), w=(), nbytes=0):
-        k = op(q, lambda e: e.dma_start(out, a), r, w, (), 80.0, 1800.0 + nbytes / 200.0, sem, 16)
+    def dma(q, out, a, sem, r=(), w=(), wide=1):
+        k = op(q, lambda e: e.dma_start(out, a), r, w, (), 70.0, 0.0, sem, 16)
+        moves(k, (), 900.0, out.shape[0] / 16.0 * (22.0 + 2 * el(out) * wide / CFG["rate"]), 600.0)
         if q in lastdma:
             ops[k]["order"] = lastdma[q]
         lastdma[q] = k
         return k
 
-    def send(dst, out, a, sem, r, name, first=False, need=None):
+    def moves(k, name, before, dur, after):
+        j = op("X", None, (), name, (), dur, after, None, 0, (k,))
+        ops[j]["lane"], ops[j]["after"], ops[k]["move"] = "D", before, j
+
+    sent, early = [], [True]
+
+    def send(dst, out, a, sem, r, name, ls="ls", after=None):
         rid, pid = topo.addr(dst, core)
-        emask, ls = topo.mask(core, dst), "ls0" if first else need or "ls"
+        emask, ne = topo.mask(core, dst), len(topo.engines(core, dst))
         fn = lambda e: e.remote_dma(out, a, T.sem[sem], T.sem[ls], pid, rid, emask)
-        k = op("G", fn, r, (name,), (), 400.0, 3000.0 if first else 1500.0, ls, len(topo.engines(core, dst)))
-        return k
+        move = (350.0 + el(out) * CFG["col"]) * 8 / ne
+        k = op("G", fn, r, (name,), (), CFG["issue"] + (0.0 if sent else 1200.0 + 40.0 * ne), 0.0, ls, ne)
+        moves(k, ("T" + name,), CFG["lat"] / 2, move, CFG["lat"] / 2)
+        if sent:
+            ops[k]["order"], ops[k + 1]["order"] = sent[-1], sent[-1] + 1
+        sent.append(k)
+        ops[k]["mark"] = CFG["marks"].get(name[1], 0.0)
+        return name
 
-    def arrive(src, sem, key, like=None, cols=0, rel=None):
-        k = op("X", None, (), (key,), (), LINK * (300.0 + cols * 2.5) if cols else 0.0, 0.0, sem, len(topo.engines(src, core)), () if like is None else (like,))
-        if rel:
-            ops[k]["link"], ops[k]["lane"], ops[k]["dur"] = rel[0], "Y" if rel[1] else key, 150.0 + rel[1] * 1.3 if rel[1] else 0.0
+    def arrive(src, sem, key, names):
+        k = op("X", None, (), (key,), (), 0.0, 0.0, sem, len(names) * len(topo.engines(src, core)))
+        ops[k]["link"], ops[k]["lane"] = [(src == nx2, "T" + s) for s in names], key
 
-    def view_out(f, a, c0, c1, r, first=False):
-        s = (V0 - f) * P
-        if F0 <= f < F - 1:
-            k = send(nx2, T["win2"][:, s + c0:s + c1], a, "brr%d" % f, r, "sentB%d_%d" % (f, c0), first)
-            arrive(nx2, "brr%d" % f, "W%d_%d" % (f, c0), k, c1 - c0)
-            views["W"].append("W%d_%d" % (f, c0))
-        else:
-            k = None
-        j = send(nxt, T["win"][:, s + c0:s + c1], a, "arr%d" % f, r, "sentA%d_%d" % (f, c0), first and F0 > 0, "ls%d" % f if f else None)
-        if k and f < F - 2:
-            ops[j]["order"] = k
-        elif k:
-            ops[k]["order"] = j
-        arrive(nx2, None, "A%d_%d" % (f, c0), j, c1 - c0)
+    win, win2 = T["win"], T["win2"]
+    slot = lambda s, ww=win: ww[:, s * P:(s + 1) * P]
+    res = lambda f: T["rs"][:, f * P:(f + 1) * P]
 
-    win = T["win"]
-    slot = lambda s: win[:, s * P:(s + 1) * P]
-    dma("S", slot(SB + 2), T.pic0[:, P:2 * P], "dp1", w=("pic1",), nbytes=131072)
-    dma("A", T["ctl"][0:8, 0:5], T.gaps[:], "dctl", w=("ctl0",))
-    dma("S", T["ctl"][0:8, 5:10], T.cmd[:], "dctl", w=("ctl1",))
-    dma("A", T["ctl"][0:8, 10:25], T.rel[:], "dctl", w=("ctl2",))
-    dma("S", T["lia"][:], T.ia[:], "dab", w=("ia",), nbytes=200000)
-    dma("A", T["lib"][:], T.ib[:], "dab", w=("ib",), nbytes=200000)
-    dma("S", T["lvy"][:], T.vy[:], "dv", w=("vy",), nbytes=500000)
-    dma("A", T["lvx"][:], T.vx[:], "dv", w=("vx",), nbytes=500000)
-    dma("S", slot(SB + 1), T.pic0[:, 0:P], "dp0", w=("pic0",), nbytes=700000)
-    dma("A", T["rs"][:, 0:P], T.res[:, 0:P], "dr0", w=("rs0",), nbytes=700000)
-    views = {"V": ["V0"], "W": []}
-    win2, rs2 = T["win2"], T["rs2"]
-    if second:
-        view_out(0, slot(SB + 2), 0, P, ("pic1",), True)
-        arrive(prv, "arr0", "V0", rel=("sent0", P))
-        arrive(prv, "pp", "pics2", rel=("sentp", P))
-        act(win2[:, (SB + 2) * P:(SB + 3) * P], slot(V0), ACT.Copy, ("V0",), ("pics3",))
-        for i in range(F0, F - 1):
-            arrive(prv, "rr%d" % i, "rs2_%d" % i, rel=("sentr%d" % i, P))
-        for f in range(F0, F - 1):
-            arrive(prv, "of%d" % f, "OF2_%d" % f, rel=("sento%d" % f, 64))
-        for f in range(1, F0 + 1):
-            arrive(prv, "arr%d" % f, "V%d" % f, rel=("sentv%d" % f, P))
-        s0key = "sentA0_0" if F0 else "sentB0_0"
-    else:
-        send(nxt, slot(V0), slot(SB + 2), "arr0", ("pic1",), "sent0", True)
-        for f in range(F):
-            for i, j in SENDS[f]:
-                arrive(prv, "arr%d" % f, "V%d" % f if i == 0 else "V%d_%d" % (f, i), rel=("A%d_%d" % (f, CH[i][0]), 0))
-        s0key = "sent0"
-    dma("S", T["rs"][:, P:3 * P], T.res[:, P:3 * P], "dr1", r=(s0key,), w=("rs1", "rs2"), nbytes=262144)
+    def res2(f, rc):
+        return slot(V0 - f + 1, win2) if f and f - 1 not in rc else T["rs2"][:, f * P:(f + 1) * P]
 
-    def after_send(f, key, k):
-        if f == 0:
-            dma("S", T["rs"][:, 3 * P:F * P], T.res[:, 3 * P:F * P], "dr2", r=(key,), w=("rs3", "rs4"), nbytes=262144)
-        if second:
-            return
-        more = [send(nxt, rs2[:, i * P:(i + 1) * P], T["rs"][:, i * P:(i + 1) * P], "rr%d" % i, ("rs%d" % i,), "sentr%d" % i)
-                for i in range(F0, F - 1) if (f == 0 and i < 3) or (f == F0 - 1 and i == 3)]
-        if f == 0:
-            more.append(send(nxt, win2[:, (SB + 1) * P:(SB + 2) * P], slot(SB + 1), "pp", ("pic0",), "sentp"))
-        for j in more:
-            ops[j]["order"] = k
+    def view_out(f, a, r):
+        s, last = (V0 - f) * P, None
+        if f - 1 not in theirs:
+            for i, j in parts if f else whole:
+                c0, c1 = CH[i][0], CH[j - 1][1]
+                last = send(nxt, win[:, s + c0:s + c1], a[:, c0:c1], "arr%d" % f, r[i:j], "sA%d_%d" % (f, i), "ls%d" % f, last)
+        if f in mine:
+            last = send(nx2, slot(V0 - f, win2), a, "brr%d" % f, r, "sB%d" % f, "ls%d" % f, last)
+        return last
 
-    cA, cB, col, cc = T["cA"], T["cB"], T["col"], T["cc"]
+    ctl, whole = T["ctl"], ((0, len(CH)),)
+    dma("S", slot(SB + 2), T.pic0[:, P:2 * P], "dp1", w=("pic1",))
+    dma("A", ctl[0:8, 0, 0:5], T.gaps[:], "dctl", w=("ctl0",))
+    dma("S", ctl[0:8, 0, 5:10], T.cmd[:], "dctl", w=("ctl1",))
+    dma("A", ctl[0:8, 0, 10:15], T.cmd[:], "dctl", w=("ctl2",))
+    dma("S", ctl[0:8, 1, 0:15], T.rel[:], "dctl", w=("ctl3",))
+    dma("A", T["lia"][:], T.ia[:], "da", w=("ia",), wide=2)
+    dma("S", T["lib"][:], T.ib[:], "db", w=("ib",), wide=2)
+    dma("A", T["lvy"][:], T.vy[:], "dvy", w=("vy",), wide=2)
+    dma("S", T["lvx"][:], T.vx[:], "dvx", w=("vx",), wide=2)
+    dma("A", slot(SB + 1), T.pic0[:, 0:P], "dp0", w=("pic0",))
+    dma("S", res(0), T.res[:, 0:P], "dr0", w=("rs0",))
+    early[0] = False
+    gone = view_out(0, slot(SB + 2), ("pic1",))
+    for f in range(1, F):
+        dma("S", res(f), T.res[:, f * P:(f + 1) * P], "dr%d" % f, r=(gone,) if f >= CFG["late"] else (), w=("rs%d" % f,))
+    for f in range(F):
+        if f - 1 not in mine:
+            arrive(prv, "arr%d" % f, "V%d" % f, ["sA%d_%d" % (f, i) for i, j in (parts if f else whole)])
+        if f in mine:
+            arrive(nx2, "brr%d" % f, "W%d" % f, ["sB%d" % f])
+            arrive(prv, "rr%d" % f, "rs2_%d" % f, ["sr%d" % f])
+            arrive(prv, "of%d" % f, "OF2_%d" % f, ["so%d" % f])
+    if mine:
+        arrive(prv, "pp", "pics2", ["sp"])
+    if theirs:
+        send(nxt, slot(SB + 1, win2), slot(SB + 1), "pp", ("pic0",), "sp")
+    given = []
+
+    def hand(kind, upto):
+        for f in theirs:
+            if f <= upto and (kind, f) not in given:
+                given.append((kind, f))
+                if kind == "r":
+                    send(nxt, res2(f, theirs), res(f), "rr%d" % f, ("rs%d" % f,), "sr%d" % f)
+                else:
+                    send(nxt, T["OF2"][:, f, :], T["OFF"][:, f, :], "of%d" % f, ("OFF%d" % f,), "so%d" % f)
+
+    hand("r", 1)
+
+    cA, cB, col, cc, fr, Coef, Q, ZU = [T[s] for s in ("cA", "cB", "col", "cc", "fr", "Coef", "Q", "ZU")]
+    small = {"allow_small_or_imprecise_dtypes": True}
     op("G", lambda e: e.iota(T["pi"][:, 0:1], [[1, 1]], 0, 1), w=("pi",), dur=200.0)
-    op("G", lambda e: e.iota(cB[:], [[1, 8], [0, 16]], 0, 0, allow_small_or_imprecise_dtypes=True), w=("cB",), dur=400.0)
-    op("G", lambda e: e.iota(cA[:], [[1, 128]], 0, -1, allow_small_or_imprecise_dtypes=True), w=("cA",), dur=400.0)
-    pc_, gc_, lc_, l1_, lq_, lm_ = [col[:, i:i + 1] for i in range(6)]
+    op("G", lambda e: e.iota(cB[:], [[1, 8], [0, 16]], 0, 0, **small), w=("cB",), dur=400.0)
+    op("G", lambda e: e.iota(cA[:], [[1, 128]], 0, -1, **small), w=("cA",), dur=400.0)
+    op("G", lambda e: e.iota(fr[:], [[0, 5], [-1, 5]], -2, 0, **small), w=("fr",), dur=200.0)
+    op("G", lambda e: e.iota(T["rw"][:, 0:15], [[1, 3], [3, 5]], 32, -1, **small), w=("rw0",), dur=170.0)
+    op("G", lambda e: e.iota(T["rw"][:, 16:26], [[-5, 2], [1, 5]], 74, -1, **small), w=("rw1",), dur=160.0)
+    op("G", lambda e: e.iota(T["ce"][:], [[-32, 2], [0, 10]], -16, 0, **small), w=("ce",), dur=180.0)
+    pc_, gc_, lc_, lq_, hu_, hl_, hn_, lh_ = [col[:, i:i + 1] for i in range(8)]
     ts(T["pj"][:, 0:1], T["pi"][:, 0:1], 4, None, ALU.arith_shift_right, r=("pi",), w=("pj0",))
     ts(T["pj"][:, 1:2], T["pi"][:, 0:1], 15, None, ALU.bitwise_and, r=("pi",), w=("pj1",))
     cp(pc_, T["pi"][:, 0:1], r=("pi",), w=("p",))
     cp(col[:, 1:3], T["pj"][:, 0:2], r=("pj0", "pj1"), w=("g", "l"))
-    act(l1_, lc_, ACT.Identity, ("l",), ("l1",), bias=1.0)
     act(lq_, lc_, ACT.Identity, ("l",), ("lq",), bias=-0.25)
-    act(lm_, lc_, ACT.Identity, ("l",), ("lm",), bias=-2.0 * MW)
-    hu_, hl_, hn_ = [col[:, i:i + 1] for i in (6, 7, 8)]
+    act(lh_, lc_, ACT.Identity, ("l",), ("lh",), bias=0.5, scale=0.5)
     ts(hu_, lc_, 0.5, None, ALU.mult, r=("l",), w=("hu",))
     ts(hl_, lc_, -0.5, 7.5, ALU.mult, ALU.add, r=("l",), w=("hl",))
-    ts(hn_, lc_, 0.5, -7.5, ALU.mult, ALU.add, r=("l",), w=("hn",))
-    ts(T["E8"][0:8, :], cB[0:8, :], col[0:8, 0:1], None, ALU.is_equal, r=("cB", "p"), w=("E8",))
-    ts(T["OO"][:], cB[:], gc_, None, ALU.is_equal, r=("cB", "g"), w=("OO",))
-    ts(T["NO"][:], cB[:], gc_, -1.0, ALU.is_equal, ALU.mult, r=("cB", "g"), w=("NO",))
+    act(hn_, lc_, ACT.Identity, ("l",), ("hn",), bias=-7.5, scale=0.5)
+    OO, NO, NU, NL, I16 = [T[s][:] for s in ("OO", "NO", "NU", "NL", "I16")]
+    ts(T["E8"][0:8, :], cB[0:8], col[0:8, 0:1], None, ALU.is_equal, r=("cB", "p"), w=("E8",))
+    ts(OO, cB[:], gc_, None, ALU.is_equal, r=("cB", "g"), w=("OO",))
+    ts(NO, OO, -1.0, None, ALU.mult, r=("OO",), w=("NO",), k=0.5)
     act(T["tU"][:], cA[:], ACT.Abs, ("cA", "hu"), ("tU",), bias=hu_)
     act(T["tL"][:], cA[:], ACT.Abs, ("cA", "hn"), ("tL",), bias=hn_)
-    ts(T["NU"][:], T["tU"][:], hu_, -1.0, ALU.is_le, ALU.mult, r=("hu", "tU"), w=("NU",), k=0.5)
-    ts(T["NL"][:], T["tL"][:], hl_, -1.0, ALU.is_le, ALU.mult, r=("hl", "tL"), w=("NL",), k=0.5)
-    ts(T["W2"][:, 0:128], cA[:], 0.0, None, ALU.is_equal, r=("cA",), w=("I",))
-    Id = T["W2"][:, 0:128]
-    act(T["W2"][:, 128:256], Id, ACT.Copy, ("I",), ("I2",))
-    act(T["N2"][:], T["W2"][:], ACT.Copy, ("I", "I2"), ("N2",), scale=-1.0)
-    act(T["I16"][:], Id, ACT.Copy, ("I",), ("I16",), scale=16.0)
-    act(T["I512"][:], Id, ACT.Copy, ("I",), ("I512",), scale=512.0)
+    ts(NU, T["tU"][:], hu_, -1.0, ALU.is_le, ALU.mult, r=("hu", "tU"), w=("NU",), k=0.5)
+    ts(NL, T["tL"][:], hl_, -1.0, ALU.is_le, ALU.mult, r=("hl", "tL"), w=("NL",), k=0.5)
+    Id, Ng = T["W2"][:, 0:128], T["N2"][:, 0:128]
+    ts(Id, cA[:], 0.0, None, ALU.is_equal, r=("cA",), w=("I",))
+    ts(T["W2"][:, 128:256], Id, 1.0, None, ALU.mult, r=("I",), w=("I2",), k=0.5)
+    ts(T["N2"][:], T["W2"][:], -1.0, None, ALU.mult, r=("I", "I2"), w=("N",), k=0.5)
+    ts(I16, Id, 16.0, None, ALU.mult, r=("I",), w=("I16",), k=0.5)
+    N16 = T["N16"][:]
+    ts(N16, Id, -16.0, None, ALU.mult, r=("I",), w=("N16",), k=0.5)
+    act(T["I32i"][:], Id, ACT.Copy, ("I",), ("I32i",), scale=1.0 / 32)
+    act(T["I512i"][:], Id, ACT.Copy, ("I",), ("I512i",), scale=1.0 / 512)
     act(cc[:], cA[:, 0:32], ACT.Identity, ("cA", "p"), ("cc",), bias=pc_)
     for i in range(2):
         act(T["K1"][:, 32 * i:32 * i + 32], cc[:], ACT.Identity, ("cc",), ("K1%d" % i,), bias=-0.25)
     act(T["K1"][:, 64:128], cA[:, 0:64], ACT.Identity, ("cA", "lq"), ("K12",), bias=lq_, scale=0.0)
-    k1 = ("K10", "K11", "K12")
-    act(T["K2"][:], T["K1"][:, 0:96], ACT.Identity, k1, ("K2",), bias=128.25)
-    for c0, s0, m in ((0, 0, 2), (2, 0, 2), (4, 0, 6), (10, 4, 2), (12, 8, 2), (14, 8, 2)):
-        act(T["CL"][:, c0:c0 + m], cc[:, s0:s0 + m], ACT.Identity, ("cc", "lm"), ("CL%d" % c0,), bias=lm_, scale=16.0)
-    cl = ("CL0", "CL2", "CL4", "CL10", "CL12", "CL14")
-    ms(slot(SB), 128.0, ("blank",))
-    if second:
-        ms(win2[:, (SB - F0) * P:(SB + 1) * P], 128.0, ("blank2",))
+    act(T["CL"][:, 0:6], cc[:, 0:6], ACT.Identity, ("cc", "l"), ("CL",), bias=lc_, scale=16.0)
+    act(T["LK"][:, 0:1], lc_, ACT.Identity, ("l",), ("LK0",), bias=97.0)
+    act(T["LK"][:, 1:25], fr[:, 1:25], ACT.Identity, ("fr", "l"), ("LK1",), bias=lc_)
+    act(T["c21"][:], fr[:], ACT.Identity, ("fr",), ("c21",), bias=7.0)
+    ts(Coef[:, 0:25], fr[:], pc_, -2.0, ALU.add, ALU.is_le, r=("fr", "p"), w=("Cf",))
+    act(Coef[:, 25:50], Coef[:, 0:25], ACT.Copy, ("Cf",), ("Cs",), scale=-1.0)
+    ts(Coef[32:64, 5:20], T["rw"][32:64, 0:15], 0.0, -1.0, ALU.is_equal, ALU.mult, r=("rw0", "Cs"), w=("Cr0",))
+    ts(Coef[32:64, 0:5], T["rw"][32:64, 0:5], 0.0, -1.0, ALU.is_equal, ALU.mult, r=("rw0", "Cs"), w=("Cr1",))
+    ts(Coef[64:96, 0:10], T["rw"][64:96, 16:26], 0.0, -99.0, ALU.is_equal, ALU.mult, r=("rw1", "Cs"), w=("Ci",))
+    ms(Coef[64:65, 0:1], 99.0, ("Ci",))
+    coef = ("Cf", "Cs", "Cr0", "Cr1", "Ci")
     ms(T["qm"][:], -0.25, ("qm",))
-    ms(T["c128"][:], 128.0, ("c128",))
+    ms(T["cK"][:, 0:32], 16.0, ("c16",))
+    ms(T["cK"][:, 32:32 + CW], 128.0, ("c128",))
     ms(T["cM"][:], MAGIC, ("cM",))
-    ms(T["one5"][:], 1.0, ("one5",))
-    act(T["ph5"][:, 0:F], cc[:, 0:F], ACT.Identity, ("cc",), ("ph5",), bias=3.0)
-    ts(T["PH"][:, F - 1:F], lc_, 2.0, l1_, ALU.is_lt, ALU.mult, r=("l", "l1"), w=("PH4",))
+    ms(T["cM2"][:], 16.0 * MAGIC, ("cM2",))
+    ms(T["ctb"][0:8], 0.0, ("ctb",))
     ms(T["R"][:, 0:1], 1.0, ("R0",))
-    ms(T["ZU"][:, 0, 0:1], 1.0, ("Z0",))
-    ms(T["LP"][:, 0:1], 0.0, ("LP0",))
-    ms(T["XE"][:, 15:16], -1.0, ("XEc",))
-    ms(T["MS"][:, 0:MW], 0, ("MS0",))
-    ms(T["M3"][:, :, 64:96], 0.0, ("M3z",))
-    act(T["wts0"][:, 3, :], T["one5"][:, 0:1], ACT.Exp, ("one5",), ("wts30",), scale=0.0, x=1400.0)
-    ms(T["wts"][:, 3, :], 1.0, ("wts3",))
+    ms(ZU[:, 1, 0:1], 0.0, ("LP0",))
+    ms(Q[:, 0, 5:6], -1.0, ("bc",))
+    ms(slot(SB), 128.0, ("blank",))
+    ms(T["MS"][:, 0:3 * MW], 0.0, ("MS0",))
+    ms(T["Pb"][:, :, 1, :], 0.0, ("Pz",))
+    ts(Q[:, 8, 5:6], lc_, 2.0, lh_, ALU.is_lt, ALU.mult, r=("l", "lh"), w=("K",))
+    ts(T["LP0"][:], OO, Q[:, 8, 5:6], 2.0, ALU.mult, ALU.mult, r=("OO", "K"), w=("LS0",), k=0.5)
+    k = act(Q[:, 9, 0:5], T["cK"][:, 0:5], ACT.Exp, ("c16",), ("one",), scale=0.0, x=1400.0)
+    ops[k]["order"] = lastdma["A"]
+    if mine:
+        if CFG["copies"][0] == "V":
+            ms(slot(SB, win2), 128.0, ("blank2",))
+        else:
+            dma("S", slot(SB, win2), slot(SB), "dk", r=("blank",), w=("blank2",))
+        if CFG["copies"][1] == "A":
+            act(slot(SB + 2, win2), slot(V0), ACT.Copy, ("V0",), ("pics3",))
+        elif CFG["copies"][1] == "V":
+            ts(slot(SB + 2, win2), slot(V0), 1.0, None, ALU.mult, r=("V0",), w=("pics3",), k=0.5)
+        else:
+            dma("S", slot(SB + 2, win2), slot(V0), "ds1", r=("V0",), w=("pics3",))
+        spare = [j for j in range(max(mine)) if j not in mine and j + 1 not in mine]
+        for j in spare:
+            ms(slot(V0 - j, win2), 0.0, ("spare%d" % j,))
 
-    C0, C1, C2 = T["C0"], T["C1"], T["C2"]
-    TG, OH, NE, R, ZU, LP, SS, XE = T["TG"], T["OH"], T["NE"], T["R"], T["ZU"], T["LP"], T["SS"], T["XE"]
-    OO, NO, NU, NL = T["OO"][:], T["NO"][:], T["NU"][:], T["NL"][:]
-    cp(T["ctb"][0:8, 0:25], T["ctl"][0:8, 0:25], r=("ctl0", "ctl1", "ctl2"), w=("ctb",))
-    mm(C2[:, 0:25], T["E8"][0:8, :], T["ctb"][0:8, 0:25], True, True, ("E8", "ctb"), ("pc",), "C2")
-    Cc = TG[:, 20:25]
-    op("V", lambda e: e.tensor_tensor_scan(Cc, C2[:, 0:5], T["one5"][:, 0:5], 1.0, ALU.add, ALU.add), ("pc", "one5"), ("C",), ("C2",))
-    ts(T["a1"][:, 0:5], C2[:, 5:10], 1.0, 99.0, ALU.not_equal, ALU.mult, r=("pc",), w=("a1",), banks=("C2",))
-    ts(T["a2"][:, 0:5], C2[:, 5:10], 2.0, 99.0, ALU.not_equal, ALU.mult, r=("pc",), w=("a2",), banks=("C2",))
-    ts(T["z0"][:, 0:1], C2[:, 0:1], 0.0, 99.0, ALU.is_equal, ALU.mult, r=("pc",), w=("z0",), banks=("C2",))
-    tt(T["tx"][:, 0:5], Cc, C2[:, 10:25:3], ALU.subtract, r=("pc", "C"), w=("tx",), banks=("C2",))
-    tt(TG[:, 10:15], Cc, C2[:, 11:25:3], ALU.subtract, r=("pc", "C"), w=("tm0",), banks=("C2",))
-    tt(TG[:, 15:20], Cc, C2[:, 12:25:3], ALU.subtract, r=("pc", "C"), w=("tm1",), banks=("C2",))
-    tt(TG[:, 0:5], T["tx"][:, 0:5], T["a1"][:, 0:5], ALU.subtract, r=("tx", "a1"), w=("t1",))
-    tt(TG[:, 6:10], T["tx"][:, 1:5], T["a2"][:, 1:5], ALU.subtract, r=("tx", "a2"), w=("t2",))
-    ts(TG[:, 5:6], T["tx"][:, 0:1], T["a2"][:, 0:1], T["z0"][:, 0:1], ALU.subtract, ALU.subtract, r=("tx", "a2", "z0"), w=("t20",))
-    tg = ("t1", "t2", "t20", "tm0", "tm1", "C")
-    ts(NE[:, 0:20], TG[:, 0:20], lc_, None, ALU.not_equal, r=tg + ("l",), w=("NE",))
-    ts(OH[:, 0:25], TG[:, 0:25], lc_, None, ALU.is_equal, r=tg + ("l",), w=("OH",))
-    act(T["c23"][:, 0:5], Cc, ACT.Identity, ("C",), ("c23",), bias=23.0, scale=-1.0)
-    ts(T["born"][:, 0:5], Cc, lc_, None, ALU.is_gt, r=("C", "l"), w=("born",))
-    ts(XE[:, 10:15], Cc, lc_, None, ALU.is_le, r=("C", "l"), w=("nb",))
-    tt(T["nm2"][:, 0, :], NE[:, 10:15], NE[:, 15:20], ALU.mult, r=("NE",), w=("nm0",))
-    act(T["nm2"][:, 1, :], T["nm2"][:, 0, :], ACT.Copy, ("nm0",), ("nm1",))
-    tt(T["k0"][:, 0:5], OH[:, 10:15], NE[:, 15:20], ALU.mult, r=("OH", "NE"), w=("k0",))
+    X0, X1, X2, C0, C1, C2, P1, AD = [T[s] for s in ("X0", "X1", "X2", "C0", "C1", "C2", "P1", "AD")]
+    R, SS, sc, ctb = T["R"], T["SS"], T["sc"], T["ctb"]
+    ck = ("ctl0", "ctl1", "ctl2", "ctl3")
+    cp(ctb[0:8, 0:2, 0:15], ctl[0:8, :, 0:15], r=ck + ("ctb",), w=("ct0",))
+    tt(ctb[0:8, 2, 0:15], ctl[0:8, 0, 0:15], cB[0:8, 0:3, 0:5], ALU.not_equal, r=ck + ("ctb", "cB"), w=("ct1",))
+    mm(X0[0:96, 0:128], ctb[0:8], T["E8"][0:8, :], ("ct0", "ct1", "E8"), ("T1",), "X0", True, True)
+    act(T["Tb"][0:96, :], X0[0:96, 0:128], ACT.Copy, ("T1",), ("Tb",), ("X0",))
+    mm(X1[:, 0:25], T["Tb"][0:96, :], Coef[0:96, 0:25], ("Tb",) + coef, ("TG",), "X1", True, True)
+    mm(X2[:, 0:25], T["Tb"][0:96, :], Coef[0:96, 25:50], ("Tb",) + coef, ("S",), "X2", True)
+    mm(X2[:, 0:25], Id, T["c21"][:], ("I", "c21"), ("S",), "X2")
+    one = Q[:, 9, 0:5]
+    for j, m in ((2, I16), (0, N16), (4, N16), (0, N16), (4, N16)):
+        mm(X2[:, 5 * j:5 * j + 5], m, one, ("I16", "N16", "one"), ("S",), "X2")
+    lk = ("TG", "LK0", "LK1")
+    tt(Q[:, 1:5, 0:5], X1[:, 0:20], T["LK"][:, 0:20], ALU.not_equal, r=lk, w=("NE",), banks=("X1",))
+    tt(Q[:, 0, 0:5], X1[:, 20:25], T["LK"][:, 20:25], ALU.is_gt, r=lk, w=("born",), banks=("X1",))
+    tt(Q[:, 5:9, 0:5], X1[:, 5:25], T["LK"][:, 5:25], ALU.is_equal, r=lk, w=("OH",), banks=("X1",))
+    tt(Q[:, 17, 0:5], Q[:, 3, 0:5], Q[:, 4, 0:5], ALU.mult, r=("NE",), w=("nm",))
+    tt(Q[:, 13, 0:5], Q[:, 5, 0:5], Q[:, 17, 0:5], ALU.mult, r=("OH", "nm"), w=("um",))
+    op("V", lambda e: e.tensor_tensor_scan(R[:, 1:6], Q[:, 2, 0:5], Q[:, 1, 0:5], 1.0, ALU.mult, ALU.mult), ("NE",), ("R",))
+    ts(ZU[:, 2, 0:1], Q[:, 0, 0:1], Q[:, 1, 0:1], None, ALU.mult, r=("NE", "born"), w=("h0",))
+    ts(ZU[:, 5, 0:1], Q[:, 5, 0:1], Q[:, 3, 0:1], Q[:, 4, 0:1], ALU.mult, ALU.mult, r=("NE", "OH"), w=("u0",))
+    ts(ZU[:, 4, 0:1], Q[:, 2, 0:1], Q[:, 3, 0:1], Q[:, 4, 0:1], ALU.mult, ALU.mult, r=("NE",), w=("t0",))
+    ts(ZU[:, 6, 0:1], ZU[:, 4, 0:1], ZU[:, 2, 0:1], None, ALU.mult, r=("h0", "t0"), w=("g0",))
 
-    def lists(t, nf, X, codes, pa, ba, pp, bp):
-        G, held, wts, H = T["G" + t], T["held" + t], T["wts" + t], T["H" + t]
-        sl = ("sh" + t, "lg" + t)
-        tt(held[:], X[:, 0:nf], X[:, nf:2 * nf], ALU.add, r=sl, w=("held" + t,))
-        tt(G[:, 0:2, :], X[:, 0:2 * nf], T["nm2"][:, :, 0:nf], ALU.mult, r=sl + ("nm0", "nm1"), w=("G01" + t,))
-        tt(G[:, 2, :], held[:], T["k0"][:, 0:nf], ALU.mult, r=("held" + t, "k0"), w=("G2" + t,))
-        tt(G[:, 3, :], held[:], OH[:, 15:15 + nf], ALU.mult, r=("held" + t, "OH"), w=("G3" + t,))
-        a_, b_, c_ = [pa[:, 64 + i * nf:64 + (i + 1) * nf] for i in range(3)]
-        abc = ("abc" + t,)
-        mm(a_, OO, held[:], True, False, ("OO", "held" + t), abc, ba)
-        mm(a_, NO, G[:, 1, :], False, False, ("NO", "G01" + t), abc, ba)
-        mm(a_, NL, G[:, 0, :], False, True, ("NL",), abc, ba)
-        mm(b_, OO, held[:], True, False, (), abc, ba)
-        mm(b_, NU, G[:, 1, :], False, True, ("NU",), abc, ba)
-        mm(c_, OO, G[:, 3, :], True, True, ("G3" + t,), abc, ba)
-        act(wts[:, 0:3, :], pa[:, 64:64 + 3 * nf], ACT.Exp, abc + ("wts30",), ("wts" + t,), (ba,), scale=LN8)
-        hk = []
-        for i, (buf, code, key) in enumerate(codes):
-            ts(T[buf][:], G[:], code, None, ALU.mult, r=("G01" + t, "G2" + t, "G3" + t, key), w=(buf,))
-            tt(H[:, :, i, :], T[buf][:], wts[:], ALU.mult, r=(buf, "wts" + t, "wts3" + t), w=("H" + buf,))
-            hk.append("H" + buf)
-        for s in range(4):
-            mm(pp[:, 16:16 + nf * len(codes)], OO, H[:, s, :, :], s == 0, s == 3, tuple(hk), ("pack" + t,), bp)
+    def places(nf, held, g0, g1, wts, name):
+        e = [C1[:, 5 * i:5 * i + nf] for i in range(4)]
+        terms = [(2, Ng, Q[:, 9, 0:nf], ("N", "one")), (3, I16, Q[:, 9, 0:nf], "one"),
+                 (2, I16, Q[:, 6, 0:nf], "OH"), (2, I16, Q[:, 4, 0:nf], "NE"), (3, I16, Q[:, 7, 0:nf], "OH")]
+        for j in reversed(range(len(held))):
+            terms += [(i, m) + held[j] for i, m in ((0, OO), (1, OO), (2, OO), (2, I16), (3, I16))]
+            terms += [(i, m) + g1[j] for i, m in ((0, NO), (1, NU), (1, I16), (2, NO))]
+        terms += [(i, m) + g0 for i, m in ((0, NL), (0, I16), (2, NO))]
+        mm(C1[:, 0:20], Id, T["ce"][:], ("I", "ce", "OO", "NO", "NU", "NL", "I16"), ("ex",), "C1", True)
+        for j, (i, m, x, key) in enumerate(terms):
+            mm(e[i], m, x, key if isinstance(key, tuple) else (key,), ("ex",), "C1", False, j + 1 == len(terms))
+        act(wts, C1[:, 0:20] if nf > 1 else C1[:, 0:20:5], ACT.Exp, ("ex", "one"), (name,), ("C1",), scale=LN8)
 
-    ts(T["XE0"][:, 0:1], T["born"][:, 0:1], NE[:, 0:1], NE[:, 5:6], ALU.mult, ALU.mult, r=("born", "NE"), w=("sh0",))
-    ts(T["XE0"][:, 1:2], TG[:, 0:1], lc_, None, ALU.is_equal, r=("t1", "l"), w=("lg0",))
-    lists("0", 1, T["XE0"], (("Gp0", T["PH"][:, F - 1:F], "PH4"),), T["X1"], "X1", T["X2"], "X2")
+    places(1, [(ZU[:, 2, 0:1], "h0")], (ZU[:, 6, 0:1], "g0"), [(ZU[:, 5, 0:1], "u0")], T["wts0"][:], "wts0")
+    for s in range(4):
+        mm(AD[:, 64:65], T["LP0"][:], T["wts0"][:, s:s + 1], ("LS0", "wts0"), ("pack0",), "AD", s == 0, s == 3)
 
-    op("V", lambda e: e.tensor_tensor_scan(R[:, 1:6], NE[:, 0:5], NE[:, 5:10], 1.0, ALU.mult, ALU.mult), ("NE",), ("R",))
-    mm(C0[:, 1:2], OO, OH[:, 0:1], True, True, ("OO", "OH"), ("Lb1",), "C0")
-    mm(C2[:, 32:37], Id, T["c23"][:, 0:5], True, False, ("I", "c23"), ("S1",), "C2")
-    mm(C2[:, 32:37], NU, R[:, 0:5], False, True, ("NU", "R", "R0"), ("S1",), "C2")
-    tt(T["f1"][:, 0:5], OH[:, 0:5], R[:, 0:5], ALU.mult, r=("OH", "R", "R0"), w=("f1",))
-    cp(SS[:, :, 0], C2[:, 32:37], r=("S1",), w=("SS0",), banks=("C2",))
-    tt(SS[:, :, 1], C2[:, 32:37], T["f1"][:, 0:5], ALU.mult, r=("S1", "f1"), w=("SS1",), banks=("C2",))
-    act(ZU[:, 0, 1:2], OH[:, 0:1], ACT.Copy, ("OH",), ("U0",))
-    ts(LP[:, 1:2], OH[:, 0:1], NE[:, 6:7], None, ALU.mult, r=("OH", "NE"), w=("LP1",))
+    for j in (0, 4, 0, 4):
+        mm(X2[:, 5 * j:5 * j + 5], I16, Q[:, 0, 0:5], ("born",), ("S",), "X2")
+    for j in range(5):
+        mm(X2[:, 5 * j:5 * j + 5], NU, R[:, 0:5], ("NU", "R", "R0"), ("S",), "X2")
+    for j, i in ((0, 0), (1, 0), (3, 0), (4, 1)):
+        mm(X2[:, 5 * j:5 * j + 5], I16, R[:, i:i + 5], (), ("S",), "X2", False, j == 4)
+    tt(SS[:], X2[:, 0:25], Q[:, 1:18:4, 0:5], ALU.mult, r=("S", "NE", "OH", "one", "nm", "um"), w=("SS",), banks=("X2",))
+    act(ZU[:, 0, 0:6], Q[:, 0, 0:6], ACT.Identity, ("born", "bc"), ("nb",), bias=1.0, scale=-1.0, acc=sc[:, 1:2])
+    act(T["jk"][:, 0:6], Q[:, 8, 0:6], ACT.Identity, ("OH", "K"), ("isF",), acc=sc[:, 0:1])
+    ts(T["LPh"][:], OO, sc[:, 0:1], sc[:, 1:2], ALU.mult, ALU.mult, r=("OO", "nb", "isF"), w=("LS",), k=0.5)
+    mm(C0[:, 1:2], OO, Q[:, 5, 0:1], ("OO", "OH"), ("L1",), "C0", True, True)
+    ts(ZU[:, 1, 1:2], Q[:, 5, 0:1], Q[:, 1, 1:2], None, ALU.mult, r=("OH", "NE"), w=("LP1",))
     for f in range(1, F):
-        cb, nb = (C0, "C0") if f % 2 else (C1, "C1")
-        ts(ZU[:, f, :], (SS if f == 1 else T["SZ"])[:, f, :], cb[:, f:f + 1], None, ALU.is_gt,
-           r=("SS0", "SS1", "Lb%d" % f) + (("SZ%d" % f,) if f > 1 else ()), w=("Z%d" % f, "U%d" % f), banks=(nb,))
+        ts(ZU[:, 2:7, f], SS[:, :, f], C0[:, f:f + 1], None, ALU.is_gt, r=("SS", "L%d" % f), w=("Z%d" % f,), banks=("C0",))
         if f + 1 < F:
-            ts(T["SZ"][:, f + 1, :], SS[:, f + 1, :], ZU[:, f, 0:1], None, ALU.mult, r=("SS0", "SS1", "Z%d" % f), w=("SZ%d" % (f + 1),))
-            cb, nb = (C1, "C1") if f % 2 else (C0, "C0")
-            mm(cb[:, f + 1:f + 2], OO, LP[:, f:f + 1], True, False, ("LP%d" % f,), ("Lb%d" % (f + 1),), nb)
-            mm(cb[:, f + 1:f + 2], OO, ZU[:, f, 1:2], False, True, ("U%d" % f,), ("Lb%d" % (f + 1),), nb)
-            ts(LP[:, f + 1:f + 2], LP[:, f:f + 1], ZU[:, f, 1:2], NE[:, 6 + f:7 + f], ALU.add, ALU.mult,
-               r=("LP%d" % f, "U%d" % f, "NE"), w=("LP%d" % (f + 1),))
-    tt(T["RB"][:, 0:5], R[:, 1:6], T["born"][:, 0:5], ALU.mult, r=("R", "born"), w=("RB",))
-    tt(T["PH"][:, 0:4], OH[:, 20:24], T["ph5"][:, 0:4], ALU.mult, r=("OH", "ph5"), w=("PH",))
-    op("V", lambda e: e.tensor_reduce(T["pe"][:, 0:1], T["PH"][:, 0:5], AxisListType.X, ALU.add), ("PH", "PH4"), ("phys",))
-    allz = tuple("Z%d" % f for f in range(F))
-    allu = tuple("U%d" % f for f in range(F)) + tuple("LP%d" % f for f in range(F))
-    tt(XE[:, 0:5], ZU[:, :, 0], T["RB"][:, 0:5], ALU.mult, r=allz + ("RB",), w=("sh",))
-    tt(XE[:, 5:10], ZU[:, :, 1], LP[:, 0:5], ALU.add, r=allu, w=("lg",))
-    op("V", lambda e: e.tensor_reduce(T["pe"][:, 1:2], XE[:, 0:16], AxisListType.X, ALU.add), ("sh", "lg", "nb", "XEc"), ("E",))
-    lists("", F, XE, (("Gp", T["pe"][:, 0:1], "phys"), ("Ge", T["pe"][:, 1:2], "E")), C2, "C2", C1, "C1")
-    ts(T["s1"][:, 0:5], C1[:, 16:21], 0.125, -0.4375, ALU.mult, ALU.add, r=("pack",), w=("s1",), banks=("C1",))
-    ts(T["s2"][:, 0:5], T["s1"][:, 0:5], 7, None, ALU.bitwise_and, r=("s1",), w=("s2",))
-    ts(T["s3"][:, 0:5], T["s2"][:, 0:5], 2.0, float(MW), ALU.max, ALU.mult, r=("s2",), w=("s3",))
+            for j, (m, x, r) in enumerate(((I16, Q[:, 9, 0:1], "one"), (OO, ZU[:, 1, f:f + 1], "LP%d" % f),
+                                           (OO, ZU[:, 3, f:f + 1], "Z%d" % f), (N16, ZU[:, 4, f:f + 1], "N16"))):
+                mm(C0[:, f + 1:f + 2], m, x, (r,), ("L%d" % (f + 1),), "C0", j == 0, j == 3)
+            ts(ZU[:, 1, f + 1:f + 2], ZU[:, 1, f:f + 1], ZU[:, 3, f:f + 1], Q[:, 1, f + 1:f + 2], ALU.add, ALU.mult,
+               r=("LP%d" % f, "Z%d" % f, "NE"), w=("LP%d" % (f + 1),))
+    allz, alll = ("h0", "u0", "g0") + tuple("Z%d" % f for f in range(1, F)), tuple("LP%d" % f for f in range(F))
+    if CFG["quick"]:
+        tt(Q[:, 18, 4:5], Q[:, 1, 4:5], Q[:, 17, 4:5], ALU.mult, r=("NE", "nm"), w=("nn",))
+        tt(T["LN"][:, 0:4], ZU[:, 1, 0:4], Q[:, 17, 0:4], ALU.mult, r=alll[:4] + ("nm",), w=("LN0",))
+        ts(T["LN"][:, 4:5], ZU[:, 1, 3:4], ZU[:, 3, 3:4], Q[:, 18, 4:5], ALU.add, ALU.mult, r=("LP3", "Z3", "nn"), w=("LN1",))
+    else:
+        tt(T["LN"][:, 0:5], ZU[:, 1, 0:5], Q[:, 17, 0:5], ALU.mult, r=alll + ("nm",), w=("LN0", "LN1"))
+    act(T["jk"][:, 8:23], ZU[:, 0:3, 0:5], ACT.Identity, allz + alll + ("nb",), ("E",), acc=sc[:, 2:3])
+    ts(T["LE"][:], OO, sc[:, 2:3], None, ALU.mult, r=("OO", "E"), w=("LE",), k=0.5)
 
-    ND, idx, VN = T["ND"], T["idx"], T["VN"]
-    ab, vv = ("ia", "ib"), ("vy", "vx")
-    for f0, f1 in ((0, 1), (1, F)):
-        t, fs = "%d" % f0, slice(f0, f1)
-        ts(ND[:, fs, 0, :], T["lia"][:, fs], 7.0, None, ALU.is_lt, r=ab, w=("ND0" + t,))
-        act(ND[:, fs, 1, :], ND[:, fs, 0, :], ACT.Copy, ("ND0" + t,), ("ND1" + t,))
-        tt(T["ibn"][:, fs], T["lib"][:, fs], ND[:, fs, 0, :], ALU.mult, r=ab + ("ND0" + t,), w=("ibn" + t,))
-        tt(idx[:, fs, 0, :], T["lia"][:, fs], ND[:, fs, 0, :], ALU.mult, r=ab + ("ND0" + t,), w=("idx0" + t,))
-        act(T["mx"][:, fs], T["ibn"][:, fs], ACT.Abs, ("ibn" + t,), ("mx" + t,), bias=-1.0)
-        ts(T["e1"][:, fs], T["ibn"][:, fs], 2.0, None, ALU.is_ge, r=("ibn" + t,), w=("e1" + t,), k=0.5)
-        tt(idx[:, fs, 1, :], T["mx"][:, fs], T["e1"][:, fs], ALU.add, r=("mx" + t, "e1" + t), w=("idx1" + t,))
-        act(T["w"][:, fs], idx[:, fs], ACT.Exp, ("idx0" + t, "idx1" + t, "wts30"), ("w" + t,), scale=-LN8)
+    IX, VN, D3, vw, ND = T["IX"], T["VN"], T["D3"], T["vw"], C2[:, 256:416]
+    ts(ND, T["lia"][:], 7.0, None, ALU.is_lt, r=("ia",), w=("ND",), banks=("C2",))
+    tt(IX[:, :, 0, :], T["lia"][:], ND, ALU.mult, r=("ND",), w=("ix0",), banks=("C2",))
+    tt(IX[:, :, 1, :], T["lib"][:], ND, ALU.mult, r=("ib", "ND"), w=("ix1",), banks=("C2",))
+    for i in range(2):
+        tt(VN[:, :, i, :], T["lvy"][:, :, i, :], ND, ALU.mult, r=("vy", "ND"), w=("VN%d" % i,), banks=("C2",))
+        tt(VN[:, :, 2 + i, :], T["lvx"][:, :, i, :], ND, ALU.mult, r=("vx", "ND"), w=("VN%d" % (2 + i),), banks=("C2",))
+    vn = ("VN0", "VN1", "VN2", "VN3")
+    ts(D3[:, 1:F, 0:32], T["lia"][:, 1:F], 7.0, None, ALU.is_ge, r=("ia",), w=("D0",))
+    for j in (1, 2):
+        if CFG["halves"] == "V":
+            ts(D3[:, 1:F, 32 * j:32 * j + 32], D3[:, 1:F, 0:32], 0.5, None, ALU.mult, r=("D0",), w=("D%d" % j,), k=0.5)
+        else:
+            act(D3[:, 1:F, 32 * j:32 * j + 32], D3[:, 1:F, 0:32], ACT.Copy, ("D0",), ("D%d" % j,), scale=0.5)
+    act(T["mx"][:], IX[:, :, 1, :], ACT.Abs, ("ix1",), ("mx",), bias=-2.0, scale=2.0)
+    if CFG["sign"] == "V":
+        ts(T["e1"][:], IX[:, :, 1, :], 2.0, 2.0, ALU.is_ge, ALU.mult, r=("ix1",), w=("e1",), k=0.5)
+    else:
+        act(T["e1"][:], IX[:, :, 1, :], ACT.Sign, ("ix1",), ("e1",), bias=-1.5)
+    mm(P1[:, 256:416], Id, T["mx"][:], ("I", "mx"), ("ib1",), "P1", True)
+    mm(P1[:, 256:416], Id, T["e1"][:], ("e1",), ("ib1",), "P1", False, True)
+    act(T["w"][:, :, 0, :], IX[:, :, 0, :], ACT.Exp, ("ix0", "one"), ("w0",), scale=-LN8)
+    act(T["w"][:, :, 1, :], P1[:, 256:416], ACT.Exp, ("ib1", "one"), ("w1",), ("P1",), scale=-LN8 / 2, bias=0.0 if CFG["sign"] == "V" else -LN8 / 2)
     for f in range(F):
-        t = "%d" % min(f, 1)
-        tt(VN[:, f, 0:64], T["lvy"][:, f], ND[:, f], ALU.mult, r=vv + ("ND0" + t, "ND1" + t), w=("VNy%d" % f,))
-        tt(VN[:, f, 64:128], T["lvx"][:, f], ND[:, f], ALU.mult, r=vv + ("ND0" + t, "ND1" + t), w=("VNx%d" % f,))
-    for j in range(4):
-        sg = 0.5 if j % 2 else -0.5
-        act(T["D4"][:, 1:F, 32 * j:32 * j + 32], ND[:, 1:F, 0, :], ACT.Identity, ("ND01",), ("D4%d" % j,), bias=-sg, scale=sg)
+        act(vw[:, f], IX[:, f], ACT.Relu, ("ix0", "ix1"), ("vw%d" % f,), bias=-5.0 * (f + 1), scale=f + 1.0)
 
-    MS, B, Y, P1, AD, OFF, ML, RC = T["MS"], T["B"], T["Y"], T["P1"], T["AD"], T["OFF"], T["ML"], T["RC"]
+    MS, OFF, ML, RC, Pb, Eb, h = [T[s] for s in ("MS", "OFF", "ML", "RC", "Pb", "Eb", "h")]
+
+    def slots(f, pack, key, bank):
+        s = "%d" % f
+        ts(T["Yp"][:, f], T["w"][:, f], pack, -0.4375, ALU.mult, ALU.add, r=("w0", "w1", key), w=("Yp" + s,), banks=(bank,))
+        ts(T["Bp"][:, f], T["Yp"][:, f], 7, None, ALU.bitwise_and, r=("Yp" + s,), w=("Bp" + s,))
+        cp(Pb[:, f, 0:3:2, :], T["Bp"][:, f], r=("Bp" + s,), w=("Pb" + s,))
+
+    def lasts(f0, f1):
+        for f in range(f0, f1):
+            ts(T["Ye"][:, f], T["w"][:, f, 0, :], C2[:, 8 + f:9 + f], -0.4375, ALU.mult, ALU.add, r=("w0", "packE"), w=("Ye%d" % f,), banks=("C2",))
+        ts(T["Be"][:, f0:f1], T["Ye"][:, f0:f1], 7, None, ALU.bitwise_and, r=tuple("Ye%d" % f for f in range(f0, f1)), w=("Be%d" % f0,))
+        cp(Eb[:, f0:f1], T["Be"][:, f0:f1], r=("Be%d" % f0,), w=tuple("Eb%d" % f for f in range(f0, f1)))
 
     def addresses(f):
-        s, t = "%d" % f, "%d" % min(f, 1)
-        m0 = (f + 1) * MW
-        act(T["nv"][:, f, :], idx[:, f], ACT.Relu, ("idx0" + t, "idx1" + t), ("nv" + s,), bias=-5.0 * (f + 1), scale=float(f + 1))
-        pk, pb, pkey = (C1, "C1", "pack") if f else (T["X2"], "X2", "pack0")
-        ts(Y[:, f, 32:96], T["w"][:, f], pk[:, 16 + f:17 + f], -0.4375, ALU.mult, ALU.add, r=("w" + t, pkey), w=("Yp" + s,), banks=(pb,))
-        ts(Y[:, f, 0:32], T["w"][:, f, 0, :], C1[:, 21 + f:22 + f], -0.4375, ALU.mult, ALU.add, r=("w" + t, "pack"), w=("Ye" + s,), banks=("C1",))
+        s = "%d" % f
+        m0 = (3 + f) * MW
+        c0 = 0 if 0 < f < F - 1 else 32
+        lo = 0 if f else 32
+        mm(P1[:, lo:160], Id, T["cK"][:, c0:c0 + 160 - lo], ("I", "c16", "c128"), ("P1",), "P1", True)
+        mm(P1[:, 32:160], Id, T["K1"][:], ("K10", "K11", "K12"), ("P1",), "P1")
+        mm(P1[:, 32:160], Id, VN[:, f], vn, ("P1",), "P1", False, f == 0)
         if f:
-            ts(B[:, f, :], Y[:, f, :], 7, None, ALU.bitwise_and, r=("Yp" + s, "Ye" + s), w=("B" + s,))
-        else:
-            ts(B[:, f, 32:96], Y[:, f, 32:96], 7, None, ALU.bitwise_and, r=("Yp" + s,), w=("B" + s,))
-            ts(MS[:, m0:m0 + 64], Y[:, f, 0:64], 7, None, ALU.bitwise_and, r=("Yp" + s, "Ye" + s), w=("MS1a",))
-        tt(T["PB"][:, f, :], B[:, f, 32:96], T["nv"][:, f, :], ALU.subtract, r=("B" + s, "nv" + s), w=("PB" + s,))
-        p1 = P1[:, 0:128]
-        mm(p1, Id, T["c128"][:, 0:128], True, False, ("I", "c128"), ("P1",), "P1")
-        mm(p1, Id, T["K1"][:], False, False, k1, ("P1",), "P1")
-        mm(p1, Id, VN[:, f], False, f == 0, ("VNy" + s, "VNx" + s), ("P1",), "P1")
-        if f:
-            mw = MS[:, 0:m0]
-            mk = tuple("MS%d%s" % (j, u) for j in range(1, f + 1) for u in "ab") + ("MS0", "ML" + s)
-            ts(ML[:, f, :], T["CL"][:], T["s3"][:, f:f + 1], None, ALU.add, r=cl + ("s3",), w=("ML" + s,))
-            act(T["thr"][:, f, :], ND[:, f], ACT.Identity, ("ND01", "ND11"), ("thr" + s,), bias=float(f), scale=99.0)
-            tt(T["h"][:, f, :], mw.indirect(ML[:, f, 8:16]), T["D4"][:, f, :], ALU.mult, r=mk + ("D40", "D41", "D42", "D43"), w=("h" + s,))
-            tt(T["ok"][:, f, :], mw.indirect(ML[:, f, 0:4]), T["thr"][:, f, :], ALU.is_ge, r=mk + ("thr" + s,), w=("ok" + s,))
-            tt(T["df"][:, f, :], mw.indirect(ML[:, f, 4:8]), B[:, f, 0:64], ALU.subtract, r=mk + ("B" + s,), w=("df" + s,))
-            tt(T["M3"][:, f, 0:64], T["ok"][:, f, :], T["df"][:, f, :], ALU.mult, r=("ok" + s, "df" + s), w=("m" + s,))
-            mm(p1, Id, T["h"][:, f, :], False, True, ("h" + s,), ("P1",), "P1")
+            mk = tuple("MS%d%s" % (j, u) for j in range(1, f + 1) for u in "ab") + ("MS0", "ML" + s, "D0", "D1", "D2")
+            tt(h[:, f], MS[:, 0:m0].indirect(ML[:, f, 0:6]), D3[:, f], ALU.mult, r=mk, w=("h" + s,), k=1.56, x=50.0)
+            act(T["t"][:, f], h[:, f, 0:32], ACT.Relu, ("h" + s,), ("t" + s,), bias=-128.0 * (16 * (f + 2) - 1), scale=128.0)
+            mm(P1[:, 0:32], Ng, vw[:, f, 0, :], ("N", "vw" + s), ("P1",), "P1")
+            mm(P1[:, 0:32], Id, Pb[:, f, 0, :], ("Pb" + s,), ("P1",), "P1")
+            if f + 1 < F:
+                mm(P1[:, 0:32], I16, Eb[:, f], ("Eb" + s,), ("P1",), "P1")
+            for j in range(4):
+                mm(P1[:, 32 + 32 * j:64 + 32 * j], Ng if j % 2 else Id, h[:, f, 32 + 32 * (j // 2):64 + 32 * (j // 2)], ("h" + s,), ("P1",), "P1")
+            mm(P1[:, 0:32], Ng, T["t"][:, f], ("t" + s,), ("P1",), "P1", False, True)
+            tt(MS[:, m0:m0 + 32], P1[:, 0:32], h[:, f, 0:32], ALU.max, r=("P1", "h" + s), w=("MS%da" % (f + 1),), banks=("P1",))
         for i, hi in ((0, 159.0), (1, 143.0)):
-            ts(RC[:, f, 64 * i:64 * i + 64], P1[:, 64 * i:64 * i + 64], 128.0, hi, ALU.max, ALU.min, r=("P1",), w=("RC%d%s" % (i, s),), banks=("P1",))
-        if f + 1 < F:
-            tt(MS[:, m0 + 64:m0 + MW], P1[:, 0:96], T["K2"][:], ALU.subtract, r=("P1", "K2"), w=("MS%db" % (f + 1),), banks=("P1",), k=1.0)
-            if f:
-                tt(MS[:, m0:m0 + 64], T["M3"][:, f, 0:64], B[:, f, 0:64], ALU.add, r=("m" + s, "B" + s), w=("MS%da" % (f + 1),))
-        ad = AD[:, 0:64]
-        mm(ad, T["I16"][:], RC[:, f, 0:64], True, False, ("I16", "RC0" + s), ("AD",), "AD")
-        mm(ad, Id, RC[:, f, 64:128], False, False, ("RC1" + s,), ("AD",), "AD")
+            ts(RC[:, f, 64 * i:64 * i + 64], P1[:, 32 + 64 * i:96 + 64 * i], 128.0, hi, ALU.max, ALU.min, r=("P1",), w=("RC%d%s" % (i, s),), banks=("P1",))
+        if f == 0:
+            act(MS[:, m0 + 32:m0 + MW], VN[:, 0, 0:3:2, :], ACT.Copy, vn, ("MS1b",))
+        elif f + 1 < F:
+            mm(C0[:, 0:64], Id, T["qm"][:, 0:64], ("qm",), ("PU",), "C0", True)
+            for i in range(2):
+                mm(C0[:, 32 * i:32 * i + 32], Id, VN[:, f, 2 * i, :], vn, ("PU",), "C0")
+            mm(C0[:, 0:64], Id, h[:, f, 32:96], ("h" + s,), ("PU",), "C0")
+            mm(C0[:, 0:64], Id, T["cM"][:, 0:64], ("cM",), ("PU",), "C0")
+            mm(C0[:, 0:64], Ng, T["cM"][:, 0:64], (), ("PU",), "C0", False, True)
+            act(MS[:, m0 + 32:m0 + MW], C0[:, 0:64], ACT.Copy, ("PU",), ("MS%db" % (f + 1),), ("C0",))
+        mm(AD[:, 0:64], Id, Pb[:, f, 1:3, :], ("Pz", "Pb" + s), ("AD",), "AD", True)
+        mm(AD[:, 32:64], Ng, vw[:, f, 1, :], ("N", "vw" + s), ("AD",), "AD")
         if f:
-            mm(ad, T["I512"][:], T["M3"][:, f, 32:96], False, False, ("I512", "m" + s, "M3z"), ("AD",), "AD")
-        mm(ad, T["I512"][:], T["PB"][:, f, :], False, True, ("I512", "PB" + s), ("AD",), "AD")
-        ts(OFF[:, f, :], ad, 512.0 * (f + 1) - 2176.0, None, ALU.add, r=("AD",), w=("OFF" + s,), banks=("AD",))
-        if not second and F0 <= f < F - 1:
-            send(nxt, T["OF2"][:, f, :], OFF[:, f, :], "of" + s, ("OFF" + s,), "sento" + s)
+            cn = MS[:, m0:m0 + 32]
+            for m, x in ((Ng, cn), (Id, T["cM2"][:]), (Ng, T["cM2"][:]), (Id, cn)):
+                mm(AD[:, 0:32], m, x, ("MS%da" % (f + 1), "cM2"), ("AD",), "AD")
+        else:
+            mm(AD[:, 0:32], Id, Pb[:, f, 0, :], (), ("AD",), "AD")
+            mm(AD[:, 0:32], Ng, vw[:, f, 0, :], (), ("AD",), "AD")
+        mm(AD[:, 0:64], T["I32i"][:], RC[:, f, 0:64], ("I32i", "RC0" + s), ("AD",), "AD")
+        mm(AD[:, 0:64], T["I512i"][:], RC[:, f, 64:128], ("I512i", "RC1" + s), ("AD",), "AD", False, True)
+        ts(OFF[:, f, :], AD[:, 0:64], 512.0, 512.0 * (f + 1) - 2176.0, ALU.mult, ALU.add, r=("AD",), w=("OFF" + s,), banks=("AD",))
+
+    slots(0, AD[:, 64:65], "pack0", "AD")
+    addresses(0)
+    places(F, [(ZU[:, 2, 0:5], allz), (ZU[:, 1, 0:5], alll)], (ZU[:, 6, 0:5], allz), [(ZU[:, 5, 0:5], allz), (T["LN"][:, 0:5], ("LN0", "LN1"))],
+           T["wts"][:], "wts")
+    ts(T["eq"][:], T["wts"][:, 0:3], 8.0, float(MW), ALU.is_equal, ALU.mult, r=("wts",), w=("eq",))
+    for bank, c0, l, x, m, r, name in (("C2", 8, "LE", "wts", 4, "LE", "packE"), ("C2", 0, "LPh", "wts", 4, "LS", "pack"),
+                                       ("C0", 256, "LPh", "eq", 3, "LS", "packM")):
+        for s in range(m):
+            mm(T[bank][:, c0:c0 + 5], T[l][:], T[x][:, s, :], (r, x), (name,), bank, s == 0, s + 1 == m)
+    for f in range(1, F):
+        ts(ML[:, f, 0:6], T["CL"][:, 0:6], C0[:, 256 + f:257 + f], None, ALU.add, r=("CL", "packM"), w=("ML%d" % f,), banks=("C0",))
+    mm(P1[:, 0:32], Id, T["cK"][:, 0:32], ("c16",), ("P1",), "P1", True)
+    mm(P1[:, 0:32], Id, Pb[:, 0, 0, :], ("Pb0",), ("P1",), "P1", False, True)
+    ts(T["Ye"][:, 0], T["w"][:, 0, 0, :], C2[:, 8:9], 16.0, ALU.mult, ALU.mult, r=("w0", "packE"), w=("Ye0",), banks=("C2",))
+    ts(T["Be"][:, 0], T["Ye"][:, 0], 7 * 16, None, ALU.bitwise_and, r=("Ye0",), w=("Be0",))
+    tt(MS[:, 3 * MW:3 * MW + 32], P1[:, 0:32], T["Be"][:, 0], ALU.add, r=("P1", "Be0"), w=("MS1a",), banks=("P1",))
+    lasts(1, 2)
+    for f in range(1, F):
+        slots(f, C2[:, f:f + 1], "pack", "C2")
+        if f == 2:
+            lasts(2, 4)
+        addresses(f)
 
     nch = range(len(CH))
+    have = {True: ["blank", "pic0", "pic1", "V0"], False: ["blank2", "pics2", "pics3"]}
+    turns, held_back, stores, gathers = [0], [], [], []
 
     def pixels(f, own):
         s = "%d" % f
         end = f + 1 == F
-        turn = (second or f < F0) and not end
+        turn = not end and (not own or f not in theirs or f + 1 in mine)
         sh = 16 * (f + 1) if turn else 0
         rot, nrot = T["W2"][:, sh:sh + 128], T["N2"][:, sh:sh + 128]
         if own:
-            ww, off, rs, rk = win, OFF, T["rs"], "rs" + s
-            wk = ("blank", "pic0", "pic1", "OFF" + s) + tuple(views["V"]) + tuple(views.get("F", ()))
+            ww, off, rs, rk, wk = win, OFF, res(f), "rs" + s, ["OFF" + s]
         else:
-            ww, off, rs, rk = win2, T["OF2"], rs2, "rs2_%d" % f
-            wk = ("blank2", "pics2", "pics3", "OF2_" + s) + tuple(k for k in views["W"] if int(k[1]) <= f) + tuple("G%d" % j for j in range(f))
+            ww, off, rs, rk = win2, T["OF2"], res2(f, mine), "rs2_" + s
+            wk = ["OF2_" + s] + [u % j for j in mine if j <= f for u in ("W%d", "rs2_%d")] + ["spare%d" % j for j in spare]
+        wk = tuple(wk + have[own])
         ww = ww[:, (V0 - f) * P:(SB + 3 + f) * P]
-        for c, (a, b, _) in enumerate(CH):
-            X, xb = T["X%d" % c][:, 0:b - a], "X%d" % c
-            mm(X, rot, rs[:, f * P + a:f * P + b], True, False, ("I", "I2", rk), (xb,), xb)
-            mm(X, Id, T["qm"][:, 0:b - a], False, False, ("qm",), (xb,), xb)
-        for c, (a, b, _) in enumerate(CH):
-            ts(T["gp"][:, a:b], ww.indirect(off[:, f, a // 16:b // 16]), 255.0, 0.5, ALU.min, ALU.mult, r=wk, w=("gp%d" % c,), k=1.56, x=50.0)
-            act(T["gq"][:, a:b], ww.indirect(off[:, f, 32 + a // 16:32 + b // 16]), ACT.Relu, wk, ("gq%d" % c,), bias=127.5, scale=-0.5, k=1.56, x=65.0)
+        z = turns[0] % 2
+        turns[0] += 1
+        gp, gq = T["gp"][:, z], T["gq"][:, z]
+        sums = []
+        for c, (a, b) in enumerate(CH):
+            xb, x0 = ("X%d" % c, 0) if own or not held_back else CFG["pair"][f][c]
+            X, xk = T[xb][:, x0:x0 + b - a], xb + "%d" % x0
+            sums.append((X, xb, xk))
+            mm(X, rot, rs[:, a:b], ("I", "I2", rk), (xk,), xb, True)
+            mm(X, Id, T["qm"][:, 0:b - a], ("qm",), (xk,), xb)
+            if end and CFG["end"][c] == "V":
+                mm(X, Id, T["cK"][:, 32:32 + b - a], ("c128",), (xk,), xb)
+        for c, (a, b) in enumerate(CH):
+            i = ts(gp[:, a:b], ww.indirect(off[:, f, a // 16:b // 16]), 255.0, 0.5, ALU.min, ALU.mult, r=wk, w=("gp%d%d" % (z, c),), k=1.56, x=50.0)
+            j = act(gq[:, a:b], ww.indirect(off[:, f, 32 + a // 16:32 + b // 16]), ACT.Relu, wk, ("gq%d%d" % (z, c),), bias=127.5, scale=-0.5, k=1.56, x=65.0)
+            if gathers:
+                ops[i]["order"], ops[j]["order"] = gathers
+            gathers[:] = [i, j]
         if end or (own and turn):
             dst, name = T["snd"][:, f * P:(f + 1) * P], "snd"
         elif own:
             dst, name = slot(SB + 3 + f), "F"
         else:
             dst, name = slot(V0 - f - 1), "Vl"
-        sk = tuple("%s%s%d" % (name, s, j) for j in nch)
-        for c, (a, b, who) in enumerate(CH):
-            X, xb = T["X%d" % c][:, 0:b - a], "X%d" % c
+        sk = tuple("%s%s_%d" % (name, s, j) for j in nch)
+
+        def finish(c):
+            (X, xb, xk), (a, b) = sums[c], CH[c]
             o, ok = dst[:, a:b], sk[c:c + 1]
-            mm(X, rot, T["gp"][:, a:b], False, False, ("gp%d" % c,), (xb,), xb)
-            mm(X, nrot, T["gq"][:, a:b], False, end, ("N2", "gq%d" % c), (xb,), xb)
-            if end:
-                ts(T["yy"][:, a:b], X, MAGIC + 128.0, MAGIC + 255.0, ALU.add, ALU.min, r=(xb,), w=("yy%d" % c,), banks=(xb,))
-                act(o, T["yy"][:, a:b], ACT.Relu, ("yy%d" % c,), ok, bias=-MAGIC)
-                dma("A" if c + 1 == len(CH) else "S", T.y[:, f * P + a:f * P + b], o, "dy", r=ok, nbytes=(b - a) * 256)
-                continue
-            mm(X, Id, T["cM"][:, 0:b - a], False, True, ("cM",), (xb,), xb)
-            if who == "V":
-                ts(o, X, 128.0 - MAGIC, 0.0, ALU.add, ALU.max, r=(xb,), w=ok, banks=(xb,))
+            if end and CFG["end"][c] == "V":
+                ts(o, X, 0.0, 255.0, ALU.max, ALU.min, r=(xk,), w=ok, banks=(xb,))
+            elif end:
+                act(T["tb"][:, a:b], X, ACT.Relu, (xk,), ("last%d" % c,), (xb,), bias=128.0 - MAGIC)
+                ts(o, T["tb"][:, a:b], 255.0, None, ALU.min, r=("last%d" % c,), w=ok, k=0.5)
+            elif CFG["finish"].get((f, own), "AAA")[c] == "V":
+                ts(o, X, 128.0 - MAGIC, 0.0, ALU.add, ALU.max, r=(xk,), w=ok, banks=(xb,))
             else:
-                act(o, X, ACT.Relu, (xb,), ok, (xb,), bias=128.0 - MAGIC)
+                act(o, X, ACT.Relu, (xk,), ok, (xb,), bias=128.0 - MAGIC)
+            if end:
+                dma("A" if c + 1 == len(CH) else "S", T.y[:, f * P + a:f * P + b], o, "dy", r=ok)
+
+        ys = T.y[:, f * P:(f + 1) * P]
+
+        def store():
+            o = T["tb"][:, f * P:(f + 1) * P]
+            for c, (a, b) in enumerate(CH):
+                ts(o[:, a:b], dst[:, a:b], 255.0, None, ALU.min, r=sk[c:c + 1], w=("yc%s%d" % (s, c),), k=0.5)
+            dma("S", ys, o, "dy", r=tuple("yc%s%d" % (s, c) for c in nch))
+
+        wait = own and not turn and f in mine and CFG["pair"]
+        for c, (a, b) in enumerate(CH):
+            X, xb, xk = sums[c]
+            both = end and CFG["end"][c] == "V"
+            mm(X, rot, gp[:, a:b], ("gp%d%d" % (z, c),), (xk,), xb)
+            mm(X, nrot, gq[:, a:b], ("N", "gq%d%d" % (z, c)), (xk,), xb)
+            mm(X, Id, T["cM"][:, 0:b - a], ("cM",), (xk,), xb, False, not both)
+            if both:
+                mm(X, Ng, T["cM"][:, 0:b - a], (), (xk,), xb, False, True)
+            if wait:
+                held_back.append(finish)
+                continue
+            finish(c)
+            if held_back:
+                held_back.pop()(c)
         if end:
             return
-        ys = T.y[:, f * P:(f + 1) * P]
-        if not second:
-            views["V"].extend("V%d" % (f + 1) if i == 0 else "V%d_%d" % (f + 1, i) for i, j in SENDS[f + 1])
-            if not turn:
-                views.setdefault("F", []).extend(sk)
-                o = T["snd"][:, f * P:(f + 1) * P]
-                ts(o, dst, 255.0, None, ALU.min, r=sk, w=("yc" + s,), k=0.5)
-                dma("S", ys, o, "dy", r=("yc" + s,), nbytes=131072)
-                return
-            gone = "sentv%d" % (f + 1)
-            after_send(f, gone, send(nxt, slot(V0 - f - 1), dst, "arr%d" % (f + 1), sk, gone, False, "ls%d" % (f + 1)))
-        elif own:
-            for i, j in SENDS[f + 1]:
-                view_out(f + 1, dst[:, CH[i][0]:CH[j - 1][1]], CH[i][0], CH[j - 1][1], sk[i:j])
-            gone = "sentA%d_0" % (f + 1)
-            after_send(f, gone, None)
-        else:
-            views["V"].extend(sk)
-        if own:
-            mm(C0[:], T["W2"][:, 128 - sh:256 - sh], dst, True, True, sk, ("UN",), "C0")
-            views.setdefault("F", []).append("F" + s)
-            o = T["tb"][:, f * P:(f + 1) * P]
-            if f in YCA:
-                act(o, C0[:], ACT.Relu, ("UN",), ("tb" + s,), ("C0",), bias=255.0, scale=-1.0)
-                act(slot(SB + 3 + f), o, ACT.Identity, ("tb" + s,), ("F" + s,), bias=255.0, scale=-1.0)
-                dma("S", ys, slot(SB + 3 + f), "dy", r=("F" + s, gone), nbytes=131072)
-                return
-            act(slot(SB + 3 + f), C0[:], ACT.Copy, ("UN",), ("F" + s,), ("C0",))
-            ts(o, slot(SB + 3 + f), 255.0, None, ALU.min, r=("F" + s,), w=("yc" + s,), k=0.5)
-            dma("S", ys, o, "dy", r=("yc" + s, gone), nbytes=131072)
-        elif f + 2 < F:
+        if not own:
+            have[True].extend(sk)
+            if stores:
+                stores.pop()()
             turn_back(f, sk)
+            return
+        if f not in mine:
+            have[True].append("V%d" % (f + 1))
+        if not turn:
+            have[True].extend(sk)
+            if wait:
+                stores.append(store)
+            else:
+                store()
+            return
+        if f and CFG["ahead"]:
+            hand("o", f + 1)
+        gone = view_out(f + 1, dst, sk)
+        hand("o", f + 1)
+        hand("r", f + 3)
+        mm(C1[:], T["W2"][:, 128 - sh:256 - sh], dst, sk, ("UN",), "C1", True, True)
+        ts(slot(SB + 3 + f), C1[:], 255.0, None, ALU.min, r=("UN",), w=("F" + s,), banks=("C1",))
+        have[True].append("F" + s)
+        dma("S", ys, slot(SB + 3 + f), "dy", r=("F" + s, gone))
 
     def turn_back(f, keys):
-        sh = 16 * (f + 1)
-        mm(C0[:], T["W2"][:, 128 - sh:256 - sh], slot(V0 - f - 1), True, True, keys, ("UN",), "C0")
-        act(win2[:, (SB + 3 + f) * P:(SB + 4 + f) * P], C0[:], ACT.Copy, ("UN",), ("G%d" % f,), ("C0",))
+        if mine and f < max(mine):
+            sh = 16 * (f + 1)
+            halves = (("A", 0, P, "C1"),) if f in mine or not CFG["split"] else (("A", 0, P // 2, "C1"), ("V", P // 2, P, "C2"))
+            for who, a, b, bank in halves:
+                x, o, key = T[bank][:, 0:b - a], slot(SB + 3 + f, win2)[:, a:b], "G%d%s" % (f, who)
+                mm(x, T["W2"][:, 128 - sh:256 - sh], slot(V0 - f - 1)[:, a:b], keys, ("UN" + who,), bank, True, True)
+                if who == "A":
+                    act(o, x, ACT.Copy, ("UN" + who,), (key,), (bank,))
+                else:
+                    cp(o, x, ("UN" + who,), (key,), (bank,))
+                have[False].append(key)
 
     for f in range(F):
-        addresses(f)
-    for f in range(F):
+        hand("o", f)
+        hand("r", f + 1)
         pixels(f, True)
-        if second and F0 <= f < F - 1:
+        if f in mine:
             pixels(f, False)
-        elif second and f < F0:
-            views["V"].append("V%d" % (f + 1))
+        elif f + 1 < F:
             turn_back(f, ("V%d" % (f + 1),))
     return ops
 
@@ -535,7 +627,7 @@ def plan(ops):
     def gap(d, k):
         if (ops[d]["q"] == "P" and ops[k]["q"] == "P") or (d == ops[k].get("order") and d not in ops[k]["deps"]):
             return 0.0
-        return ops[d]["lat"] + HOP
+        return ops[k]["after"] if "after" in ops[k] else ops[d]["lat"] + (0.0 if ops[k]["q"] == "X" else CFG["hop"])
 
     def sweep(prio, before, after, rev):
         start, busy = [0.0] * n, {}
@@ -549,7 +641,7 @@ def plan(ops):
                 left[s] -= 1
                 if not left[s]:
                     ready.append((prio[s], s))
-            t = max(ops[k]["lat"], ops[k].get("tail", 0.0)) if rev else ops[k].get("rel", 0.0)
+            t = ops[k]["lat"] if rev else 0.0
             for d in before[k]:
                 t = max(t, start[d] + ops[d]["dur"] + (gap(k, d) if rev else gap(d, k)))
             iv = busy.setdefault(ops[k]["lane"], [])
@@ -562,7 +654,7 @@ def plan(ops):
             iv.sort()
         return start
 
-    end = lambda st: max(st[k] + ops[k]["dur"] + max(ops[k]["lat"], ops[k].get("tail", 0.0)) for k in range(n))
+    end = lambda st: max(st[k] + ops[k]["dur"] + ops[k]["lat"] for k in range(n))
     rk, seed = [0.0] * n, [12345]
     left = [len(s) for s in suc]
     todo = [k for k in range(n) if not left[k]]
@@ -580,14 +672,100 @@ def plan(ops):
 
     start = sweep([-r for r in rk], pre, suc, False)
     best = (end(start), start)
-    for it in range(SWEEPS):
+    for it in range(CFG["sweeps"]):
         a, start = 400.0 * (it % 3 > 0), best[1]
         back = sweep([jit(a) - start[j] - ops[j]["dur"] for j in range(n)], suc, pre, True)
         start = sweep([jit(a) - back[j] - ops[j]["dur"] for j in range(n)], pre, suc, False)
         if end(start) < best[0]:
             best = (end(start), start)
     start = best[1]
-    return sorted(range(n), key=lambda j: (start[j], j)), start
+    return polish(ops, pre, suc, gap, sorted(range(n), key=lambda j: (start[j], j)), jit)
+
+
+def polish(ops, pre, suc, gap, seq, jit):
+    n, hop = len(ops), CFG["hop"]
+    lanes = {}
+    lane = [lanes.setdefault(o["lane"], len(lanes)) for o in ops]
+    up = [0] * n
+    for k in seq:
+        for d in pre[k]:
+            up[k] |= up[d] | 1 << d
+    near = [[d for d in pre[k] if ops[d]["lat"] or not any(up[e] >> d & 1 for e in pre[k])] for k in range(n)]
+    cases = []
+    for speed, wait, link in CFG["cases"]:
+        dur = [o["dur"] * (speed if o["q"] in "VAP" else link if o["q"] == "X" else 1.0) for o in ops]
+        edges = []
+        for k in range(n):
+            e = []
+            for d in near[k]:
+                g0 = gap(d, k)
+                e.append((d, g0 - hop + wait if g0 and ops[k]["q"] != "X" else g0))
+            edges.append(e)
+        cases.append((dur, edges))
+    tail = [o["lat"] for o in ops]
+    marks = [k for k in range(n) if ops[k].get("mark")]
+
+    sinks = [k for k in range(n) if not suc[k]]
+    weight = [(j, ops[j]["mark"]) for j in marks]
+
+    def run(seq, case, i=0, old=None):
+        dur, edges = case
+        end, why = (old[1][:], old[2][:]) if old else ([0.0] * n, [-1] * n)
+        free, last = [0.0] * len(lanes), [-1] * len(lanes)
+        for k in seq[max(0, i - 160):i] if old else ():
+            free[lane[k]], last[lane[k]] = end[k], k
+        for k in seq[i:]:
+            l = lane[k]
+            t, w = free[l], last[l]
+            for d, g0 in edges[k]:
+                if end[d] + g0 >= t:
+                    t, w = end[d] + g0, d
+            end[k] = free[l] = t + dur[k]
+            why[k], last[l] = w, k
+        k = max(sinks, key=lambda j: end[j] + tail[j])
+        return end[k] + tail[k] + sum(end[j] * m for j, m in weight), end, why, k
+
+    now = [run(seq, c) for c in cases]
+    best = (sum(r[0] for r in now), seq)
+    for it in range(CFG["polish"]):
+        _, end, why, k = now[it % len(cases)]
+        if it % 5 > 1:
+            k = marks[int(jit(len(marks)))]
+        pairs = []
+        while why[k] >= 0:
+            if lane[why[k]] == lane[k] and not up[k] >> why[k] & 1:
+                pairs.append((why[k], k))
+            k = why[k]
+        if not pairs:
+            continue
+        u, k = pairs[int(jit(len(pairs)))]
+        i, j = seq.index(u), seq.index(k)
+        mid = seq[i + 1:j]
+        how = jit(1.0)
+        if how < 0.35:
+            new = seq[:i] + [x for x in mid if up[k] >> x & 1] + [k, u] + [x for x in mid if not up[k] >> x & 1] + seq[j + 1:]
+        elif how < 0.7:
+            new = seq[:i] + [x for x in mid if not up[x] >> u & 1] + [k, u] + [x for x in mid if up[x] >> u & 1] + seq[j + 1:]
+        elif how < 0.85:
+            j = min(n, j + 1 + int(jit(jit(500))))
+            mid = seq[i + 1:j]
+            new = seq[:i] + [x for x in mid if not up[x] >> u & 1] + [u] + [x for x in mid if up[x] >> u & 1] + seq[j:]
+        else:
+            j, i = i, max(0, i - 1 - int(jit(jit(500))))
+            mid = seq[i:j]
+            new = seq[:i] + [x for x in mid if up[u] >> x & 1] + [u] + [x for x in mid if not up[u] >> x & 1] + seq[j + 1:]
+        got = [run(new, c, i, o) for c, o in zip(cases, now)]
+        a, b = sum(r[0] for r in got), sum(r[0] for r in now)
+        if a <= b + jit(CFG["heat"] * (1.0 - it / CFG["polish"])):
+            seq, now = new, got
+            if a < best[0]:
+                best = (a, new)
+            if it % 16 == 0:
+                dur, end = cases[0][0], now[0][1]
+                place = {x: i for i, x in enumerate(seq)}
+                seq = sorted(seq, key=lambda x: (end[x] - dur[x], place[x]))
+    end = run(best[1], cases[0])[1]
+    return best[1], [end[k] - cases[0][0][k] for k in range(n)]
 
 
 def rank_program(g, core, T, topo):
@@ -657,4 +835,4 @@ def rank_program(g, core, T, topo):
             ins.then_inc(T.sem[o["sem"]], 16)
     for s in sorted(total):
         if s not in waited:
-            (g if s == "ls" else g.sync).wait_ge(T.sem[s], total[s])
+            (g if s.startswith("ls") else g.sync).wait_ge(T.sem[s], total[s])

import math
from concourse.mybir import AluOpType as ALU, ActivationFunctionType as ACT

F = 5
P = 512
CH = ((0, 192), (192, 384), (384, 512))
CW = 256
MAGIC = 12582912.0
LN8 = math.log(8.0)
V0 = F - 1
SB = F
MW = 96
CFG = {
    "remake": {False: (1, 3), True: (1, 3)},
    "finish": {(1, True): "AVV", (3, True): "AVV", (1, False): "AVA", (3, False): "AVA", (0, True): "AVA", (2, True): "AVA"},
    "parts": ((0, 3),),
    "cases": ((0.85, 220.0, 1.0), (1.05, 150.0, 1.1)), "polish": 20000, "heat": 80.0, "marks": {"A": 0.4, "o": 0.2}, "ahead": False,
    "late": 2, "copies": "VA", "rate": 34.0, "split": True,
    "pair": {1: (("X0", 256), ("C2", 0), ("C1", 0)), 3: (("P1", 0), ("AD", 0), ("C0", 0))}, "end": "VVV", "quick": True,
    "halves": "A", "sign": "A", "cyc": 1.1, "pe": 0.55, "hop": 200.0, "sweeps": 10, "issue": 350.0, "lat": 1500.0, "col": 1.25,
}


def _sb(shape, dt):
    return ("sbuf", [128] + shape, dt)


BF, F32, I32, U16 = "bfloat16", "float32", "int32", "uint16"
SCRATCH = {
    "win": _sb([12 * P], BF), "rs": _sb([F * P], BF), "snd": _sb([F * P], BF),
    "win2": _sb([11 * P], BF), "rs2": _sb([(F - 1) * P], BF), "OF2": _sb([F - 1, 64], U16),
    "gp": _sb([2, P], BF), "gq": _sb([2, P], BF), "tb": _sb([(F - 1) * P], BF),
    "ctl": _sb([2, 16], I32), "ctb": _sb([3, 32], BF), "Tb": _sb([128], BF), "Coef": _sb([50], BF),
    "lia": _sb([F, 32], I32), "lib": _sb([F, 32], I32), "lvy": _sb([F, 2, 32], I32), "lvx": _sb([F, 2, 32], I32),
    "cA": _sb([128], F32), "cB": _sb([8, 16], F32), "fr": _sb([25], F32), "LK": _sb([25], F32), "c21": _sb([25], BF),
    "pi": _sb([2], I32), "pj": _sb([4], I32), "col": _sb([12], F32), "ce": _sb([4, F], BF), "rw": _sb([32], F32),
    "W2": _sb([256], BF), "N2": _sb([256], BF), "I16": _sb([128], BF), "N16": _sb([128], BF), "I32i": _sb([128], BF), "I512i": _sb([128], BF),
    "OO": _sb([128], BF), "NO": _sb([128], BF), "NU": _sb([128], BF), "NL": _sb([128], BF),
    "tU": _sb([128], BF), "tL": _sb([128], BF), "E8": _sb([128], BF),
    "LP0": _sb([128], BF), "LPh": _sb([128], BF), "LE": _sb([128], BF),
    "qm": _sb([CW], BF), "cK": _sb([32 + CW], BF), "cM": _sb([CW], BF), "cM2": _sb([32], BF), "K1": _sb([128], BF),
    "cc": _sb([32], F32), "CL": _sb([8], F32), "Q": _sb([27, 6], BF), "R": _sb([8], BF), "SS": _sb([5, F], F32),
    "ZU": _sb([7, 6], BF), "LN": _sb([8], BF), "sc": _sb([4], F32), "jk": _sb([24], BF),
    "wts": _sb([4, F], BF), "wts0": _sb([4], BF), "eq": _sb([3, F], BF), "ML": _sb([F, 8], U16),
    "IX": _sb([F, 2, 32], BF), "mx": _sb([F, 32], BF), "e1": _sb([F, 32], BF), "w": _sb([F, 2, 32], BF), "vw": _sb([F, 2, 32], BF),
    "D3": _sb([F, MW], BF), "VN": _sb([F, 4, 32], BF), "Yp": _sb([F, 64], I32), "Bp": _sb([F, 64], I32),
    "Ye": _sb([F - 1, 32], I32), "Be": _sb([F - 1, 32], I32), "Pb": _sb([F, 3, 32], BF), "Eb": _sb([F - 1, 32], BF),
    "MS": _sb([8 * MW], BF), "h": _sb([F, MW], BF), "t": _sb([F, 32], BF), "RC": _sb([F, 128], BF), "OFF": _sb([F, 64], U16),
}
for _n in ("X0", "X1", "X2", "C0", "C1", "C2", "P1", "AD"):
    SCRATCH[_n] = ("psum", [128, 512], F32)
SEMAPHORES = (["nV", "nA", "nP", "nG", "dctl", "da", "db", "dvy", "dvx", "dp0", "dp1", "dy", "ls", "pp", "dk", "ds1", "dbl"]
              + [s + str(f) for s in ("arr", "brr", "of", "rr", "dr", "ls") for f in range(F)])
PLAN = {}


def joint(T, topo):
    if not PLAN:
        pair = sorted(T.cores[:2], key=lambda c: T.cores[T.rank_of(c) - 1] in topo.cores_of(c))
        parts = [build(T, topo, c) for c in pair]
        names = [{o["name"][0]: k for k, o in enumerate(p) if o["name"]} for p in parts]
        base, ops = (0, len(parts[0])), []
        for i, p in enumerate(parts):
            for o in p:
                u = dict(o, lane=o.get("lane", o["q"]) + str(i), deps={d + base[i] for d in o["deps"]}, soft={d + base[i] for d in o["soft"]})
                if "order" in o:
                    u["order"] = o["order"] + base[i]
                u["soft"].update(p[d]["move"] + base[i] for d in o["deps"] if "move" in p[d])
                for same, name in o.get("link", ()):
                    j = i if same else 1 - i
                    u["soft"].add(names[j][name] + base[j])
                ops.append(u)
        order, start = plan(ops)
        PLAN[False] = [k for k in order if k < base[1]]
        PLAN[True] = [k - base[1] for k in order if k >= base[1]]
        PLAN["ops"], PLAN["start"] = ops, start
    return PLAN


def build(T, topo, core):
    rank = T.rank_of(core)
    n = len(T.cores)
    nxt, prv, nx2 = T.cores[(rank + 1) % n], T.cores[(rank - 1) % n], T.cores[(rank + 2) % n]
    second = prv in topo.cores_of(core)
    mine, theirs = CFG["remake"][second], CFG["remake"][not second]
    cyc, parts = CFG["cyc"], CFG["parts"]
    ops, wr, rd, bk, lastdma = [], {}, {}, {}, {}

    def op(q, fn, r=(), w=(), banks=(), dur=70.0, lat=0.0, sem=None, inc=0, soft=()):
        k = len(ops)
        deps = set()
        for key in r:
            deps.add(wr[key])
        for key in w:
            if key in wr:
                deps.add(wr[key])
            deps.update(rd.get(key, ()))
        for b in banks:
            deps.update(o for qq, o in bk.get(b, ()) if qq != q or q == "P")
            bk.setdefault(b, []).append((q, k))
        for key in r:
            rd.setdefault(key, []).append(k)
        for key in w:
            wr[key] = k
            rd[key] = []
        ops.append({"q": q, "fn": fn, "deps": deps, "soft": set(soft), "dur": dur, "lat": lat, "sem": sem, "inc": inc, "name": tuple(w)})
        return k

    def el(ap):
        m = 1
        for s in ap.shape[1:]:
            m *= s
        return m

    def ts(out, in0, s1, s2, o0, o1=None, r=(), w=(), banks=(), k=1.0, x=0.0):
        if o1 is None:
            fn = lambda e: e.tensor_scalar(out, in0, s1, None, o0)
        else:
            fn = lambda e: e.tensor_scalar(out, in0, s1, s2, o0, o1)
        return op("V", fn, r, w, banks, max(64, el(out) * k) * cyc + x)

    def tt(out, a, b, o, r=(), w=(), banks=(), k=2.0, x=0.0):
        return op("V", lambda e: e.tensor_tensor(out, a, b, o), r, w, banks, max(64, el(out) * (1.0 if banks else k)) * cyc + x)

    def cp(out, a, r=(), w=(), banks=()):
        return op("V", lambda e: e.tensor_copy(out, a), r, w, banks, max(64, el(out)) * cyc)

    def ms(out, v, w):
        return op("V", lambda e: e.memset(out, v), (), w, (), max(64, el(out) / 2) * cyc)

    def mm(out, l, x, r, w, bank, st=False, sp=False):
        return op("P", lambda e: e.matmul(out, l, x, st, sp), r, w, (bank,), max(64, el(out)) * CFG["pe"])

    def act(out, a, fu, r, w, banks=(), bias=0.0, scale=1.0, k=1.0, x=0.0, acc=None):
        return op("A", lambda e: e.activation(out, a, fu, bias, scale, accum_out=acc), r, w, banks, max(64, el(out) * k) * cyc + x)

    def dma(q, out, a, sem, r=(), w=(), wide=1):
        k = op(q, lambda e: e.dma_start(out, a), r, w, (), 70.0, 0.0, sem, 16)
        moves(k, (), 900.0, out.shape[0] / 16.0 * (22.0 + 2 * el(out) * wide / CFG["rate"]), 600.0)
        if q in lastdma:
            ops[k]["order"] = lastdma[q]
        lastdma[q] = k
        return k

    def moves(k, name, before, dur, after):
        j = op("X", None, (), name, (), dur, after, None, 0, (k,))
        ops[j]["lane"], ops[j]["after"], ops[k]["move"] = "D", before, j

    sent, early = [], [True]

    def send(dst, out, a, sem, r, name, ls="ls", after=None):
        rid, pid = topo.addr(dst, core)
        emask, ne = topo.mask(core, dst), len(topo.engines(core, dst))
        fn = lambda e: e.remote_dma(out, a, T.sem[sem], T.sem[ls], pid, rid, emask)
        move = (350.0 + el(out) * CFG["col"]) * 8 / ne
        k = op("G", fn, r, (name,), (), CFG["issue"] + (0.0 if sent else 1200.0 + 40.0 * ne), 0.0, ls, ne)
        moves(k, ("T" + name,), CFG["lat"] / 2, move, CFG["lat"] / 2)
        if sent:
            ops[k]["order"], ops[k + 1]["order"] = sent[-1], sent[-1] + 1
        sent.append(k)
        ops[k]["mark"] = CFG["marks"].get(name[1], 0.0)
        return name

    def arrive(src, sem, key, names):
        k = op("X", None, (), (key,), (), 0.0, 0.0, sem, len(names) * len(topo.engines(src, core)))
        ops[k]["link"], ops[k]["lane"] = [(src == nx2, "T" + s) for s in names], key

    win, win2 = T["win"], T["win2"]
    slot = lambda s, ww=win: ww[:, s * P:(s + 1) * P]
    res = lambda f: T["rs"][:, f * P:(f + 1) * P]

    def res2(f, rc):
        return slot(V0 - f + 1, win2) if f and f - 1 not in rc else T["rs2"][:, f * P:(f + 1) * P]

    def view_out(f, a, r):
        s, last = (V0 - f) * P, None
        if f - 1 not in theirs:
            for i, j in parts if f else whole:
                c0, c1 = CH[i][0], CH[j - 1][1]
                last = send(nxt, win[:, s + c0:s + c1], a[:, c0:c1], "arr%d" % f, r[i:j], "sA%d_%d" % (f, i), "ls%d" % f, last)
        if f in mine:
            last = send(nx2, slot(V0 - f, win2), a, "brr%d" % f, r, "sB%d" % f, "ls%d" % f, last)
        return last

    ctl, whole = T["ctl"], ((0, len(CH)),)
    dma("S", slot(SB + 2), T.pic0[:, P:2 * P], "dp1", w=("pic1",))
    dma("A", ctl[0:8, 0, 0:5], T.gaps[:], "dctl", w=("ctl0",))
    dma("S", ctl[0:8, 0, 5:10], T.cmd[:], "dctl", w=("ctl1",))
    dma("A", ctl[0:8, 0, 10:15], T.cmd[:], "dctl", w=("ctl2",))
    dma("S", ctl[0:8, 1, 0:15], T.rel[:], "dctl", w=("ctl3",))
    dma("A", T["lia"][:], T.ia[:], "da", w=("ia",), wide=2)
    dma("S", T["lib"][:], T.ib[:], "db", w=("ib",), wide=2)
    dma("A", T["lvy"][:], T.vy[:], "dvy", w=("vy",), wide=2)
    dma("S", T["lvx"][:], T.vx[:], "dvx", w=("vx",), wide=2)
    dma("A", slot(SB + 1), T.pic0[:, 0:P], "dp0", w=("pic0",))
    dma("S", res(0), T.res[:, 0:P], "dr0", w=("rs0",))
    early[0] = False
    gone = view_out(0, slot(SB + 2), ("pic1",))
    for f in range(1, F):
        dma("S", res(f), T.res[:, f * P:(f + 1) * P], "dr%d" % f, r=(gone,) if f >= CFG["late"] else (), w=("rs%d" % f,))
    for f in range(F):
        if f - 1 not in mine:
            arrive(prv, "arr%d" % f, "V%d" % f, ["sA%d_%d" % (f, i) for i, j in (parts if f else whole)])
        if f in mine:
            arrive(nx2, "brr%d" % f, "W%d" % f, ["sB%d" % f])
            arrive(prv, "rr%d" % f, "rs2_%d" % f, ["sr%d" % f])
            arrive(prv, "of%d" % f, "OF2_%d" % f, ["so%d" % f])
    if mine:
        arrive(prv, "pp", "pics2", ["sp"])
    if theirs:
        send(nxt, slot(SB + 1, win2), slot(SB + 1), "pp", ("pic0",), "sp")
    given = []

    def hand(kind, upto):
        for f in theirs:
            if f <= upto and (kind, f) not in given:
                given.append((kind, f))
                if kind == "r":
                    send(nxt, res2(f, theirs), res(f), "rr%d" % f, ("rs%d" % f,), "sr%d" % f)
                else:
                    send(nxt, T["OF2"][:, f, :], T["OFF"][:, f, :], "of%d" % f, ("OFF%d" % f,), "so%d" % f)

    hand("r", 1)

    cA, cB, col, cc, fr, Coef, Q, ZU = [T[s] for s in ("cA", "cB", "col", "cc", "fr", "Coef", "Q", "ZU")]
    small = {"allow_small_or_imprecise_dtypes": True}
    op("G", lambda e: e.iota(T["pi"][:, 0:1], [[1, 1]], 0, 1), w=("pi",), dur=200.0)
    op("G", lambda e: e.iota(cB[:], [[1, 8], [0, 16]], 0, 0, **small), w=("cB",), dur=400.0)
    op("G", lambda e: e.iota(cA[:], [[1, 128]], 0, -1, **small), w=("cA",), dur=400.0)
    op("G", lambda e: e.iota(fr[:], [[0, 5], [-1, 5]], -2, 0, **small), w=("fr",), dur=200.0)
    op("G", lambda e: e.iota(T["rw"][:, 0:15], [[1, 3], [3, 5]], 32, -1, **small), w=("rw0",), dur=170.0)
    op("G", lambda e: e.iota(T["rw"][:, 16:26], [[-5, 2], [1, 5]], 74, -1, **small), w=("rw1",), dur=160.0)
    op("G", lambda e: e.iota(T["ce"][:], [[-32, 2], [0, 10]], -16, 0, **small), w=("ce",), dur=180.0)
    pc_, gc_, lc_, lq_, hu_, hl_, hn_, lh_ = [col[:, i:i + 1] for i in range(8)]
    ts(T["pj"][:, 0:1], T["pi"][:, 0:1], 4, None, ALU.arith_shift_right, r=("pi",), w=("pj0",))
    ts(T["pj"][:, 1:2], T["pi"][:, 0:1], 15, None, ALU.bitwise_and, r=("pi",), w=("pj1",))
    cp(pc_, T["pi"][:, 0:1], r=("pi",), w=("p",))
    cp(col[:, 1:3], T["pj"][:, 0:2], r=("pj0", "pj1"), w=("g", "l"))
    act(lq_, lc_, ACT.Identity, ("l",), ("lq",), bias=-0.25)
    act(lh_, lc_, ACT.Identity, ("l",), ("lh",), bias=0.5, scale=0.5)
    ts(hu_, lc_, 0.5, None, ALU.mult, r=("l",), w=("hu",))
    ts(hl_, lc_, -0.5, 7.5, ALU.mult, ALU.add, r=("l",), w=("hl",))
    act(hn_, lc_, ACT.Identity, ("l",), ("hn",), bias=-7.5, scale=0.5)
    OO, NO, NU, NL, I16 = [T[s][:] for s in ("OO", "NO", "NU", "NL", "I16")]
    ts(T["E8"][0:8, :], cB[0:8], col[0:8, 0:1], None, ALU.is_equal, r=("cB", "p"), w=("E8",))
    ts(OO, cB[:], gc_, None, ALU.is_equal, r=("cB", "g"), w=("OO",))
    ts(NO, OO, -1.0, None, ALU.mult, r=("OO",), w=("NO",), k=0.5)
    act(T["tU"][:], cA[:], ACT.Abs, ("cA", "hu"), ("tU",), bias=hu_)
    act(T["tL"][:], cA[:], ACT.Abs, ("cA", "hn"), ("tL",), bias=hn_)
    ts(NU, T["tU"][:], hu_, -1.0, ALU.is_le, ALU.mult, r=("hu", "tU"), w=("NU",), k=0.5)
    ts(NL, T["tL"][:], hl_, -1.0, ALU.is_le, ALU.mult, r=("hl", "tL"), w=("NL",), k=0.5)
    Id, Ng = T["W2"][:, 0:128], T["N2"][:, 0:128]
    ts(Id, cA[:], 0.0, None, ALU.is_equal, r=("cA",), w=("I",))
    ts(T["W2"][:, 128:256], Id, 1.0, None, ALU.mult, r=("I",), w=("I2",), k=0.5)
    ts(T["N2"][:], T["W2"][:], -1.0, None, ALU.mult, r=("I", "I2"), w=("N",), k=0.5)
    ts(I16, Id, 16.0, None, ALU.mult, r=("I",), w=("I16",), k=0.5)
    N16 = T["N16"][:]
    ts(N16, Id, -16.0, None, ALU.mult, r=("I",), w=("N16",), k=0.5)
    act(T["I32i"][:], Id, ACT.Copy, ("I",), ("I32i",), scale=1.0 / 32)
    act(T["I512i"][:], Id, ACT.Copy, ("I",), ("I512i",), scale=1.0 / 512)
    act(cc[:], cA[:, 0:32], ACT.Identity, ("cA", "p"), ("cc",), bias=pc_)
    for i in range(2):
        act(T["K1"][:, 32 * i:32 * i + 32], cc[:], ACT.Identity, ("cc",), ("K1%d" % i,), bias=-0.25)
    act(T["K1"][:, 64:128], cA[:, 0:64], ACT.Identity, ("cA", "lq"), ("K12",), bias=lq_, scale=0.0)
    act(T["CL"][:, 0:6], cc[:, 0:6], ACT.Identity, ("cc", "l"), ("CL",), bias=lc_, scale=16.0)
    act(T["LK"][:, 0:1], lc_, ACT.Identity, ("l",), ("LK0",), bias=97.0)
    act(T["LK"][:, 1:25], fr[:, 1:25], ACT.Identity, ("fr", "l"), ("LK1",), bias=lc_)
    act(T["c21"][:], fr[:], ACT.Identity, ("fr",), ("c21",), bias=7.0)
    ts(Coef[:, 0:25], fr[:], pc_, -2.0, ALU.add, ALU.is_le, r=("fr", "p"), w=("Cf",))
    act(Coef[:, 25:50], Coef[:, 0:25], ACT.Copy, ("Cf",), ("Cs",), scale=-1.0)
    ts(Coef[32:64, 5:20], T["rw"][32:64, 0:15], 0.0, -1.0, ALU.is_equal, ALU.mult, r=("rw0", "Cs"), w=("Cr0",))
    ts(Coef[32:64, 0:5], T["rw"][32:64, 0:5], 0.0, -1.0, ALU.is_equal, ALU.mult, r=("rw0", "Cs"), w=("Cr1",))
    ts(Coef[64:96, 0:10], T["rw"][64:96, 16:26], 0.0, -99.0, ALU.is_equal, ALU.mult, r=("rw1", "Cs"), w=("Ci",))
    ms(Coef[64:65, 0:1], 99.0, ("Ci",))
    coef = ("Cf", "Cs", "Cr0", "Cr1", "Ci")
    ms(T["qm"][:], -0.25, ("qm",))
    ms(T["cK"][:, 0:32], 16.0, ("c16",))
    ms(T["cK"][:, 32:32 + CW], 128.0, ("c128",))
    ms(T["cM"][:], MAGIC, ("cM",))
    ms(T["cM2"][:], 16.0 * MAGIC, ("cM2",))
    ms(T["ctb"][0:8], 0.0, ("ctb",))
    ms(T["R"][:, 0:1], 1.0, ("R0",))
    ms(ZU[:, 1, 0:1], 0.0, ("LP0",))
    ms(Q[:, 0, 5:6], -1.0, ("bc",))
    ms(slot(SB), 128.0, ("blank",))
    ms(T["MS"][:, 0:3 * MW], 0.0, ("MS0",))
    ms(T["Pb"][:, :, 1, :], 0.0, ("Pz",))
    ts(Q[:, 8, 5:6], lc_, 2.0, lh_, ALU.is_lt, ALU.mult, r=("l", "lh"), w=("K",))
    ts(T["LP0"][:], OO, Q[:, 8, 5:6], 2.0, ALU.mult, ALU.mult, r=("OO", "K"), w=("LS0",), k=0.5)
    k = act(Q[:, 9, 0:5], T["cK"][:, 0:5], ACT.Exp, ("c16",), ("one",), scale=0.0, x=1400.0)
    ops[k]["order"] = lastdma["A"]
    if mine:
        if CFG["copies"][0] == "V":
            ms(slot(SB, win2), 128.0, ("blank2",))
        else:
            dma("S", slot(SB, win2), slot(SB), "dk", r=("blank",), w=("blank2",))
        if CFG["copies"][1] == "A":
            act(slot(SB + 2, win2), slot(V0), ACT.Copy, ("V0",), ("pics3",))
        elif CFG["copies"][1] == "V":
            ts(slot(SB + 2, win2), slot(V0), 1.0, None, ALU.mult, r=("V0",), w=("pics3",), k=0.5)
        else:
            dma("S", slot(SB + 2, win2), slot(V0), "ds1", r=("V0",), w=("pics3",))
        spare = [j for j in range(max(mine)) if j not in mine and j + 1 not in mine]
        for j in spare:
            ms(slot(V0 - j, win2), 0.0, ("spare%d" % j,))

    X0, X1, X2, C0, C1, C2, P1, AD = [T[s] for s in ("X0", "X1", "X2", "C0", "C1", "C2", "P1", "AD")]
    R, SS, sc, ctb = T["R"], T["SS"], T["sc"], T["ctb"]
    ck = ("ctl0", "ctl1", "ctl2", "ctl3")
    cp(ctb[0:8, 0:2, 0:15], ctl[0:8, :, 0:15], r=ck + ("ctb",), w=("ct0",))
    tt(ctb[0:8, 2, 0:15], ctl[0:8, 0, 0:15], cB[0:8, 0:3, 0:5], ALU.not_equal, r=ck + ("ctb", "cB"), w=("ct1",))
    mm(X0[0:96, 0:128], ctb[0:8], T["E8"][0:8, :], ("ct0", "ct1", "E8"), ("T1",), "X0", True, True)
    act(T["Tb"][0:96, :], X0[0:96, 0:128], ACT.Copy, ("T1",), ("Tb",), ("X0",))
    mm(X1[:, 0:25], T["Tb"][0:96, :], Coef[0:96, 0:25], ("Tb",) + coef, ("TG",), "X1", True, True)
    mm(X2[:, 0:25], T["Tb"][0:96, :], Coef[0:96, 25:50], ("Tb",) + coef, ("S",), "X2", True)
    mm(X2[:, 0:25], Id, T["c21"][:], ("I", "c21"), ("S",), "X2")
    one = Q[:, 9, 0:5]
    for j, m in ((2, I16), (0, N16), (4, N16), (0, N16), (4, N16)):
        mm(X2[:, 5 * j:5 * j + 5], m, one, ("I16", "N16", "one"), ("S",), "X2")
    lk = ("TG", "LK0", "LK1")
    tt(Q[:, 1:5, 0:5], X1[:, 0:20], T["LK"][:, 0:20], ALU.not_equal, r=lk, w=("NE",), banks=("X1",))
    tt(Q[:, 0, 0:5], X1[:, 20:25], T["LK"][:, 20:25], ALU.is_gt, r=lk, w=("born",), banks=("X1",))
    tt(Q[:, 5:9, 0:5], X1[:, 5:25], T["LK"][:, 5:25], ALU.is_equal, r=lk, w=("OH",), banks=("X1",))
    tt(Q[:, 17, 0:5], Q[:, 3, 0:5], Q[:, 4, 0:5], ALU.mult, r=("NE",), w=("nm",))
    tt(Q[:, 13, 0:5], Q[:, 5, 0:5], Q[:, 17, 0:5], ALU.mult, r=("OH", "nm"), w=("um",))
    op("V", lambda e: e.tensor_tensor_scan(R[:, 1:6], Q[:, 2, 0:5], Q[:, 1, 0:5], 1.0, ALU.mult, ALU.mult), ("NE",), ("R",))
    ts(ZU[:, 2, 0:1], Q[:, 0, 0:1], Q[:, 1, 0:1], None, ALU.mult, r=("NE", "born"), w=("h0",))
    ts(ZU[:, 5, 0:1], Q[:, 5, 0:1], Q[:, 3, 0:1], Q[:, 4, 0:1], ALU.mult, ALU.mult, r=("NE", "OH"), w=("u0",))
    ts(ZU[:, 4, 0:1], Q[:, 2, 0:1], Q[:, 3, 0:1], Q[:, 4, 0:1], ALU.mult, ALU.mult, r=("NE",), w=("t0",))
    ts(ZU[:, 6, 0:1], ZU[:, 4, 0:1], ZU[:, 2, 0:1], None, ALU.mult, r=("h0", "t0"), w=("g0",))

    def places(nf, held, g0, g1, wts, name):
        e = [C1[:, 5 * i:5 * i + nf] for i in range(4)]
        terms = [(2, Ng, Q[:, 9, 0:nf], ("N", "one")), (3, I16, Q[:, 9, 0:nf], "one"),
                 (2, I16, Q[:, 6, 0:nf], "OH"), (2, I16, Q[:, 4, 0:nf], "NE"), (3, I16, Q[:, 7, 0:nf], "OH")]
        for j in reversed(range(len(held))):
            terms += [(i, m) + held[j] for i, m in ((0, OO), (1, OO), (2, OO), (2, I16), (3, I16))]
            terms += [(i, m) + g1[j] for i, m in ((0, NO), (1, NU), (1, I16), (2, NO))]
        terms += [(i, m) + g0 for i, m in ((0, NL), (0, I16), (2, NO))]
        mm(C1[:, 0:20], Id, T["ce"][:], ("I", "ce", "OO", "NO", "NU", "NL", "I16"), ("ex",), "C1", True)
        for j, (i, m, x, key) in enumerate(terms):
            mm(e[i], m, x, key if isinstance(key, tuple) else (key,), ("ex",), "C1", False, j + 1 == len(terms))
        act(wts, C1[:, 0:20] if nf > 1 else C1[:, 0:20:5], ACT.Exp, ("ex", "one"), (name,), ("C1",), scale=LN8)

    places(1, [(ZU[:, 2, 0:1], "h0")], (ZU[:, 6, 0:1], "g0"), [(ZU[:, 5, 0:1], "u0")], T["wts0"][:], "wts0")
    for s in range(4):
        mm(AD[:, 64:65], T["LP0"][:], T["wts0"][:, s:s + 1], ("LS0", "wts0"), ("pack0",), "AD", s == 0, s == 3)

    for j in (0, 4, 0, 4):
        mm(X2[:, 5 * j:5 * j + 5], I16, Q[:, 0, 0:5], ("born",), ("S",), "X2")
    for j in range(5):
        mm(X2[:, 5 * j:5 * j + 5], NU, R[:, 0:5], ("NU", "R", "R0"), ("S",), "X2")
    for j, i in ((0, 0), (1, 0), (3, 0), (4, 1)):
        mm(X2[:, 5 * j:5 * j + 5], I16, R[:, i:i + 5], (), ("S",), "X2", False, j == 4)
    tt(SS[:], X2[:, 0:25], Q[:, 1:18:4, 0:5], ALU.mult, r=("S", "NE", "OH", "one", "nm", "um"), w=("SS",), banks=("X2",))
    act(ZU[:, 0, 0:6], Q[:, 0, 0:6], ACT.Identity, ("born", "bc"), ("nb",), bias=1.0, scale=-1.0, acc=sc[:, 1:2])
    act(T["jk"][:, 0:6], Q[:, 8, 0:6], ACT.Identity, ("OH", "K"), ("isF",), acc=sc[:, 0:1])
    ts(T["LPh"][:], OO, sc[:, 0:1], sc[:, 1:2], ALU.mult, ALU.mult, r=("OO", "nb", "isF"), w=("LS",), k=0.5)
    mm(C0[:, 1:2], OO, Q[:, 5, 0:1], ("OO", "OH"), ("L1",), "C0", True, True)
    ts(ZU[:, 1, 1:2], Q[:, 5, 0:1], Q[:, 1, 1:2], None, ALU.mult, r=("OH", "NE"), w=("LP1",))
    for f in range(1, F):
        ts(ZU[:, 2:7, f], SS[:, :, f], C0[:, f:f + 1], None, ALU.is_gt, r=("SS", "L%d" % f), w=("Z%d" % f,), banks=("C0",))
        if f + 1 < F:
            for j, (m, x, r) in enumerate(((I16, Q[:, 9, 0:1], "one"), (OO, ZU[:, 1, f:f + 1], "LP%d" % f),
                                           (OO, ZU[:, 3, f:f + 1], "Z%d" % f), (N16, ZU[:, 4, f:f + 1], "N16"))):
                mm(C0[:, f + 1:f + 2], m, x, (r,), ("L%d" % (f + 1),), "C0", j == 0, j == 3)
            ts(ZU[:, 1, f + 1:f + 2], ZU[:, 1, f:f + 1], ZU[:, 3, f:f + 1], Q[:, 1, f + 1:f + 2], ALU.add, ALU.mult,
               r=("LP%d" % f, "Z%d" % f, "NE"), w=("LP%d" % (f + 1),))
    allz, alll = ("h0", "u0", "g0") + tuple("Z%d" % f for f in range(1, F)), tuple("LP%d" % f for f in range(F))
    if CFG["quick"]:
        tt(Q[:, 18, 4:5], Q[:, 1, 4:5], Q[:, 17, 4:5], ALU.mult, r=("NE", "nm"), w=("nn",))
        tt(T["LN"][:, 0:4], ZU[:, 1, 0:4], Q[:, 17, 0:4], ALU.mult, r=alll[:4] + ("nm",), w=("LN0",))
        ts(T["LN"][:, 4:5], ZU[:, 1, 3:4], ZU[:, 3, 3:4], Q[:, 18, 4:5], ALU.add, ALU.mult, r=("LP3", "Z3", "nn"), w=("LN1",))
    else:
        tt(T["LN"][:, 0:5], ZU[:, 1, 0:5], Q[:, 17, 0:5], ALU.mult, r=alll + ("nm",), w=("LN0", "LN1"))
    act(T["jk"][:, 8:23], ZU[:, 0:3, 0:5], ACT.Identity, allz + alll + ("nb",), ("E",), acc=sc[:, 2:3])
    ts(T["LE"][:], OO, sc[:, 2:3], None, ALU.mult, r=("OO", "E"), w=("LE",), k=0.5)

    IX, VN, D3, vw, ND = T["IX"], T["VN"], T["D3"], T["vw"], C2[:, 256:416]
    ts(ND, T["lia"][:], 7.0, None, ALU.is_lt, r=("ia",), w=("ND",), banks=("C2",))
    tt(IX[:, :, 0, :], T["lia"][:], ND, ALU.mult, r=("ND",), w=("ix0",), banks=("C2",))
    tt(IX[:, :, 1, :], T["lib"][:], ND, ALU.mult, r=("ib", "ND"), w=("ix1",), banks=("C2",))
    for i in range(2):
        tt(VN[:, :, i, :], T["lvy"][:, :, i, :], ND, ALU.mult, r=("vy", "ND"), w=("VN%d" % i,), banks=("C2",))
        tt(VN[:, :, 2 + i, :], T["lvx"][:, :, i, :], ND, ALU.mult, r=("vx", "ND"), w=("VN%d" % (2 + i),), banks=("C2",))
    vn = ("VN0", "VN1", "VN2", "VN3")
    ts(D3[:, 1:F, 0:32], T["lia"][:, 1:F], 7.0, None, ALU.is_ge, r=("ia",), w=("D0",))
    for j in (1, 2):
        if CFG["halves"] == "V":
            ts(D3[:, 1:F, 32 * j:32 * j + 32], D3[:, 1:F, 0:32], 0.5, None, ALU.mult, r=("D0",), w=("D%d" % j,), k=0.5)
        else:
            act(D3[:, 1:F, 32 * j:32 * j + 32], D3[:, 1:F, 0:32], ACT.Copy, ("D0",), ("D%d" % j,), scale=0.5)
    act(T["mx"][:], IX[:, :, 1, :], ACT.Abs, ("ix1",), ("mx",), bias=-2.0, scale=2.0)
    if CFG["sign"] == "V":
        ts(T["e1"][:], IX[:, :, 1, :], 2.0, 2.0, ALU.is_ge, ALU.mult, r=("ix1",), w=("e1",), k=0.5)
    else:
        act(T["e1"][:], IX[:, :, 1, :], ACT.Sign, ("ix1",), ("e1",), bias=-1.5)
    mm(P1[:, 256:416], Id, T["mx"][:], ("I", "mx"), ("ib1",), "P1", True)
    mm(P1[:, 256:416], Id, T["e1"][:], ("e1",), ("ib1",), "P1", False, True)
    act(T["w"][:, :, 0, :], IX[:, :, 0, :], ACT.Exp, ("ix0", "one"), ("w0",), scale=-LN8)
    act(T["w"][:, :, 1, :], P1[:, 256:416], ACT.Exp, ("ib1", "one"), ("w1",), ("P1",), scale=-LN8 / 2, bias=0.0 if CFG["sign"] == "V" else -LN8 / 2)
    for f in range(F):
        act(vw[:, f], IX[:, f], ACT.Relu, ("ix0", "ix1"), ("vw%d" % f,), bias=-5.0 * (f + 1), scale=f + 1.0)

    MS, OFF, ML, RC, Pb, Eb, h = [T[s] for s in ("MS", "OFF", "ML", "RC", "Pb", "Eb", "h")]

    def slots(f, pack, key, bank):
        s = "%d" % f
        ts(T["Yp"][:, f], T["w"][:, f], pack, -0.4375, ALU.mult, ALU.add, r=("w0", "w1", key), w=("Yp" + s,), banks=(bank,))
        ts(T["Bp"][:, f], T["Yp"][:, f], 7, None, ALU.bitwise_and, r=("Yp" + s,), w=("Bp" + s,))
        cp(Pb[:, f, 0:3:2, :], T["Bp"][:, f], r=("Bp" + s,), w=("Pb" + s,))

    def lasts(f0, f1):
        for f in range(f0, f1):
            ts(T["Ye"][:, f], T["w"][:, f, 0, :], C2[:, 8 + f:9 + f], -0.4375, ALU.mult, ALU.add, r=("w0", "packE"), w=("Ye%d" % f,), banks=("C2",))
        ts(T["Be"][:, f0:f1], T["Ye"][:, f0:f1], 7, None, ALU.bitwise_and, r=tuple("Ye%d" % f for f in range(f0, f1)), w=("Be%d" % f0,))
        cp(Eb[:, f0:f1], T["Be"][:, f0:f1], r=("Be%d" % f0,), w=tuple("Eb%d" % f for f in range(f0, f1)))

    def addresses(f):
        s = "%d" % f
        m0 = (3 + f) * MW
        c0 = 0 if 0 < f < F - 1 else 32
        lo = 0 if f else 32
        mm(P1[:, lo:160], Id, T["cK"][:, c0:c0 + 160 - lo], ("I", "c16", "c128"), ("P1",), "P1", True)
        mm(P1[:, 32:160], Id, T["K1"][:], ("K10", "K11", "K12"), ("P1",), "P1")
        mm(P1[:, 32:160], Id, VN[:, f], vn, ("P1",), "P1", False, f == 0)
        if f:
            mk = tuple("MS%d%s" % (j, u) for j in range(1, f + 1) for u in "ab") + ("MS0", "ML" + s, "D0", "D1", "D2")
            tt(h[:, f], MS[:, 0:m0].indirect(ML[:, f, 0:6]), D3[:, f], ALU.mult, r=mk, w=("h" + s,), k=1.56, x=50.0)
            act(T["t"][:, f], h[:, f, 0:32], ACT.Relu, ("h" + s,), ("t" + s,), bias=-128.0 * (16 * (f + 2) - 1), scale=128.0)
            mm(P1[:, 0:32], Ng, vw[:, f, 0, :], ("N", "vw" + s), ("P1",), "P1")
            mm(P1[:, 0:32], Id, Pb[:, f, 0, :], ("Pb" + s,), ("P1",), "P1")
            if f + 1 < F:
                mm(P1[:, 0:32], I16, Eb[:, f], ("Eb" + s,), ("P1",), "P1")
            for j in range(4):
                mm(P1[:, 32 + 32 * j:64 + 32 * j], Ng if j % 2 else Id, h[:, f, 32 + 32 * (j // 2):64 + 32 * (j // 2)], ("h" + s,), ("P1",), "P1")
            mm(P1[:, 0:32], Ng, T["t"][:, f], ("t" + s,), ("P1",), "P1", False, True)
            tt(MS[:, m0:m0 + 32], P1[:, 0:32], h[:, f, 0:32], ALU.max, r=("P1", "h" + s), w=("MS%da" % (f + 1),), banks=("P1",))
        for i, hi in ((0, 159.0), (1, 143.0)):
            ts(RC[:, f, 64 * i:64 * i + 64], P1[:, 32 + 64 * i:96 + 64 * i], 128.0, hi, ALU.max, ALU.min, r=("P1",), w=("RC%d%s" % (i, s),), banks=("P1",))
        if f == 0:
            act(MS[:, m0 + 32:m0 + MW], VN[:, 0, 0:3:2, :], ACT.Copy, vn, ("MS1b",))
        elif f + 1 < F:
            mm(C0[:, 0:64], Id, T["qm"][:, 0:64], ("qm",), ("PU",), "C0", True)
            for i in range(2):
                mm(C0[:, 32 * i:32 * i + 32], Id, VN[:, f, 2 * i, :], vn, ("PU",), "C0")
            mm(C0[:, 0:64], Id, h[:, f, 32:96], ("h" + s,), ("PU",), "C0")
            mm(C0[:, 0:64], Id, T["cM"][:, 0:64], ("cM",), ("PU",), "C0")
            mm(C0[:, 0:64], Ng, T["cM"][:, 0:64], (), ("PU",), "C0", False, True)
            act(MS[:, m0 + 32:m0 + MW], C0[:, 0:64], ACT.Copy, ("PU",), ("MS%db" % (f + 1),), ("C0",))
        mm(AD[:, 0:64], Id, Pb[:, f, 1:3, :], ("Pz", "Pb" + s), ("AD",), "AD", True)
        mm(AD[:, 32:64], Ng, vw[:, f, 1, :], ("N", "vw" + s), ("AD",), "AD")
        if f:
            cn = MS[:, m0:m0 + 32]
            for m, x in ((Ng, cn), (Id, T["cM2"][:]), (Ng, T["cM2"][:]), (Id, cn)):
                mm(AD[:, 0:32], m, x, ("MS%da" % (f + 1), "cM2"), ("AD",), "AD")
        else:
            mm(AD[:, 0:32], Id, Pb[:, f, 0, :], (), ("AD",), "AD")
            mm(AD[:, 0:32], Ng, vw[:, f, 0, :], (), ("AD",), "AD")
        mm(AD[:, 0:64], T["I32i"][:], RC[:, f, 0:64], ("I32i", "RC0" + s), ("AD",), "AD")
        mm(AD[:, 0:64], T["I512i"][:], RC[:, f, 64:128], ("I512i", "RC1" + s), ("AD",), "AD", False, True)
        ts(OFF[:, f, :], AD[:, 0:64], 512.0, 512.0 * (f + 1) - 2176.0, ALU.mult, ALU.add, r=("AD",), w=("OFF" + s,), banks=("AD",))

    slots(0, AD[:, 64:65], "pack0", "AD")
    addresses(0)
    places(F, [(ZU[:, 2, 0:5], allz), (ZU[:, 1, 0:5], alll)], (ZU[:, 6, 0:5], allz), [(ZU[:, 5, 0:5], allz), (T["LN"][:, 0:5], ("LN0", "LN1"))],
           T["wts"][:], "wts")
    ts(T["eq"][:], T["wts"][:, 0:3], 8.0, float(MW), ALU.is_equal, ALU.mult, r=("wts",), w=("eq",))
    for bank, c0, l, x, m, r, name in (("C2", 8, "LE", "wts", 4, "LE", "packE"), ("C2", 0, "LPh", "wts", 4, "LS", "pack"),
                                       ("C0", 256, "LPh", "eq", 3, "LS", "packM")):
        for s in range(m):
            mm(T[bank][:, c0:c0 + 5], T[l][:], T[x][:, s, :], (r, x), (name,), bank, s == 0, s + 1 == m)
    for f in range(1, F):
        ts(ML[:, f, 0:6], T["CL"][:, 0:6], C0[:, 256 + f:257 + f], None, ALU.add, r=("CL", "packM"), w=("ML%d" % f,), banks=("C0",))
    mm(P1[:, 0:32], Id, T["cK"][:, 0:32], ("c16",), ("P1",), "P1", True)
    mm(P1[:, 0:32], Id, Pb[:, 0, 0, :], ("Pb0",), ("P1",), "P1", False, True)
    ts(T["Ye"][:, 0], T["w"][:, 0, 0, :], C2[:, 8:9], 16.0, ALU.mult, ALU.mult, r=("w0", "packE"), w=("Ye0",), banks=("C2",))
    ts(T["Be"][:, 0], T["Ye"][:, 0], 7 * 16, None, ALU.bitwise_and, r=("Ye0",), w=("Be0",))
    tt(MS[:, 3 * MW:3 * MW + 32], P1[:, 0:32], T["Be"][:, 0], ALU.add, r=("P1", "Be0"), w=("MS1a",), banks=("P1",))
    lasts(1, 2)
    for f in range(1, F):
        slots(f, C2[:, f:f + 1], "pack", "C2")
        if f == 2:
            lasts(2, 4)
        addresses(f)

    nch = range(len(CH))
    have = {True: ["blank", "pic0", "pic1", "V0"], False: ["blank2", "pics2", "pics3"]}
    turns, held_back, stores, gathers = [0], [], [], []

    def pixels(f, own):
        s = "%d" % f
        end = f + 1 == F
        turn = not end and (not own or f not in theirs or f + 1 in mine)
        sh = 16 * (f + 1) if turn else 0
        rot, nrot = T["W2"][:, sh:sh + 128], T["N2"][:, sh:sh + 128]
        if own:
            ww, off, rs, rk, wk = win, OFF, res(f), "rs" + s, ["OFF" + s]
        else:
            ww, off, rs, rk = win2, T["OF2"], res2(f, mine), "rs2_" + s
            wk = ["OF2_" + s] + [u % j for j in mine if j <= f for u in ("W%d", "rs2_%d")] + ["spare%d" % j for j in spare]
        wk = tuple(wk + have[own])
        ww = ww[:, (V0 - f) * P:(SB + 3 + f) * P]
        z = turns[0] % 2
        turns[0] += 1
        gp, gq = T["gp"][:, z], T["gq"][:, z]
        sums = []
        for c, (a, b) in enumerate(CH):
            xb, x0 = ("X%d" % c, 0) if own or not held_back else CFG["pair"][f][c]
            X, xk = T[xb][:, x0:x0 + b - a], xb + "%d" % x0
            sums.append((X, xb, xk))
            mm(X, rot, rs[:, a:b], ("I", "I2", rk), (xk,), xb, True)
            mm(X, Id, T["qm"][:, 0:b - a], ("qm",), (xk,), xb)
            if end and CFG["end"][c] == "V":
                mm(X, Id, T["cK"][:, 32:32 + b - a], ("c128",), (xk,), xb)
        for c, (a, b) in enumerate(CH):
            i = ts(gp[:, a:b], ww.indirect(off[:, f, a // 16:b // 16]), 255.0, 0.5, ALU.min, ALU.mult, r=wk, w=("gp%d%d" % (z, c),), k=1.56, x=50.0)
            j = act(gq[:, a:b], ww.indirect(off[:, f, 32 + a // 16:32 + b // 16]), ACT.Relu, wk, ("gq%d%d" % (z, c),), bias=127.5, scale=-0.5, k=1.56, x=65.0)
            if gathers:
                ops[i]["order"], ops[j]["order"] = gathers
            gathers[:] = [i, j]
        if end or (own and turn):
            dst, name = T["snd"][:, f * P:(f + 1) * P], "snd"
        elif own:
            dst, name = slot(SB + 3 + f), "F"
        else:
            dst, name = slot(V0 - f - 1), "Vl"
        sk = tuple("%s%s_%d" % (name, s, j) for j in nch)

        def finish(c):
            (X, xb, xk), (a, b) = sums[c], CH[c]
            o, ok = dst[:, a:b], sk[c:c + 1]
            if end and CFG["end"][c] == "V":
                ts(o, X, 0.0, 255.0, ALU.max, ALU.min, r=(xk,), w=ok, banks=(xb,))
            elif end:
                act(T["tb"][:, a:b], X, ACT.Relu, (xk,), ("last%d" % c,), (xb,), bias=128.0 - MAGIC)
                ts(o, T["tb"][:, a:b], 255.0, None, ALU.min, r=("last%d" % c,), w=ok, k=0.5)
            elif CFG["finish"].get((f, own), "AAA")[c] == "V":
                ts(o, X, 128.0 - MAGIC, 0.0, ALU.add, ALU.max, r=(xk,), w=ok, banks=(xb,))
            else:
                act(o, X, ACT.Relu, (xk,), ok, (xb,), bias=128.0 - MAGIC)
            if end:
                dma("A" if c + 1 == len(CH) else "S", T.y[:, f * P + a:f * P + b], o, "dy", r=ok)

        ys = T.y[:, f * P:(f + 1) * P]

        def store():
            o = T["tb"][:, f * P:(f + 1) * P]
            for c, (a, b) in enumerate(CH):
                ts(o[:, a:b], dst[:, a:b], 255.0, None, ALU.min, r=sk[c:c + 1], w=("yc%s%d" % (s, c),), k=0.5)
            dma("S", ys, o, "dy", r=tuple("yc%s%d" % (s, c) for c in nch))

        wait = own and not turn and f in mine and CFG["pair"]
        for c, (a, b) in enumerate(CH):
            X, xb, xk = sums[c]
            both = end and CFG["end"][c] == "V"
            mm(X, rot, gp[:, a:b], ("gp%d%d" % (z, c),), (xk,), xb)
            mm(X, nrot, gq[:, a:b], ("N", "gq%d%d" % (z, c)), (xk,), xb)
            mm(X, Id, T["cM"][:, 0:b - a], ("cM",), (xk,), xb, False, not both)
            if both:
                mm(X, Ng, T["cM"][:, 0:b - a], (), (xk,), xb, False, True)
            if wait:
                held_back.append(finish)
                continue
            finish(c)
            if held_back:
                held_back.pop()(c)
        if end:
            return
        if not own:
            have[True].extend(sk)
            if stores:
                stores.pop()()
            turn_back(f, sk)
            return
        if f not in mine:
            have[True].append("V%d" % (f + 1))
        if not turn:
            have[True].extend(sk)
            if wait:
                stores.append(store)
            else:
                store()
            return
        if f and CFG["ahead"]:
            hand("o", f + 1)
        gone = view_out(f + 1, dst, sk)
        hand("o", f + 1)
        hand("r", f + 3)
        mm(C1[:], T["W2"][:, 128 - sh:256 - sh], dst, sk, ("UN",), "C1", True, True)
        ts(slot(SB + 3 + f), C1[:], 255.0, None, ALU.min, r=("UN",), w=("F" + s,), banks=("C1",))
        have[True].append("F" + s)
        dma("S", ys, slot(SB + 3 + f), "dy", r=("F" + s, gone))

    def turn_back(f, keys):
        if mine and f < max(mine):
            sh = 16 * (f + 1)
            halves = (("A", 0, P, "C1"),) if f in mine or not CFG["split"] else (("A", 0, P // 2, "C1"), ("V", P // 2, P, "C2"))
            for who, a, b, bank in halves:
                x, o, key = T[bank][:, 0:b - a], slot(SB + 3 + f, win2)[:, a:b], "G%d%s" % (f, who)
                mm(x, T["W2"][:, 128 - sh:256 - sh], slot(V0 - f - 1)[:, a:b], keys, ("UN" + who,), bank, True, True)
                if who == "A":
                    act(o, x, ACT.Copy, ("UN" + who,), (key,), (bank,))
                else:
                    cp(o, x, ("UN" + who,), (key,), (bank,))
                have[False].append(key)

    for f in range(F):
        hand("o", f)
        hand("r", f + 1)
        pixels(f, True)
        if f in mine:
            pixels(f, False)
        elif f + 1 < F:
            turn_back(f, ("V%d" % (f + 1),))
    return ops


def plan(ops):
    n = len(ops)
    pre = [o["deps"] | o["soft"] | ({o["order"]} if "order" in o else set()) for o in ops]
    suc = [[] for _ in ops]
    for k in range(n):
        for d in pre[k]:
            suc[d].append(k)

    def gap(d, k):
        if (ops[d]["q"] == "P" and ops[k]["q"] == "P") or (d == ops[k].get("order") and d not in ops[k]["deps"]):
            return 0.0
        return ops[k]["after"] if "after" in ops[k] else ops[d]["lat"] + (0.0 if ops[k]["q"] == "X" else CFG["hop"])

    def sweep(prio, before, after, rev):
        start, busy = [0.0] * n, {}
        left = [len(b) for b in before]
        ready = [(prio[k], k) for k in range(n) if not left[k]]
        while ready:
            top = min(ready)
            ready.remove(top)
            k = top[1]
            for s in after[k]:
                left[s] -= 1
                if not left[s]:
                    ready.append((prio[s], s))
            t = ops[k]["lat"] if rev else 0.0
            for d in before[k]:
                t = max(t, start[d] + ops[d]["dur"] + (gap(k, d) if rev else gap(d, k)))
            iv = busy.setdefault(ops[k]["lane"], [])
            for a, b in iv:
                if t + ops[k]["dur"] <= a:
                    break
                t = max(t, b)
            start[k] = t
            iv.append((t, t + ops[k]["dur"]))
            iv.sort()
        return start

    end = lambda st: max(st[k] + ops[k]["dur"] + ops[k]["lat"] for k in range(n))
    rk, seed = [0.0] * n, [12345]
    left = [len(s) for s in suc]
    todo = [k for k in range(n) if not left[k]]
    while todo:
        k = todo.pop()
        rk[k] = ops[k]["dur"] + max([gap(k, s) + rk[s] for s in suc[k]] + [ops[k]["lat"]])
        for d in pre[k]:
            left[d] -= 1
            if not left[d]:
                todo.append(d)

    def jit(a):
        seed[0] = (seed[0] * 1103515245 + 12345) % 2147483648
        return a * seed[0] / 2147483648.0

    start = sweep([-r for r in rk], pre, suc, False)
    best = (end(start), start)
    for it in range(CFG["sweeps"]):
        a, start = 400.0 * (it % 3 > 0), best[1]
        back = sweep([jit(a) - start[j] - ops[j]["dur"] for j in range(n)], suc, pre, True)
        start = sweep([jit(a) - back[j] - ops[j]["dur"] for j in range(n)], pre, suc, False)
        if end(start) < best[0]:
            best = (end(start), start)
    start = best[1]
    return polish(ops, pre, suc, gap, sorted(range(n), key=lambda j: (start[j], j)), jit)


def polish(ops, pre, suc, gap, seq, jit):
    n, hop = len(ops), CFG["hop"]
    lanes = {}
    lane = [lanes.setdefault(o["lane"], len(lanes)) for o in ops]
    up = [0] * n
    for k in seq:
        for d in pre[k]:
            up[k] |= up[d] | 1 << d
    near = [[d for d in pre[k] if ops[d]["lat"] or not any(up[e] >> d & 1 for e in pre[k])] for k in range(n)]
    cases = []
    for speed, wait, link in CFG["cases"]:
        dur = [o["dur"] * (speed if o["q"] in "VAP" else link if o["q"] == "X" else 1.0) for o in ops]
        edges = []
        for k in range(n):
            e = []
            for d in near[k]:
                g0 = gap(d, k)
                e.append((d, g0 - hop + wait if g0 and ops[k]["q"] != "X" else g0))
            edges.append(e)
        cases.append((dur, edges))
    tail = [o["lat"] for o in ops]
    marks = [k for k in range(n) if ops[k].get("mark")]

    sinks = [k for k in range(n) if not suc[k]]
    weight = [(j, ops[j]["mark"]) for j in marks]

    def run(seq, case, i=0, old=None):
        dur, edges = case
        end, why = (old[1][:], old[2][:]) if old else ([0.0] * n, [-1] * n)
        free, last = [0.0] * len(lanes), [-1] * len(lanes)
        for k in seq[max(0, i - 160):i] if old else ():
            free[lane[k]], last[lane[k]] = end[k], k
        for k in seq[i:]:
            l = lane[k]
            t, w = free[l], last[l]
            for d, g0 in edges[k]:
                if end[d] + g0 >= t:
                    t, w = end[d] + g0, d
            end[k] = free[l] = t + dur[k]
            why[k], last[l] = w, k
        k = max(sinks, key=lambda j: end[j] + tail[j])
        return end[k] + tail[k] + sum(end[j] * m for j, m in weight), end, why, k

    now = [run(seq, c) for c in cases]
    best = (sum(r[0] for r in now), seq)
    for it in range(CFG["polish"]):
        _, end, why, k = now[it % len(cases)]
        if it % 5 > 1:
            k = marks[int(jit(len(marks)))]
        pairs = []
        while why[k] >= 0:
            if lane[why[k]] == lane[k] and not up[k] >> why[k] & 1:
                pairs.append((why[k], k))
            k = why[k]
        if not pairs:
            continue
        u, k = pairs[int(jit(len(pairs)))]
        i, j = seq.index(u), seq.index(k)
        mid = seq[i + 1:j]
        how = jit(1.0)
        if how < 0.35:
            new = seq[:i] + [x for x in mid if up[k] >> x & 1] + [k, u] + [x for x in mid if not up[k] >> x & 1] + seq[j + 1:]
        elif how < 0.7:
            new = seq[:i] + [x for x in mid if not up[x] >> u & 1] + [k, u] + [x for x in mid if up[x] >> u & 1] + seq[j + 1:]
        elif how < 0.85:
            j = min(n, j + 1 + int(jit(jit(500))))
            mid = seq[i + 1:j]
            new = seq[:i] + [x for x in mid if not up[x] >> u & 1] + [u] + [x for x in mid if up[x] >> u & 1] + seq[j:]
        else:
            j, i = i, max(0, i - 1 - int(jit(jit(500))))
            mid = seq[i:j]
            new = seq[:i] + [x for x in mid if up[u] >> x & 1] + [u] + [x for x in mid if not up[u] >> x & 1] + seq[j + 1:]
        got = [run(new, c, i, o) for c, o in zip(cases, now)]
        a, b = sum(r[0] for r in got), sum(r[0] for r in now)
        if a <= b + jit(CFG["heat"] * (1.0 - it / CFG["polish"])):
            seq, now = new, got
            if a < best[0]:
                best = (a, new)
            if it % 16 == 0:
                dur, end = cases[0][0], now[0][1]
                place = {x: i for i, x in enumerate(seq)}
                seq = sorted(seq, key=lambda x: (end[x] - dur[x], place[x]))
    end = run(best[1], cases[0])[1]
    return best[1], [end[k] - cases[0][0][k] for k in range(n)]


def rank_program(g, core, T, topo):
    if T.rank_of(core) is None:
        return
    ops = build(T, topo, core)
    order = joint(T, topo)[T.cores[T.rank_of(core) - 1] in topo.cores_of(core)]
    eng = {"V": g.vector, "A": g.scalar, "P": g.tensor, "G": g, "S": g.sync}
    total, many = {}, {}
    for o in ops:
        if o["sem"]:
            total[o["sem"]] = total.get(o["sem"], 0) + o["inc"]
            many[o["sem"]] = many.get(o["sem"], 0) + 1
    pos, cnt = {}, {}
    for k in order:
        q = ops[k]["q"]
        if not ops[k]["sem"]:
            cnt[q] = cnt.get(q, 0) + 1
            pos[k] = cnt[q]
    known, clock, waits = {}, {}, {}
    for k in order:
        o = ops[k]
        q = o["q"]
        if q == "X":
            clock[k] = {}
            continue
        kn = known.setdefault(q, {})
        need = []
        for d in sorted(o["deps"], key=lambda j: -pos.get(j, 0)):
            dq, ds = ops[d]["q"], ops[d]["sem"]
            if dq == "P" and q == "P":
                continue
            key, val = (ds, 1) if ds else ("n" + dq, pos[d])
            if kn.get(key, 0) >= val:
                continue
            need.append(d)
            kn[key] = val
            if not ds or many[ds] == 1:
                for kk, vv in clock[d].items():
                    kn[kk] = max(kn.get(kk, 0), vv)
        waits[k] = need
        clock[k] = dict(kn)
    signal = set(d for k in waits for d in waits[k] if not ops[d]["sem"])
    val, cnt = {}, {}
    for k in order:
        if k in signal:
            q = ops[k]["q"]
            cnt[q] = cnt.get(q, 0) + 1
            val[k] = cnt[q]
    waited = set()
    for k in order:
        o = ops[k]
        if o["q"] == "X":
            continue
        e = eng[o["q"]]
        for d in waits[k]:
            ds = ops[d]["sem"]
            if ds:
                e.wait_ge(T.sem[ds], total[ds])
                waited.add(ds)
            else:
                e.wait_ge(T.sem["n" + ops[d]["q"]], val[d])
        ins = o["fn"](e)
        if k in signal:
            ins.then_inc(T.sem["n" + o["q"]], 1)
        elif o["sem"] and o["q"] != "G":
            ins.then_inc(T.sem[o["sem"]], 16)
    for s in sorted(total):
        if s not in waited:
            (g if s.startswith("ls") else g.sync).wait_ge(T.sem[s], total[s])
